import numpy as np, ml_dtypes
CORES = [48,51,52,55]
N = 4
BF = ml_dtypes.bfloat16
P, CB, W, RU, HB = 4096, 12, 4096, 4, 1
def step(x, inv, wa, kc, hi, lo):
    v = np.add.reduce(x * wa[..., None], axis=2); src = v >= hi[..., None]; blk = v <= lo[..., None]
    cl = np.add.reduce((x >= 128) * kc[..., None], axis=2)
    new = []
    for a in range(N):
        b = max(0, a - HB); L = (a - b + 1) * P; at = np.arange(L)
        s = np.concatenate(src[b:a + 1], axis=1); k = np.concatenate(cl[b:a + 1], axis=1)
        wall = np.maximum.accumulate(np.where(np.concatenate(blk[b:a + 1], axis=1), at, -1), axis=1)[:, L - P:]
        near = np.full((8, P), -1)
        for c in range(16):
            last = np.maximum.accumulate(np.where(s & (k == c), at, -1), axis=1)
            last = np.concatenate([np.full((8, 1), -1), last[:, :-1]], axis=1)[:, L - P:]
            near = np.where(cl[a] == c, last, near)
        ok = (near > wall) & ~blk[a]
        got = np.take_along_axis(np.concatenate(x[b:a + 1], axis=2), np.maximum(near, 0)[:, None, :], 2)
        new.append(np.where(ok[:, None, :] & (x[a] < 64), got, x[a]))
    x = np.stack(new)
    code = np.add.reduce((x[:, :, :CB] >= 128) * (1 << np.arange(CB))[:, None], axis=2)
    return (x + np.take_along_axis(inv, code[:, :, None, :], 3)) & 255
def parts(rng):
    x = rng.integers(0, 256, (N, 8, 16, P)); few = rng.choice(np.array([0.0, 0.2, 0.4]), (N, 8, 1, 1))
    x = np.where(rng.random(x.shape) < few, x >> 2, x); inv = rng.integers(0, 256, (N, 8, 16, W))
    wa = rng.integers(-3, 4, (N, 8, 16, RU)); wa[:, :, 0] = rng.choice(np.array([-3, -2, 2, 3]), (N, 8, RU))
    o = np.argsort(rng.random((N, 8, 16, RU)), axis=2); kc = np.where(o < 4, 1 << np.minimum(o, 3), 0)
    m = 127.5 * np.sum(wa, axis=2); s = 74.0 * np.sqrt(np.sum(wa * wa, axis=2))
    hi = np.floor(m + s * rng.choice(np.array([0.5, 1.0, 1.5, 3.0]), (N, 8, RU))).astype(np.int64)
    lo = np.floor(m - s * rng.choice(np.array([1.5, 2.0, 2.5, 9.0]), (N, 8, RU))).astype(np.int64)
    return x, inv, wa, kc, hi, lo
def pack(x, inv, wa, kc, hi, lo):
    return {"x": x.reshape(N, 128, P).astype(np.float32).astype(BF), "inv": inv.reshape(N, 128, W).astype(np.float32).astype(BF),
            "wa": wa.reshape(N, 128, RU).astype(np.float32).astype(BF), "kc": kc.reshape(N, 128, RU).astype(np.float32).astype(BF),
            "hl": np.repeat(np.concatenate([hi, lo], axis=2), 16, axis=1).astype(np.float32)}
def fit(x, inv, wa, kc, qh, ql):
    hi = np.zeros((N, 8, RU), np.int64); lo = np.zeros((N, 8, RU), np.int64)
    ih = (qh * (P - 1)).astype(np.int64)[..., None]; il = np.maximum(ql * (P - 1), 0).astype(np.int64)[..., None]
    for u in range(RU):
        v = np.sort(np.add.reduce(x * wa[..., u][..., None], axis=2), axis=-1)
        hi[..., u] = np.take_along_axis(v, ih, -1)[..., 0]
        lo[..., u] = np.minimum(np.where(ql < 0, v[..., 0] - 1, np.take_along_axis(v, il, -1)[..., 0]), hi[..., u] - 1)
        x = step(x, inv, wa[..., u], kc[..., u], hi[..., u], lo[..., u])
    return hi, lo
def staged(rng, x, inv, wa, kc, hi, lo, kind, kl):
    wa[..., 0] = 0; wa[:, :, 15, 0] = 3; kc[..., 0] = 0; hi[..., 0] = 738; lo[..., 0] = 27
    x[:, :, 15] = np.where(kind == 1, rng.integers(246, 256, kind.shape), np.where(kind == 2, rng.integers(0, 10, kind.shape), rng.integers(10, 246, kind.shape)))
    for i, w in enumerate((1, 6, 11, 14)):
        kc[:, :, w, 0] = 1 << i; x[:, :, w] = (x[:, :, w] & 127) + 128 * ((kl >> i) & 1)
    return pack(x, inv, wa, kc, hi, lo)
def setup_inputs(rng):
    return pack(*parts(rng))
def setup_inputs_full(rng):
    p = parts(rng); r = rng.random((N, 8, P)); kind = np.where(r < 0.05, 1, np.where(r < 0.055, 2, 0)); kl = rng.integers(0, 16, (N, 8, P))
    x, hi, lo = p[0], p[4], p[5]
    for q in range(N):
        for g in range(8):
            e = P - 16 - int(rng.integers(0, 48)); mode = g % 5 if q == 0 else int(rng.integers(0, 5))
            if mode == 2:
                kind[q, g] = np.where(kind[q, g] == 2, 0, kind[q, g]); kl[q, g] = np.where(kind[q, g] == 1, rng.integers(0, 16), kl[q, g])
            else:
                kind[q, g, e:] = 0; kind[q, g, e:e + 16] = 1; kl[q, g, e:e + 16] = rng.permutation(16)
                if mode == 1: kind[q, g, P - 1] = 2
                if mode == 3: kind[q, g, e - 1] = 2
                if mode == 4: kind[q, g, e + 8] = 2
            kind[q, g, :P // 2 if q == 1 else int(rng.choice(np.array([0, 1, 40, P // 2])))] = 0
    c = rng.permutation(16)
    kind[0, 2] = np.where(rng.random(P) < 0.97, 1, 0); kl[0, 2] = np.where(kind[0, 2] == 1, c[2], kl[0, 2])
    kind[:HB + 1, 7] = 1; kl[:HB + 1, 7] = c[0]; kl[0, 7, 1] = c[1]
    kind[HB, 7, P - 32:] = 0; kl[HB, 7, P - 32:] = c[1]
    x[:HB + 1, 7, 2:4] = x[:HB + 1, 7, 2:4] >> 2; x[HB, 7, 0, P - 32:] = x[HB, 7, 0, P - 32:] >> 2; x[0, 7, 0, 1] = 200
    hi[:2, 0, 1] = 16384; lo[:2, 0, 1] = -16384
    return staged(rng, *p, kind, kl)
def setup_inputs_ends(rng):
    p = parts(rng); kind = np.zeros((N, 8, P), np.int64); kl = rng.integers(0, 16, (N, 8, P)); some = (rng.random((N, 8, P)) < 0.05).astype(np.int64)
    g, h, j = rng.permutation(8)[:3]
    for q in range(N):
        o = np.concatenate([np.array([g]), rng.permutation(np.delete(np.arange(8), g))])
        kind[q, o[1], 0] = 1; kind[q, o[2], P - 1] = 1
        kind[q, o[3]] = some[q, o[3]]; kind[q, o[3], 0] = 2
        kind[q, o[4]] = 1; kind[q, o[5]] = 2
        kind[q, o[6], ::2] = 1; kind[q, o[6], 1::2] = 2
        kind[q, o[7]] = some[q, o[7]]; kind[q, o[7], P - 2] = 1; kind[q, o[7], P - 1] = 2
    kind[:, g] = 0; kind[0, g] = some[0, g]
    kind[:2, h] = 0; kind[0, h, 0] = 1; kind[:2, j] = 0; kind[0, j, P - 1] = 1
    return staged(rng, *p, kind, kl)
def setup_inputs_ties(rng):
    x, inv, wa, kc, hi, lo = parts(rng)
    x = np.where(rng.random(x.shape) < 0.5, rng.choice(np.array([0, 63, 64, 127, 128, 255]), x.shape), x)
    inv = np.where(rng.random(inv.shape) < 0.5, rng.choice(np.array([0, 1, 64, 128, 192, 255]), inv.shape), inv)
    ql = rng.choice(np.array([0.0, 0.03, 0.1, 0.85]), (N, 8)); ql[0, 0] = 0.85; ql[1, 0] = 0.03
    for g, w in ((2, 3), (3, -3)):
        wa[:, g, :, 0] = w; ql[:, g] = 0.03
        small = (kc[:, g, :, 0] == 0)[..., None] & (rng.random((N, 16, P)) < 0.15)
        x[:, g] = np.where(rng.random((N, 1, P)) < 0.2, 255, np.where(small, 0, 192) + (x[:, g] >> 2))
    hi, lo = fit(x, inv, wa, kc, np.full((N, 8), 0.85), ql)
    return pack(x, inv, wa, kc, hi, lo)
def setup_inputs_alike(rng):
    x, inv, wa, kc, hi, lo = parts(rng)
    pat = rng.choice(np.array([0, 63, 64, 128, 255]), (N, 8, 16, 6)); pat[..., 0] = 0; pat[..., 1] = 255; pat[:, :, 0, 2] = 64; pat[:, :, 1, 2] = 128
    x = np.take_along_axis(pat, rng.integers(0, 6, (N, 8, 1, P)), 3); inv[:, 1::2] = 0
    hi, lo = fit(x, inv, wa, kc, np.full((N, 8), 0.6), rng.choice(np.array([-1.0, 0.05]), (N, 8)))
    return pack(x, inv, wa, kc, hi, lo)
def setup_inputs_spread(rng):
    x, inv, wa, kc, hi, lo = parts(rng)
    x = np.floor(np.exp2(8 * rng.random((N, 8, 1, P))) * rng.random((N, 8, 16, P))).astype(np.int64)
    inv = np.where(rng.random((N, 8, 1, W)) < 0.5, np.floor(np.exp2(8 * rng.random((N, 8, 1, W))) * rng.random((N, 8, 16, W))).astype(np.int64), inv)
    wa = np.where(rng.random(wa.shape) < 0.6, 0, rng.choice(np.array([-3, -1, 1, 3]), wa.shape))
    hi, lo = fit(x, inv, wa, kc, rng.choice(np.array([0.5, 0.9, 0.99, 0.9995]), (N, 8)), rng.choice(np.array([-1.0, 0.0, 0.01, 0.1]), (N, 8)))
    return pack(x, inv, wa, kc, hi, lo)
def check_inputs(d):
    bad = []
    for k, lo, hi in (("x", 0, 255), ("inv", 0, 255), ("wa", -3, 3), ("kc", 0, 8), ("hl", -16384, 16384)):
        a = np.asarray(d[k]).astype(np.float32)
        if not np.all((a >= lo) & (a <= hi) & (a == np.floor(a))): bad.append("range of " + k)
    k = np.sort(np.asarray(d["kc"]).astype(np.float32).reshape(N, 8, 16, RU), axis=2)
    if not np.all(k == np.array([0] * 12 + [1, 2, 4, 8], np.float32)[:, None]): bad.append("class weights of kc")
    h = np.asarray(d["hl"]).astype(np.float32).reshape(N, 8, 16, 2 * RU)
    if not np.all(h == h[:, :, :1]): bad.append("rows of hl alike in a group")
    if not np.all(h[..., RU:] < h[..., :RU]): bad.append("lo under hi")
    return bad
def reference(x, inv, wa, kc, hl):
    z = x.astype(np.float32).astype(np.int32).reshape(N, 8, 16, P); tab = inv.astype(np.float32).astype(np.int32).reshape(N, 8, 16, W)
    w = wa.astype(np.float32).astype(np.int32).reshape(N, 8, 16, RU); k = kc.astype(np.float32).astype(np.int32).reshape(N, 8, 16, RU)
    h = hl.astype(np.int32).reshape(N, 8, 16, 2 * RU)[:, :, 0]
    for u in range(RU): z = step(z, tab, w[..., u], k[..., u], h[..., u], h[..., RU + u])
    return {"y": z.reshape(N, 128, P).astype(np.float32).astype(BF)}

@@ -1,0 +1,497 @@
+from concourse.mybir import AluOpType, AxisListType, ActivationFunctionType
+
+ALU = AluOpType
+ACT = ActivationFunctionType
+P, RU, NSEG = 4096, 4, 4
+SG = P // NSEG
+EXT = 16
+WS = SG + EXT
+W0 = 16
+SS = SG + 8
+KC = SG // 16
+PW = 512
+NB = 8
+U = 2.0 ** -13
+MG = 12582912.0
+NENG = 4
+
+SCRATCH = {"tab": ("sbuf", [128, P], "bfloat16"), "yo": ("sbuf", [128, P], "bfloat16")}
+for _u in range(RU):
+    SCRATCH["w%d" % _u] = ("sbuf", [128, W0 + NSEG * WS], "bfloat16")
+    SCRATCH["msg%d" % _u] = ("sbuf", [128, 24], "bfloat16")
+for _n in ("bit", "low", "rc", "gl", "gb", "tg", "sg"):
+    SCRATCH[_n] = ("sbuf", [128, P], "bfloat16")
+SCRATCH["rr"] = ("sbuf", [128, NSEG * SS], "bfloat16")
+for _n in ("inc", "st", "s1"):
+    SCRATCH[_n] = ("sbuf", [128, NSEG * SS], "float16")
+for _n in ("gm", "mm", "m1", "ib", "is", "i63"):
+    SCRATCH[_n] = ("sbuf", [128, 128], "bfloat16")
+for _n in ("dk", "oh", "wm", "lbv", "l4v", "lba", "l4a"):
+    SCRATCH[_n] = ("sbuf", [128, 512], "bfloat16")
+SCRATCH.update({
+    "vv": ("sbuf", [128, P], "float16"),
+    "poff": ("sbuf", [128, 256], "uint16"), "coff": ("sbuf", [128, 256], "uint16"), "toff": ("sbuf", [128, 16], "uint16"),
+    "ini": ("sbuf", [128, 4], "float32"), "ex": ("sbuf", [128, 8], "float32"),
+    "was": ("sbuf", [128, 4], "bfloat16"), "kcs": ("sbuf", [128, 4], "bfloat16"), "hls": ("sbuf", [128, 8], "float32"),
+    "wa2": ("sbuf", [128, 4], "bfloat16"), "thl": ("sbuf", [128, 4], "float32"), "bhi": ("sbuf", [128, 4], "float32"),
+    "bh2": ("sbuf", [128, 4], "float32"),
+    "jj": ("sbuf", [128, 144], "float32"), "ga": ("sbuf", [128, 128], "float32"), "cm": ("sbuf", [128, 128], "float32"),
+    "ji": ("sbuf", [128, 128], "int32"), "jk": ("sbuf", [128, 128], "int32"), "cf": ("sbuf", [128, 12], "float32"),
+    "pw": ("sbuf", [128, 32], "float32"), "t16": ("sbuf", [128, KC], "float32"), "th": ("sbuf", [128, KC], "float16"),
+    "ih": ("sbuf", [128, 128], "float16"),
+    "zd": ("sbuf", [128, 144], "float16"), "zcv": ("sbuf", [128, 144], "bfloat16"), "zca": ("sbuf", [128, 144], "bfloat16"),
+})
+for _k in range(NB):
+    SCRATCH["p%d" % _k] = ("psum", [128, PW], "float32")
+
+SEMAPHORES = (["qv", "qa", "qp", "qg", "sent"] + ["arr%d" % u for u in range(RU)]
+              + ["ld%d" % k for k in range(10)] + ["so%d" % k for k in range(8)])
+
+CY, PCY, GA, FIX, LAT, WIRE = 1.0, 0.5, 1.56, 60.0, 130.0, 2500.0
+ROUNDS, SLACK = 10, 60.0
+
+BASE = {"bit": "aavv" * 4, "gb": "v" * 16, "rc": "a" * 16, "tg": "a" * 32, "carry": "v" * 16, "out": "v" * 8}
+MIDDLE = dict(BASE, bit="aaav" * 4, gb="avvv" * 3 + "vvvv")
+CFG = {0: BASE, 1: MIDDLE, 2: MIDDLE, 3: BASE}
+
+
+def plan(rank, n_ranks, bank):
+    ops, cfg = [], CFG[rank]
+
+    def add(q, fn, rd, wr, cost, **kw):
+        d = {"q": q, "fn": fn, "rd": rd, "wr": wr, "cost": cost}
+        d.update(kw)
+        ops.append(d)
+        return d
+
+    def R(name, a=0, b=None):
+        return (name, a, SCRATCH[name][1][1] if b is None else b)
+
+    def ap(T, r):
+        return T["p%d" % bank[(rank, r[0])] if r[0][0] == "@" else r[0]][:, r[1]:r[2]]
+
+    def vcost(rs, n):
+        half = all(r[0][0] != "@" and SCRATCH[r[0]][2] in ("bfloat16", "float16", "uint16") for r in rs)
+        return FIX + max(64, n * (0.5 if half else 1.0)) * CY
+
+    def ts(out, in0, s1, s2, op0, op1=None):
+        rd = [in0] + [s for s in (s1, s2) if isinstance(s, tuple)]
+
+        def fn(g, T):
+            a = ap(T, s1) if isinstance(s1, tuple) else s1
+            b = ap(T, s2) if isinstance(s2, tuple) else s2
+            if op1 is None:
+                return g.vector.tensor_scalar(ap(T, out), ap(T, in0), a, None, op0)
+            return g.vector.tensor_scalar(ap(T, out), ap(T, in0), a, b, op0, op1)
+        return add("v", fn, rd, [out], vcost([out, in0], in0[2] - in0[1]))
+
+    def tt(out, in0, in1, op):
+        f = 1 if "@" in (in0[0][0], in1[0][0]) else 2
+        return add("v", lambda g, T: g.vector.tensor_tensor(ap(T, out), ap(T, in0), ap(T, in1), op), [in0, in1], [out],
+                   FIX + max(64, f * (out[2] - out[1])) * CY)
+
+    def cp(out, in0):
+        return add("v", lambda g, T: g.vector.tensor_copy(ap(T, out), ap(T, in0)), [in0], [out], vcost([out, in0], out[2] - out[1]))
+
+    def product(out, in0):
+        return add("v", lambda g, T: g.vector.tensor_reduce(ap(T, out), ap(T, in0), AxisListType.X, ALU.mult), [in0], [out], FIX + 64)
+
+    def scan(out, a, b, init):
+        d0, d1, o = R("rr", a, b), R("inc", a, b), R(out, a, b)
+        rd = [d0, d1] + ([init] if isinstance(init, tuple) else [])
+        return add("v", lambda g, T: g.vector.tensor_tensor_scan(ap(T, o), ap(T, d0), ap(T, d1),
+                   ap(T, init) if isinstance(init, tuple) else init, ALU.mult, ALU.add), rd, [o], vcost([o], b - a))
+
+    def act(out, in0, func, bias=0.0, scale=1.0):
+        rd = [in0] + ([bias] if isinstance(bias, tuple) else [])
+        return add("a", lambda g, T: g.scalar.activation(ap(T, out), ap(T, in0), func,
+                   bias=ap(T, bias) if isinstance(bias, tuple) else bias, scale=scale), rd, [out], FIX + max(64, out[2] - out[1]) * CY)
+
+    def mm(out, terms, first=True, last=True):
+        def fn(g, T):
+            for k, (l, r, step) in enumerate(terms):
+                ins = g.tensor.matmul(ap(T, out), ap(T, l), T[r[0]][:, r[1]:r[2]:step] if step > 1 else ap(T, r),
+                                      first and k == 0, last and k == len(terms) - 1)
+            return ins
+        return add("p", fn, [t[0] for t in terms] + [t[1] for t in terms], [out], 30 + len(terms) * max(64, out[2] - out[1]) * PCY)
+
+    def wrap(z, src):
+        return [(R(z, 15 - i, 143 - i), (src[0], src[1] + i, src[2]), 16) for i in range(16)]
+
+    def gather(out, win, off, q, kind):
+        def fn(g, T):
+            src = ap(T, win).indirect(ap(T, off))
+            if q == "a":
+                if kind == "copy":
+                    return g.scalar.activation(ap(T, out), src, ACT.Copy)
+                return g.scalar.activation(ap(T, out), src, ACT.Identity, bias=-1.0, scale=1.0 / 128)
+            if kind == "table":
+                return g.vector.tensor_scalar(ap(T, out), src, 1.0 / 128, -1.0, ALU.mult, ALU.add)
+            if kind == "copy":
+                return g.vector.tensor_copy(ap(T, out), src)
+            return g.vector.tensor_tensor(ap(T, out), src, ap(T, kind), ALU.mult)
+        return add(q, fn, [win, off] + ([kind] if isinstance(kind, tuple) else []), [out], FIX + max(64, (out[2] - out[1]) * GA) * CY)
+
+    def iota(out, pat, base, mult):
+        return add("g", lambda g, T: g.iota(ap(T, out), pat, base, mult, allow_small_or_imprecise_dtypes=True), [], [out],
+                   130 + 2 * (out[2] - out[1]) * CY)
+
+    num = {"ld": 0, "so": 0, "@": 0}
+
+    def fresh(kind):
+        num[kind] += 1
+        return "%s%d" % (kind, num[kind] - 1)
+
+    def tile(n=PW):
+        return (fresh("@"), 0, n)
+
+    def load(q, out, src, a, b):
+        add(q, lambda g, T: (g.sync if q == "s" else g.scalar).dma_start(ap(T, out), T[src][:, a:b]), [], [out], 100,
+            sem=fresh("ld"), inc=16, dma=(b - a) * 256)
+
+    def wseg(u, s, a=EXT, b=WS):
+        return ("w%d" % u, W0 + s * WS + a, W0 + s * WS + b)
+
+    def blk(name, u):
+        return R(name, 128 * u, 128 * u + 128)
+
+    def col(name, k):
+        return R(name, k, k + 1)
+
+    def cf(k):
+        return col("cf", k)
+
+    def gaps(name, a, val):
+        add("v", lambda g, T: g.vector.tensor_scalar(T[name][:, a:NSEG * SS:SS], T["cm"][:, 0:NSEG], 0.0, val, ALU.mult, ALU.add),
+            [R("cm")], [col(name, c) for c in range(a, NSEG * SS, SS)], FIX + 64)
+
+    load("a", R("kcs"), "kc", 0, 4)
+    load("a", R("was"), "wa", 0, 4)
+    load("a", R("hls"), "hl", 0, 8)
+    for s in range(NSEG):
+        load("s", wseg(0, s), "x", s * SG, (s + 1) * SG)
+    load("s", R("tab", 0, P // 2), "inv", 0, P // 2)
+    load("s", R("tab", P // 2, P), "inv", P // 2, P)
+
+    iota(cf(0), [[0, 1]], -15, 2)
+    iota(cf(7), [[0, 1]], 0, 1)
+    iota(R("cm"), [[0, 8], [1, 16]], 0, 0)
+    iota(R("ga"), [[1, 8], [0, 16]], int(MG), 0)
+    iota(R("jj"), [[1, 144]], 0, -1)
+    iota(R("t16"), [[16, KC]], EXT, 0)
+    gaps("rr", 0, 1.0)
+    gaps("inc", SG, -(WS - 1) * U)
+    ts(cf(1), cf(0), 1.0 / 32, MG, ALU.mult, ALU.add)
+    ts(cf(2), cf(1), MG, -16.0, ALU.subtract, ALU.mult)
+    ts(cf(8), cf(7), cf(2), None, ALU.add)
+    ts(R("gm"), R("ga"), cf(1), None, ALU.is_equal)
+    ts(R("ib"), R("jj", 0, 128), 0.0, None, ALU.is_equal)
+    ts(R("pw", 0, 16), R("cm", 0, 16), cf(8), 1.0, ALU.is_lt, ALU.add)
+    ts(R("pw", 16, 32), R("cm", 0, 16), cf(8), 0.5, ALU.is_ge, ALU.max)
+    product(cf(3), R("pw", 0, 16))
+    product(cf(4), R("pw", 16, 32))
+    ts(R("ji"), R("cm"), cf(4), -0.4375, ALU.mult, ALU.add)
+    ts(R("jk"), R("ji"), 1, None, ALU.bitwise_and)
+    ts(R("m1"), R("jk"), -2.0, 1.0, ALU.mult, ALU.add)
+    tt(R("mm"), R("m1"), R("gm"), ALU.mult)
+    for u in range(RU):
+        ts(blk("wm", u), R("gm"), col("was", u), -2.0 if u == 0 else -256.0, ALU.mult, ALU.mult)
+        ts(blk("dk", u), R("ib"), col("kcs", u), None, ALU.mult)
+        t, t2 = tile(128), tile(128)
+        mm(t, [(R("gm"), blk("dk", u), 1)])
+        ts(blk("oh", u), t, cf(3), None, ALU.is_equal)
+        mm(t2, [(blk("oh", u), R("mm"), 1)])
+        for e in sorted(set(cfg["bit"][NSEG * u:NSEG * u + NSEG])):
+            h = 0.5 if e == "a" else 1.0
+            act(blk("lb" + e, u), t2, ACT.Copy, scale=65536.0 * h)
+            act(blk("l4" + e, u), t2, ACT.Copy, scale=-4.0 * h)
+    ts(R("thl"), R("hls", 4, 8), -2.0, None, ALU.mult)
+    ts(R("bhi"), R("hls", 0, 4), 2.0, 131071.0, ALU.mult, ALU.add)
+    ts(col("bh2", 0), col("bhi", 0), 128.0, None, ALU.mult)
+    ts(R("wa2"), R("was"), 126.0, None, ALU.mult)
+    t = tile(4)
+    mm(t, [(R("gm"), R("wa2"), 1)])
+    tt(R("thl", 1, 4), R("thl", 1, 4), (t[0], 1, 4), ALU.add)
+    tt(R("bhi", 1, 4), R("bhi", 1, 4), (t[0], 1, 4), ALU.subtract)
+    ts(R("bh2", 1, 4), R("bhi", 1, 4), 128.0, None, ALU.mult)
+    for n, f in (("ih", 1.0), ("is", 1.0 / 128), ("i63", -63.0 / 128)):
+        act(R(n), R("ib"), ACT.Copy, scale=f)
+    ts(cf(5), cf(3), 4000.0, cf(3), ALU.is_lt, ALU.mult)
+    ts(cf(6), cf(8), -1.0, 15.0, ALU.mult, ALU.add)
+    ts(cf(9), cf(6), U, -1.0, ALU.mult, ALU.add)
+    ts(R("zd"), R("jj"), cf(6), -1.0 / U, ALU.is_equal, ALU.mult)
+    ts(R("zcv"), R("jj"), cf(6), cf(5), ALU.is_equal, ALU.mult)
+    act(R("zca"), R("zcv"), ACT.Copy, scale=0.5)
+    ts(R("th"), R("t16"), cf(8), None, ALU.add)
+    sends, takes = rank + 1 < n_ranks, rank > 0
+    for u in range(RU):
+        if sends:
+            iota(R("msg%d" % u, 0, 8), [[0, 8]], 0, 0)
+        for s in range(NSEG):
+            if (s == 0 and not takes) or (s > 0 and sends and takes):
+                iota(wseg(u, s, 0, EXT), [[0, EXT]], 0, 0)
+
+    def end_of(name, s):
+        return col(name, s * SS + SG)
+
+    def judge(u, s):
+        o, f = (63.0, 1.0) if u == 0 else (0.0, 1.0 / 128)
+        c, e, k0 = s * SG, cfg["bit"][NSEG * u + s], s * SS
+        for h in range(0, SG, PW):
+            w, b, k = wseg(u, s, EXT + h, EXT + h + PW), R("bit", c + h, c + h + PW), k0 + h
+            if e == "a":
+                act(b, w, ACT.Sign, bias=-(64.5 + o) * f)
+            else:
+                ts(b, w, (65.0 + o) * f, 0.5, ALU.is_ge, ALU.subtract)
+            t, t2 = tile(), tile()
+            mm(t, [(blk("wm", u), w, 1)])
+            ts(R("inc", k, k + PW), t, col("thl", u), 1.0 - U, ALU.is_lt, ALU.subtract)
+            mm(t2, [(blk("wm", u), w, 1), (blk("lb" + e, u), b, 1)])
+            act(R("rr", k + 1, k + 1 + PW), t2, ACT.Sigmoid, bias=col("bh2", u), scale=128.0)
+        if sends and takes:
+            cuts = [k0, k0 + PW, k0 + SG + 1] if s + 1 == NSEG else [k0, k0 + SG + 1]
+            for a, b in zip(cuts, cuts[1:]):
+                scan("s1", a, b, col("s1", a - 1) if a > k0 else SG * U if s else -1.0)
+            z = end_of("s1", s)
+            step = (EXT - s * WS) * U if s + 1 == NSEG else (WS - (2 * SG - WS + 1)) * U
+            if s == 0:
+                ts(col("ex", 0), z, step, None, ALU.add)
+            else:
+                ts(col("ex", 4 + s), z, 0.0, col("ex", s - 1), ALU.is_ge, ALU.mult)
+                ts(col("ex", s), z, col("ex", 4 + s), step, ALU.add, ALU.add)
+        ts(R("low", c, c + SG), wseg(u, s), o, None, ALU.is_le)
+        if cfg["rc"][NSEG * u + s] == "a":
+            act(R("rc", c, c + SG), wseg(u, s), ACT.Relu, bias=-o)
+        else:
+            ts(R("rc", c, c + SG), wseg(u, s), o, 0.0, ALU.subtract, ALU.max)
+
+    def send(u):
+        add("g", None, [R("msg%d" % u)], [], 300, send=u)
+
+    def export(u):
+        e = col("ex", NSEG - 1)
+        ts(col("toff", 8), e, -1.0 / U, float(NSEG * WS - EXT - 1), ALU.mult, ALU.min)
+        ts(col("msg%d" % u, 7), e, -0.6, None, ALU.is_ge)
+        gather(R("msg%d" % u, 8, 24), R("w%d" % u, W0 + EXT), col("toff", 8), "v", "copy")
+        send(u)
+
+    def point(u, s):
+        c, e = s * SG, cfg["bit"][NSEG * u + s]
+        if s == 0 and takes:
+            add("x", None, [], [("w%d" % u, W0 - 8, W0 + EXT)], 0, arrive=u)
+            ts(col("ini", 0), col("w%d" % u, W0 - 1), cf(9), None, ALU.add)
+        scan("st", s * SS, s * SS + SG + 1, col("ini", s) if s > 0 or takes else -1.0)
+        z = end_of("st", s)
+        if s + 1 < NSEG or not takes:
+            last = s + 1 == NSEG
+            if last:
+                ts(col("msg%d" % u, 7), z, -0.5, None, ALU.is_ge)
+            else:
+                ts(col("ini", s + 1), z, -0.5, cf(9), ALU.is_ge, ALU.add)
+            ts(col("toff", 2 * s), z, -1.0 / U, WS - 1.0, ALU.mult, ALU.min)
+            gather(R("msg%d" % u, 8, 24) if last else wseg(u, s + 1, 0, EXT), wseg(u, s, 0, WS), col("toff", 2 * s),
+                   cfg["carry"][NSEG * u + s], "copy")
+            if last:
+                send(u)
+        for h in range(0, SG, PW):
+            t = tile()
+            mm(t, [(blk("l4" + e, u), R("bit", c + h, c + h + PW), 1), (R("ih"), R("st", s * SS + h, s * SS + h + PW), 1)])
+            act(R("vv", c + h, c + h + PW), t, ACT.Relu, bias=-8.0)
+        t = tile(KC)
+        mm(t, [(R("ih"), R("th"), 1)] + wrap("zd", R("vv", c, c + SG)))
+        cp(R("poff", s * KC, (s + 1) * KC), t)
+
+    def apply(u, s):
+        a, b, e = s * SG, (s + 1) * SG, cfg["gb"][NSEG * u + s]
+        edge = 127.5 if u == 0 else 64.5 / 128
+        gather(R("gl", a, b), wseg(u, s, 0, WS), R("poff", a // 16, b // 16), "v", R("low", a, b))
+        if e == "a":
+            act(R("gb", a, b), R("gl", a, b), ACT.Sign, bias=-edge)
+        else:
+            ts(R("gb", a, b), R("gl", a, b), edge, None, ALU.is_ge)
+        t = tile(KC)
+        mm(t, wrap("zc" + cfg["bit"][NSEG * u + s], R("bit", a, b)), last=False)
+        mm(t, wrap("zc" + e, R("gb", a, b)), first=False)
+        ts(R("coff", a // 16, b // 16), t, 4095.0 if e == "a" else 2047.5, None, ALU.add)
+        for h in range(0, SG, PW):
+            a, j = s * SG + h, 2 * s + h // PW
+            b = a + PW
+            gather(R("tg", a, b), R("tab"), R("coff", a // 16, b // 16), cfg["tg"][2 * NSEG * u + j], "table")
+            t = tile()
+            mm(t, ([(R("i63"), R("low", a, b), 1)] if u == 0 else [])
+               + [(R("is" if u == 0 else "ib"), R(n, a, b), 1) for n in ("rc", "gl")] + [(R("ib"), R("tg", a, b), 1)])
+            act(R("sg", a, b), t, ACT.Sign, bias=-64.5 / 128)
+            if u + 1 < RU:
+                tt(wseg(u + 1, s, EXT + h, EXT + h + PW), t, R("sg", a, b), ALU.subtract)
+                continue
+            tt(R("gb", a, b), t, R("sg", a, b), ALU.subtract)
+            if cfg["out"][j] == "a":
+                act(R("yo", a, b), R("gb", a, b), ACT.Identity, bias=63.0, scale=128.0)
+            else:
+                ts(R("yo", a, b), R("gb", a, b), 128.0, 63.0, ALU.mult, ALU.add)
+            add("s", lambda g, T, a=a, b=b: g.sync.dma_start(T["y"][:, a:b], T["yo"][:, a:b]), [R("yo", a, b)], [], 100,
+                sem=fresh("so"), inc=16, dma=PW * 256)
+
+    for s in range(NSEG):
+        judge(0, s)
+    for u in range(RU):
+        if sends and takes:
+            export(u)
+        for s in range(NSEG):
+            point(u, s)
+        for s in range(NSEG):
+            apply(u, s)
+            if u + 1 < RU:
+                judge(u + 1, s)
+    return ops
+
+
+def link(ops):
+    seen = {}
+    for i, o in enumerate(ops):
+        dep = set()
+        acc = [(r, False) for r in o["rd"]] + [(r, True) for r in o["wr"]]
+        for r, w in acc:
+            for (j, a, b, wj) in seen.get(r[0], []):
+                if r[0][0] == "@" or ((w or wj) and a < r[2] and r[1] < b):
+                    dep.add(j)
+        for r, w in acc:
+            if r[0][0] == "@":
+                o["tile"], o["opens"] = r[0], r[0] not in seen
+                seen[r[0]] = [(i, 0, 0, True)]
+            else:
+                keep = [e for e in seen.get(r[0], []) if not (w and r[1] <= e[1] and e[2] <= r[2])]
+                seen[r[0]] = keep + [(i, r[1], r[2], w)]
+        dep.discard(i)
+        o["dep"] = sorted(dep)
+    for name in seen:
+        if name[0] == "@":
+            ops[seen[name][0][0]]["closes"] = True
+
+
+def sweep(ops, pre, key, back):
+    n = len(ops)
+    succ = [[] for _ in ops]
+    for i in range(n):
+        for j, d in pre[i]:
+            succ[j].append((i, d))
+    left, due, ready = [len(p) for p in pre], [0.0] * n, {}
+    for i in range(n):
+        if not left[i]:
+            ready.setdefault(ops[i]["e"], []).append(i)
+    free, at, end, seq, after, bank, banks, wire = {}, [0.0] * n, [0.0] * n, [], {}, {}, {}, {}
+    opens, closes = ("closes", "opens") if back else ("opens", "closes")
+    for _ in range(n):
+        best = None
+        for e, line in ready.items():
+            bk = banks.setdefault(e[0], {k: (0.0, None) for k in range(NB)})
+            bt = min([v[0] for v in bk.values()]) if bk else None
+            f = free.get(e, 0.0)
+            st = [(max(due[i], f, bt if ops[i].get(opens) else 0.0), i) for i in line if bt is not None or not ops[i].get(opens)]
+            if st and (best is None or min(st)[0] < best[0]):
+                best = (min(st)[0], e, st)
+        t0, e, st = best
+        t, i = min([x for x in st if x[0] <= t0 + SLACK], key=lambda x: (key[x[1]], x[1]))
+        o = ops[i]
+        ready[e].remove(i)
+        at[i] = t
+        end[i] = free[e] = t + o["cost"]
+        bk = banks[e[0]]
+        if o.get(opens):
+            b = min(bk, key=lambda k: bk[k][0])
+            bank[(e[0], o["tile"])] = b
+            after[i] = bk.pop(b)[1]
+        if o.get(closes):
+            bk[bank[(e[0], o["tile"])]] = (end[i] + LAT, i)
+        if "dma" in o and not back:
+            wire[e[0]] = end[i] = max(wire.get(e[0], 0.0), end[i] + 1500) + o["dma"] / 250.0
+        seq.append(i)
+        for k, d in succ[i]:
+            due[k] = max(due[k], end[i] + d)
+            left[k] -= 1
+            if not left[k]:
+                ready.setdefault(ops[k]["e"], []).append(k)
+    return seq, at, end, after, bank
+
+
+CACHE = {}
+
+
+def schedule(n_ranks):
+    if n_ranks in CACHE:
+        return CACHE[n_ranks]
+    ops, pre, sent, bank = [], [], {}, {}
+    for r in range(n_ranks):
+        mine = plan(r, n_ranks, bank)
+        link(mine)
+        base = len(ops)
+        for i, o in enumerate(mine):
+            o["e"] = (r, o["q"])
+            p = [(base + j, 0.0 if mine[j]["q"] == "p" == o["q"] else LAT) for j in o["dep"]]
+            o["dep"] = [base + j for j in o["dep"]]
+            if "send" in o:
+                sent[(r, o["send"])] = base + i
+            if "arrive" in o:
+                p.append((sent[(r - 1, o["arrive"])], WIRE))
+            pre.append(p)
+        ops += mine
+    rev = [[] for _ in ops]
+    for i, p in enumerate(pre):
+        for j, d in p:
+            rev[j].append((i, d + (1500 + ops[j]["dma"] / 250.0 if "dma" in ops[j] else 0)))
+    key, best = list(range(len(ops))), None
+    for _ in range(ROUNDS):
+        out = sweep(ops, pre, key, False)
+        if best is None or max(out[2]) < max(best[2]):
+            best = out
+        key = [-x for x in sweep(ops, rev, [-x for x in out[2]], True)[2]]
+    bank.update(best[4])
+    for i, j in best[3].items():
+        if j is not None:
+            ops[i]["dep"].append(j)
+    CACHE[n_ranks] = (ops,) + best[:3]
+    return CACHE[n_ranks]
+
+
+def rank_program(g, core, T, topo):
+    rank = T.rank_of(core)
+    if rank is None:
+        return
+    ops, seq = schedule(len(T.cores))[:2]
+    queue = {"v": g.vector, "a": g.scalar, "p": g.tensor, "g": g, "s": g.sync}
+    count, mark, known, sent = {}, {}, {}, 0
+
+    def wait(q, sem, val):
+        if known.get((q, sem), 0) < val:
+            known[(q, sem)] = val
+            queue[q].wait_ge(T.sem[sem], val)
+
+    for i in seq:
+        o = ops[i]
+        if o["e"][0] != rank:
+            continue
+        q = o["q"]
+        if "arrive" in o:
+            mark[i] = ("arr%d" % o["arrive"], NENG)
+            continue
+        need = {}
+        for j in o["dep"]:
+            if not (q == "p" and ops[j]["q"] == "p"):
+                need[mark[j][0]] = max(need.get(mark[j][0], 0), mark[j][1])
+        for sem in sorted(need):
+            wait(q, sem, need[sem])
+        if "send" in o:
+            u, dst = o["send"], T.cores[rank + 1]
+            rid, pid = topo.addr(dst)[:2]
+            mask = sum(1 << e for e in topo.engines(core, dst)[:NENG])
+            g.remote_dma(T["w%d" % u][:, W0 - 8:W0 + EXT], T["msg%d" % u][:], T.sem["arr%d" % u], T.sem["sent"], pid, rid, mask)
+            sent += NENG
+            continue
+        sem, inc = o.get("sem", "q" + q), o.get("inc", 1)
+        count[sem] = count.get(sem, 0) + inc
+        mark[i] = (sem, count[sem])
+        o["fn"](g, T).then_inc(T.sem[sem], inc)
+    for sem in sorted(count):
+        wait("s", sem, count[sem])
+    if sent:
+        wait("g", "sent", sent)

@@ -13,7 +13,7 @@ PW = 512
 NB = 8
 U = 2.0 ** -13
 MG = 12582912.0
-NENG = 4
+NENG = 8
 
 SCRATCH = {"tab": ("sbuf", [128, P], "bfloat16"), "yo": ("sbuf", [128, P], "bfloat16")}
 for _u in range(RU):
@@ -26,10 +26,10 @@ for _n in ("inc", "st", "s1"):
     SCRATCH[_n] = ("sbuf", [128, NSEG * SS], "float16")
 for _n in ("gm", "mm", "m1", "ib", "is", "i63"):
     SCRATCH[_n] = ("sbuf", [128, 128], "bfloat16")
-for _n in ("dk", "oh", "wm", "lbv", "l4v", "lba", "l4a"):
+for _n in ("dk", "oh", "wm", "lb", "l4"):
     SCRATCH[_n] = ("sbuf", [128, 512], "bfloat16")
 SCRATCH.update({
-    "vv": ("sbuf", [128, P], "float16"),
+    "vv": ("sbuf", [128, P], "float16"), "one": ("sbuf", [128, 2], "bfloat16"),
     "poff": ("sbuf", [128, 256], "uint16"), "coff": ("sbuf", [128, 256], "uint16"), "toff": ("sbuf", [128, 16], "uint16"),
     "ini": ("sbuf", [128, 4], "float32"), "ex": ("sbuf", [128, 8], "float32"),
     "was": ("sbuf", [128, 4], "bfloat16"), "kcs": ("sbuf", [128, 4], "bfloat16"), "hls": ("sbuf", [128, 8], "float32"),
@@ -38,21 +38,20 @@ SCRATCH.update({
     "jj": ("sbuf", [128, 144], "float32"), "ga": ("sbuf", [128, 128], "float32"), "cm": ("sbuf", [128, 128], "float32"),
     "ji": ("sbuf", [128, 128], "int32"), "jk": ("sbuf", [128, 128], "int32"), "cf": ("sbuf", [128, 12], "float32"),
     "pw": ("sbuf", [128, 32], "float32"), "t16": ("sbuf", [128, KC], "float32"), "th": ("sbuf", [128, KC], "float16"),
-    "ih": ("sbuf", [128, 128], "float16"),
-    "zd": ("sbuf", [128, 144], "float16"), "zcv": ("sbuf", [128, 144], "bfloat16"), "zca": ("sbuf", [128, 144], "bfloat16"),
+    "ih": ("sbuf", [128, 128], "float16"), "zd": ("sbuf", [128, 144], "float16"), "zc": ("sbuf", [128, 144], "bfloat16"),
 })
 for _k in range(NB):
     SCRATCH["p%d" % _k] = ("psum", [128, PW], "float32")
 
 SEMAPHORES = (["qv", "qa", "qp", "qg", "sent"] + ["arr%d" % u for u in range(RU)]
-              + ["ld%d" % k for k in range(10)] + ["so%d" % k for k in range(8)])
+              + ["ld%d" % k for k in range(12)] + ["so%d" % k for k in range(8)])
 
-CY, PCY, GA, FIX, LAT, WIRE = 1.0, 0.5, 1.56, 60.0, 130.0, 2500.0
+CY, PCY, GA, FIX, LAT, WIRE = 0.95, 0.48, 1.56, 60.0, 130.0, 2500.0
 ROUNDS, SLACK = 10, 60.0
 
-BASE = {"bit": "aavv" * 4, "gb": "v" * 16, "rc": "a" * 16, "tg": "a" * 32, "carry": "v" * 16, "out": "v" * 8}
-MIDDLE = dict(BASE, bit="aaav" * 4, gb="avvv" * 3 + "vvvv")
-CFG = {0: BASE, 1: MIDDLE, 2: MIDDLE, 3: BASE}
+BASE = {"bit": "aaaaaava" + "v" * 24, "gb": "avvv" * 4, "rc": "a" * 16, "tg": "a" * 32, "carry": "a" + "v" * 15, "out": "v" * 8}
+CFG = {0: BASE, 1: dict(BASE, bit="aaaaaavavvvvaavaavvvaavavvvvaava"), 2: dict(BASE, bit="aaaaaavavvvvaavavvvvaavavvvvaava"),
+       3: dict(BASE, tg="a" * 8 + "aaaaaava" * 3)}
 
 
 def plan(rank, n_ranks, bank):
@@ -161,14 +160,12 @@ def plan(rank, n_ranks, bank):
     def cf(k):
         return col("cf", k)
 
-    def gaps(name, a, val):
-        add("v", lambda g, T: g.vector.tensor_scalar(T[name][:, a:NSEG * SS:SS], T["cm"][:, 0:NSEG], 0.0, val, ALU.mult, ALU.add),
-            [R("cm")], [col(name, c) for c in range(a, NSEG * SS, SS)], FIX + 64)
-
     load("a", R("kcs"), "kc", 0, 4)
     load("a", R("was"), "wa", 0, 4)
     load("a", R("hls"), "hl", 0, 8)
-    for s in range(NSEG):
+    load("s", wseg(0, 0, EXT, EXT + PW), "x", 0, PW)
+    load("s", wseg(0, 0, EXT + PW, WS), "x", PW, SG)
+    for s in range(1, NSEG):
         load("s", wseg(0, s), "x", s * SG, (s + 1) * SG)
     load("s", R("tab", 0, P // 2), "inv", 0, P // 2)
     load("s", R("tab", P // 2, P), "inv", P // 2, P)
@@ -179,8 +176,10 @@ def plan(rank, n_ranks, bank):
     iota(R("ga"), [[1, 8], [0, 16]], int(MG), 0)
     iota(R("jj"), [[1, 144]], 0, -1)
     iota(R("t16"), [[16, KC]], EXT, 0)
-    gaps("rr", 0, 1.0)
-    gaps("inc", SG, -(WS - 1) * U)
+    iota(col("one", 0), [[0, 1]], 1, 0)
+    for s in range(NSEG):
+        iota(col("rr", s * SS), [[0, 1]], 1, 0)
+        act(col("inc", s * SS + SG), col("one", 0), ACT.Copy, scale=-(WS - 1) * U)
     ts(cf(1), cf(0), 1.0 / 32, MG, ALU.mult, ALU.add)
     ts(cf(2), cf(1), MG, -16.0, ALU.subtract, ALU.mult)
     ts(cf(8), cf(7), cf(2), None, ALU.add)
@@ -201,12 +200,14 @@ def plan(rank, n_ranks, bank):
         mm(t, [(R("gm"), blk("dk", u), 1)])
         ts(blk("oh", u), t, cf(3), None, ALU.is_equal)
         mm(t2, [(blk("oh", u), R("mm"), 1)])
-        for e in sorted(set(cfg["bit"][NSEG * u:NSEG * u + NSEG])):
-            h = 0.5 if e == "a" else 1.0
-            act(blk("lb" + e, u), t2, ACT.Copy, scale=65536.0 * h)
-            act(blk("l4" + e, u), t2, ACT.Copy, scale=-4.0 * h)
+        act(blk("lb", u), t2, ACT.Copy, scale=65536.0)
+        act(blk("l4", u), t2, ACT.Copy, scale=-4.0)
+    t = tile(1)
+    mm(t, [(R("mm"), col("one", 0), 1)])
+    ts(cf(10), t, -32768.0, 524287.0, ALU.mult, ALU.add)
+    ts(cf(11), t, 2.0, -32.0, ALU.mult, ALU.add)
     ts(R("thl"), R("hls", 4, 8), -2.0, None, ALU.mult)
-    ts(R("bhi"), R("hls", 0, 4), 2.0, 131071.0, ALU.mult, ALU.add)
+    ts(R("bhi"), R("hls", 0, 4), 2.0, cf(10), ALU.mult, ALU.add)
     ts(col("bh2", 0), col("bhi", 0), 128.0, None, ALU.mult)
     ts(R("wa2"), R("was"), 126.0, None, ALU.mult)
     t = tile(4)
@@ -220,8 +221,7 @@ def plan(rank, n_ranks, bank):
     ts(cf(6), cf(8), -1.0, 15.0, ALU.mult, ALU.add)
     ts(cf(9), cf(6), U, -1.0, ALU.mult, ALU.add)
     ts(R("zd"), R("jj"), cf(6), -1.0 / U, ALU.is_equal, ALU.mult)
-    ts(R("zcv"), R("jj"), cf(6), cf(5), ALU.is_equal, ALU.mult)
-    act(R("zca"), R("zcv"), ACT.Copy, scale=0.5)
+    ts(R("zc"), R("jj"), cf(6), cf(5), ALU.is_equal, ALU.mult)
     ts(R("th"), R("t16"), cf(8), None, ALU.add)
     sends, takes = rank + 1 < n_ranks, rank > 0
     for u in range(RU):
@@ -234,22 +234,25 @@ def plan(rank, n_ranks, bank):
     def end_of(name, s):
         return col(name, s * SS + SG)
 
+    def step01(out, in0, edge, e, f):
+        if e == "a":
+            act(out, in0, ACT.Sigmoid, bias=-edge * 256.0, scale=256.0 / f)
+        else:
+            ts(out, in0, edge * f, None, ALU.is_ge)
+
     def judge(u, s):
         o, f = (63.0, 1.0) if u == 0 else (0.0, 1.0 / 128)
-        c, e, k0 = s * SG, cfg["bit"][NSEG * u + s], s * SS
+        c, k0 = s * SG, s * SS
         for h in range(0, SG, PW):
             w, b, k = wseg(u, s, EXT + h, EXT + h + PW), R("bit", c + h, c + h + PW), k0 + h
-            if e == "a":
-                act(b, w, ACT.Sign, bias=-(64.5 + o) * f)
-            else:
-                ts(b, w, (65.0 + o) * f, 0.5, ALU.is_ge, ALU.subtract)
+            step01(b, w, 64.5 + o, cfg["bit"][8 * u + (c + h) // PW], f)
             t, t2 = tile(), tile()
             mm(t, [(blk("wm", u), w, 1)])
             ts(R("inc", k, k + PW), t, col("thl", u), 1.0 - U, ALU.is_lt, ALU.subtract)
-            mm(t2, [(blk("wm", u), w, 1), (blk("lb" + e, u), b, 1)])
+            mm(t2, [(blk("wm", u), w, 1), (blk("lb", u), b, 1)])
             act(R("rr", k + 1, k + 1 + PW), t2, ACT.Sigmoid, bias=col("bh2", u), scale=128.0)
         if sends and takes:
-            cuts = [k0, k0 + PW, k0 + SG + 1] if s + 1 == NSEG else [k0, k0 + SG + 1]
+            cuts = [k0, k0 + SG - PW, k0 + SG + 1] if s + 1 == NSEG else [k0, k0 + SG + 1]
             for a, b in zip(cuts, cuts[1:]):
                 scan("s1", a, b, col("s1", a - 1) if a > k0 else SG * U if s else -1.0)
             z = end_of("s1", s)
@@ -260,7 +263,7 @@ def plan(rank, n_ranks, bank):
                 ts(col("ex", 4 + s), z, 0.0, col("ex", s - 1), ALU.is_ge, ALU.mult)
                 ts(col("ex", s), z, col("ex", 4 + s), step, ALU.add, ALU.add)
         ts(R("low", c, c + SG), wseg(u, s), o, None, ALU.is_le)
-        if cfg["rc"][NSEG * u + s] == "a":
+        if cfg["rc"][4 * u + s] == "a":
             act(R("rc", c, c + SG), wseg(u, s), ACT.Relu, bias=-o)
         else:
             ts(R("rc", c, c + SG), wseg(u, s), o, 0.0, ALU.subtract, ALU.max)
@@ -271,58 +274,54 @@ def plan(rank, n_ranks, bank):
     def export(u):
         e = col("ex", NSEG - 1)
         ts(col("toff", 8), e, -1.0 / U, float(NSEG * WS - EXT - 1), ALU.mult, ALU.min)
-        ts(col("msg%d" % u, 7), e, -0.6, None, ALU.is_ge)
+        ts(col("msg%d" % u, 7), e, -0.6, cf(9), ALU.is_ge, ALU.add)
         gather(R("msg%d" % u, 8, 24), R("w%d" % u, W0 + EXT), col("toff", 8), "v", "copy")
         send(u)
 
     def point(u, s):
-        c, e = s * SG, cfg["bit"][NSEG * u + s]
+        c, k0 = s * SG, s * SS
         if s == 0 and takes:
             add("x", None, [], [("w%d" % u, W0 - 8, W0 + EXT)], 0, arrive=u)
-            ts(col("ini", 0), col("w%d" % u, W0 - 1), cf(9), None, ALU.add)
-        scan("st", s * SS, s * SS + SG + 1, col("ini", s) if s > 0 or takes else -1.0)
+        if s == 0:
+            scan("st", k0, k0 + PW, col("w%d" % u, W0 - 1) if takes else -1.0)
+            scan("st", k0 + PW, k0 + SG + 1, col("st", k0 + PW - 1))
+        else:
+            scan("st", k0, k0 + SG + 1, col("ini", s))
         z = end_of("st", s)
         if s + 1 < NSEG or not takes:
             last = s + 1 == NSEG
-            if last:
-                ts(col("msg%d" % u, 7), z, -0.5, None, ALU.is_ge)
-            else:
-                ts(col("ini", s + 1), z, -0.5, cf(9), ALU.is_ge, ALU.add)
+            ts(col("msg%d" % u, 7) if last else col("ini", s + 1), z, -0.5, cf(9), ALU.is_ge, ALU.add)
             ts(col("toff", 2 * s), z, -1.0 / U, WS - 1.0, ALU.mult, ALU.min)
-            gather(R("msg%d" % u, 8, 24) if last else wseg(u, s + 1, 0, EXT), wseg(u, s, 0, WS), col("toff", 2 * s),
-                   cfg["carry"][NSEG * u + s], "copy")
+            gather(R("msg%d" % u, 8, 24) if last else wseg(u, s + 1, 0, EXT), wseg(u, s, 0), col("toff", 2 * s),
+                   cfg["carry"][4 * u + s], "copy")
             if last:
                 send(u)
         for h in range(0, SG, PW):
             t = tile()
-            mm(t, [(blk("l4" + e, u), R("bit", c + h, c + h + PW), 1), (R("ih"), R("st", s * SS + h, s * SS + h + PW), 1)])
-            act(R("vv", c + h, c + h + PW), t, ACT.Relu, bias=-8.0)
+            mm(t, [(blk("l4", u), R("bit", c + h, c + h + PW), 1), (R("ih"), R("st", k0 + h, k0 + h + PW), 1)])
+            act(R("vv", c + h, c + h + PW), t, ACT.Relu, bias=cf(11))
         t = tile(KC)
         mm(t, [(R("ih"), R("th"), 1)] + wrap("zd", R("vv", c, c + SG)))
-        cp(R("poff", s * KC, (s + 1) * KC), t)
+        cp(R("poff", c // 16, (c + SG) // 16), t)
 
     def apply(u, s):
-        a, b, e = s * SG, (s + 1) * SG, cfg["gb"][NSEG * u + s]
-        edge = 127.5 if u == 0 else 64.5 / 128
-        gather(R("gl", a, b), wseg(u, s, 0, WS), R("poff", a // 16, b // 16), "v", R("low", a, b))
-        if e == "a":
-            act(R("gb", a, b), R("gl", a, b), ACT.Sign, bias=-edge)
-        else:
-            ts(R("gb", a, b), R("gl", a, b), edge, None, ALU.is_ge)
+        c = s * SG
+        a, b = c, c + SG
+        gather(R("gl", a, b), wseg(u, s, 0), R("poff", a // 16, b // 16), "v", R("low", a, b))
+        step01(R("gb", a, b), R("gl", a, b), 127.5 if u == 0 else 64.5, cfg["gb"][4 * u + s], 1.0 if u == 0 else 1.0 / 128)
         t = tile(KC)
-        mm(t, wrap("zc" + cfg["bit"][NSEG * u + s], R("bit", a, b)), last=False)
-        mm(t, wrap("zc" + e, R("gb", a, b)), first=False)
-        ts(R("coff", a // 16, b // 16), t, 4095.0 if e == "a" else 2047.5, None, ALU.add)
-        for h in range(0, SG, PW):
-            a, j = s * SG + h, 2 * s + h // PW
-            b = a + PW
-            gather(R("tg", a, b), R("tab"), R("coff", a // 16, b // 16), cfg["tg"][2 * NSEG * u + j], "table")
+        mm(t, wrap("zc", R("bit", a, b)), last=False)
+        mm(t, wrap("zc", R("gb", a, b)), first=False)
+        cp(R("coff", a // 16, b // 16), t)
+        for a in range(c, c + SG, PW):
+            b, j = a + PW, a // PW
+            gather(R("tg", a, b), R("tab"), R("coff", a // 16, b // 16), cfg["tg"][8 * u + j], "table")
             t = tile()
             mm(t, ([(R("i63"), R("low", a, b), 1)] if u == 0 else [])
-               + [(R("is" if u == 0 else "ib"), R(n, a, b), 1) for n in ("rc", "gl")] + [(R("ib"), R("tg", a, b), 1)])
+               + [(R("is" if u == 0 else "ib"), R(x, a, b), 1) for x in ("rc", "gl")] + [(R("ib"), R("tg", a, b), 1)])
             act(R("sg", a, b), t, ACT.Sign, bias=-64.5 / 128)
             if u + 1 < RU:
-                tt(wseg(u + 1, s, EXT + h, EXT + h + PW), t, R("sg", a, b), ALU.subtract)
+                tt(wseg(u + 1, s, EXT + a - c, EXT + b - c), t, R("sg", a, b), ALU.subtract)
                 continue
             tt(R("gb", a, b), t, R("sg", a, b), ALU.subtract)
             if cfg["out"][j] == "a":

@@ -5,40 +5,44 @@ ACT = ActivationFunctionType
 P, RU, NSEG = 4096, 4, 4
 SG = P // NSEG
 EXT = 16
-WS = SG + EXT
-W0 = 16
+E0, X0 = 8, 32
+WS = SG + X0
 SS = SG + 8
 KC = SG // 16
 PW = 512
 NB = 8
-U = 2.0 ** -13
+NJ = 96
 MG = 12582912.0
+MQ = 3145728.25
+QB = 1536.0
+EMPTY = -1000
 NENG = 8
 
-SCRATCH = {"tab": ("sbuf", [128, P], "bfloat16"), "yo": ("sbuf", [128, P], "bfloat16")}
+SCRATCH = {}
 for _u in range(RU):
-    SCRATCH["w%d" % _u] = ("sbuf", [128, W0 + NSEG * WS], "bfloat16")
-    SCRATCH["msg%d" % _u] = ("sbuf", [128, 24], "bfloat16")
-for _n in ("bit", "low", "rc", "gl", "gb", "tg", "sg"):
+    SCRATCH["w%d" % _u] = ("sbuf", [128, NSEG * WS + E0], "float32")
+    SCRATCH["msg%d" % _u] = ("sbuf", [128, EXT], "float32")
+for _n in ("tab", "yo", "xs", "a", "bit", "gb"):
     SCRATCH[_n] = ("sbuf", [128, P], "bfloat16")
-SCRATCH["rr"] = ("sbuf", [128, NSEG * SS], "bfloat16")
-for _n in ("inc", "st", "s1"):
-    SCRATCH[_n] = ("sbuf", [128, NSEG * SS], "float16")
-for _n in ("gm", "mm", "m1", "ib", "is", "i63"):
-    SCRATCH[_n] = ("sbuf", [128, 128], "bfloat16")
-for _n in ("dk", "oh", "wm", "lb", "l4"):
-    SCRATCH[_n] = ("sbuf", [128, 512], "bfloat16")
+for _n in ("cp", "tg", "qq", "vv", "ao"):
+    SCRATCH[_n] = ("sbuf", [128, P], "float16")
+DIAG = {"ih": 1.0, "iz": -0.5, "im": -1.0, "ie": -1.0 / 4096, "ir": 0.5, "is": 0.5 / 4096, "i513": 513.0, "iq": -256.0,
+        "j513": 513.0 / 256, "j1": 1.0 / 256}
+for _n in DIAG:
+    SCRATCH[_n] = ("sbuf", [128, 128], "float16")
 SCRATCH.update({
-    "vv": ("sbuf", [128, P], "float16"), "one": ("sbuf", [128, 2], "bfloat16"),
+    "st": ("sbuf", [128, NSEG * SS], "float16"), "sj": ("sbuf", [128, P // 2], "float16"), "cc": ("sbuf", [128, SG], "float32"),
+    "ud": ("sbuf", [128, 256], "float16"), "us": ("sbuf", [128, 256], "float16"), "cu": ("sbuf", [128, 256], "float32"),
+    "gp": ("sbuf", [128, 256], "float32"), "mk": ("sbuf", [128, 256], "float32"),
+    "wj": ("sbuf", [128, RU * 112], "bfloat16"), "gc1": ("sbuf", [128, 112], "float32"), "g1": ("sbuf", [128, 112], "float32"),
+    "gw": ("sbuf", [128, 112], "float32"), "gi": ("sbuf", [128, 48], "float32"), "gs": ("sbuf", [128, 48], "float32"),
+    "gt": ("sbuf", [128, 48], "bfloat16"), "jb": ("sbuf", [128, 4], "float32"),
+    "ib": ("sbuf", [128, 128], "bfloat16"), "th": ("sbuf", [128, KC], "bfloat16"), "rn": ("sbuf", [128, 264], "float16"),
+    "vn": ("sbuf", [128, 256], "float16"), "qb": ("sbuf", [128, PW], "bfloat16"),
     "poff": ("sbuf", [128, 256], "uint16"), "coff": ("sbuf", [128, 256], "uint16"), "toff": ("sbuf", [128, 16], "uint16"),
-    "ini": ("sbuf", [128, 4], "float32"), "ex": ("sbuf", [128, 8], "float32"),
     "was": ("sbuf", [128, 4], "bfloat16"), "kcs": ("sbuf", [128, 4], "bfloat16"), "hls": ("sbuf", [128, 8], "float32"),
-    "wa2": ("sbuf", [128, 4], "bfloat16"), "thl": ("sbuf", [128, 4], "float32"), "bhi": ("sbuf", [128, 4], "float32"),
-    "bh2": ("sbuf", [128, 4], "float32"),
-    "jj": ("sbuf", [128, 144], "float32"), "ga": ("sbuf", [128, 128], "float32"), "cm": ("sbuf", [128, 128], "float32"),
-    "ji": ("sbuf", [128, 128], "int32"), "jk": ("sbuf", [128, 128], "int32"), "cf": ("sbuf", [128, 12], "float32"),
-    "pw": ("sbuf", [128, 32], "float32"), "t16": ("sbuf", [128, KC], "float32"), "th": ("sbuf", [128, KC], "float16"),
-    "ih": ("sbuf", [128, 128], "float16"), "zd": ("sbuf", [128, 144], "float16"), "zc": ("sbuf", [128, 144], "bfloat16"),
+    "jj": ("sbuf", [128, 144], "float32"), "cm": ("sbuf", [128, 16], "float32"), "cf": ("sbuf", [128, 12], "float32"),
+    "pw": ("sbuf", [128, 16], "float32"), "zd": ("sbuf", [128, 144], "float16"), "zc": ("sbuf", [128, 144], "bfloat16"),
 })
 for _k in range(NB):
     SCRATCH["p%d" % _k] = ("psum", [128, PW], "float32")
@@ -49,13 +53,15 @@ SEMAPHORES = (["qv", "qa", "qp", "qg", "sent"] + ["arr%d" % u for u in range(RU)
 CY, PCY, GA, FIX, LAT, WIRE = 0.95, 0.48, 1.56, 60.0, 130.0, 2500.0
 ROUNDS, SLACK = 10, 60.0
 
-BASE = {"bit": "aaaaaava" + "v" * 24, "gb": "avvv" * 4, "rc": "a" * 16, "tg": "a" * 32, "carry": "a" + "v" * 15, "out": "v" * 8}
-CFG = {0: BASE, 1: dict(BASE, bit="aaaaaavavvvvaavaavvvaavavvvvaava"), 2: dict(BASE, bit="aaaaaavavvvvaavavvvvaavavvvvaava"),
-       3: dict(BASE, tg="a" * 8 + "aaaaaava" * 3)}
+CFG = {"win": "a", "tg": "a", "qq": "a", "own": "a", "carry": "a", "shift": "v", "half": "a", "out": "v", "mod": "v"}
+CFG.update({("mod", _u, _j): "p" for _u in range(RU) for _j in range(1, 2 * NSEG, 2)})
 
 
 def plan(rank, n_ranks, bank):
-    ops, cfg = [], CFG[rank]
+    ops = []
+
+    def eng(kind, u, j):
+        return CFG.get((kind, rank, u, j), CFG.get((kind, u, j), CFG.get((kind, u), CFG[kind])))
 
     def add(q, fn, rd, wr, cost, **kw):
         d = {"q": q, "fn": fn, "rd": rd, "wr": wr, "cost": cost}
@@ -63,96 +69,103 @@ def plan(rank, n_ranks, bank):
         ops.append(d)
         return d
 
-    def R(name, a=0, b=None):
-        return (name, a, SCRATCH[name][1][1] if b is None else b)
+    def R(name, a=0, b=None, step=1):
+        return (name, a, SCRATCH[name][1][1] if b is None else b, step, 0, 128)
+
+    def part(r, p0, p1):
+        return r[:4] + (p0, p1)
+
+    def size(r):
+        return len(range(r[1], r[2], r[3]))
 
     def ap(T, r):
-        return T["p%d" % bank[(rank, r[0])] if r[0][0] == "@" else r[0]][:, r[1]:r[2]]
+        if not isinstance(r, tuple):
+            return r
+        t = T["p%d" % bank[(rank, r[0])] if r[0][0] == "@" else r[0]]
+        return t[r[4]:r[5], r[1]:r[2]:r[3]] if r[3] > 1 else t[r[4]:r[5], r[1]:r[2]]
 
-    def vcost(rs, n):
-        half = all(r[0][0] != "@" and SCRATCH[r[0]][2] in ("bfloat16", "float16", "uint16") for r in rs)
-        return FIX + max(64, n * (0.5 if half else 1.0)) * CY
+    def kind(r):
+        return "float32" if r[0][0] == "@" else SCRATCH[r[0]][2]
+
+    def vcost(rs):
+        half = all(kind(r) in ("bfloat16", "float16", "uint16") for r in rs)
+        return FIX + max(64, size(rs[0]) * (0.5 if half else 1.0)) * CY
 
     def ts(out, in0, s1, s2, op0, op1=None):
         rd = [in0] + [s for s in (s1, s2) if isinstance(s, tuple)]
 
         def fn(g, T):
-            a = ap(T, s1) if isinstance(s1, tuple) else s1
-            b = ap(T, s2) if isinstance(s2, tuple) else s2
             if op1 is None:
-                return g.vector.tensor_scalar(ap(T, out), ap(T, in0), a, None, op0)
-            return g.vector.tensor_scalar(ap(T, out), ap(T, in0), a, b, op0, op1)
-        return add("v", fn, rd, [out], vcost([out, in0], in0[2] - in0[1]))
+                return g.vector.tensor_scalar(ap(T, out), ap(T, in0), ap(T, s1), None, op0)
+            return g.vector.tensor_scalar(ap(T, out), ap(T, in0), ap(T, s1), ap(T, s2), op0, op1)
+        return add("v", fn, rd, [out], vcost([out, in0]))
 
     def tt(out, in0, in1, op):
         f = 1 if "@" in (in0[0][0], in1[0][0]) else 2
         return add("v", lambda g, T: g.vector.tensor_tensor(ap(T, out), ap(T, in0), ap(T, in1), op), [in0, in1], [out],
-                   FIX + max(64, f * (out[2] - out[1])) * CY)
+                   FIX + max(64, f * size(out)) * CY)
 
     def cp(out, in0):
-        return add("v", lambda g, T: g.vector.tensor_copy(ap(T, out), ap(T, in0)), [in0], [out], vcost([out, in0], out[2] - out[1]))
+        return add("v", lambda g, T: g.vector.tensor_copy(ap(T, out), ap(T, in0)), [in0], [out], vcost([out, in0]))
 
-    def product(out, in0):
-        return add("v", lambda g, T: g.vector.tensor_reduce(ap(T, out), ap(T, in0), AxisListType.X, ALU.mult), [in0], [out], FIX + 64)
-
-    def scan(out, a, b, init):
-        d0, d1, o = R("rr", a, b), R("inc", a, b), R(out, a, b)
-        rd = [d0, d1] + ([init] if isinstance(init, tuple) else [])
-        return add("v", lambda g, T: g.vector.tensor_tensor_scan(ap(T, o), ap(T, d0), ap(T, d1),
-                   ap(T, init) if isinstance(init, tuple) else init, ALU.mult, ALU.add), rd, [o], vcost([o], b - a))
+    def fill(out, c):
+        return add("v", lambda g, T: g.vector.memset(ap(T, out), c), [], [out], vcost([out]))
 
     def act(out, in0, func, bias=0.0, scale=1.0):
-        rd = [in0] + ([bias] if isinstance(bias, tuple) else [])
-        return add("a", lambda g, T: g.scalar.activation(ap(T, out), ap(T, in0), func,
-                   bias=ap(T, bias) if isinstance(bias, tuple) else bias, scale=scale), rd, [out], FIX + max(64, out[2] - out[1]) * CY)
+        rd = [in0] + [s for s in (bias, scale) if isinstance(s, tuple)]
+        return add("a", lambda g, T: g.scalar.activation(ap(T, out), ap(T, in0), func, bias=ap(T, bias), scale=ap(T, scale)),
+                   rd, [out], FIX + max(64, size(out)) * CY)
+
+    def affine(e, out, in0, scale, bias):
+        if e == "a":
+            return act(out, in0, ACT.Identity, bias=bias, scale=scale)
+        return ts(out, in0, scale, bias, ALU.mult, ALU.add)
 
     def mm(out, terms, first=True, last=True):
         def fn(g, T):
-            for k, (l, r, step) in enumerate(terms):
-                ins = g.tensor.matmul(ap(T, out), ap(T, l), T[r[0]][:, r[1]:r[2]:step] if step > 1 else ap(T, r),
+            for k, t in enumerate(terms):
+                ins = g.tensor.matmul(ap(T, t[2] if len(t) > 2 else out), ap(T, t[0]), ap(T, t[1]),
                                       first and k == 0, last and k == len(terms) - 1)
             return ins
-        return add("p", fn, [t[0] for t in terms] + [t[1] for t in terms], [out], 30 + len(terms) * max(64, out[2] - out[1]) * PCY)
+        cost = sum(max(64, size(out)) * PCY * (4 if kind(t[0]) == "float32" else 1) for t in terms)
+        return add("p", fn, [t[0] for t in terms] + [t[1] for t in terms], [out], 30 + cost)
 
     def wrap(z, src):
-        return [(R(z, 15 - i, 143 - i), (src[0], src[1] + i, src[2]), 16) for i in range(16)]
+        return [(R(z, 15 - i, 143 - i), R(src[0], src[1] + i, src[2], 16)) for i in range(16)]
 
-    def gather(out, win, off, q, kind):
+    def gather(out, win, off, q, how):
         def fn(g, T):
             src = ap(T, win).indirect(ap(T, off))
             if q == "a":
-                if kind == "copy":
+                if how == "copy":
                     return g.scalar.activation(ap(T, out), src, ACT.Copy)
-                return g.scalar.activation(ap(T, out), src, ACT.Identity, bias=-1.0, scale=1.0 / 128)
-            if kind == "table":
-                return g.vector.tensor_scalar(ap(T, out), src, 1.0 / 128, -1.0, ALU.mult, ALU.add)
-            if kind == "copy":
+                return g.scalar.activation(ap(T, out), src, ACT.Identity, bias=0.375)
+            if how == "table":
+                return g.vector.tensor_scalar(ap(T, out), src, 0.375, None, ALU.add)
+            if how == "copy":
                 return g.vector.tensor_copy(ap(T, out), src)
-            return g.vector.tensor_tensor(ap(T, out), src, ap(T, kind), ALU.mult)
-        return add(q, fn, [win, off] + ([kind] if isinstance(kind, tuple) else []), [out], FIX + max(64, (out[2] - out[1]) * GA) * CY)
+            return g.vector.tensor_tensor(ap(T, out), src, ap(T, how), ALU.max)
+        return add(q, fn, [win, off] + ([how] if isinstance(how, tuple) else []), [out], FIX + max(64, size(out) * GA) * CY)
 
-    def iota(out, pat, base, mult):
+    def iota(out, pat, base, mult=0):
         return add("g", lambda g, T: g.iota(ap(T, out), pat, base, mult, allow_small_or_imprecise_dtypes=True), [], [out],
-                   130 + 2 * (out[2] - out[1]) * CY)
+                   130 + 2 * size(out) * CY)
 
     num = {"ld": 0, "so": 0, "@": 0}
 
-    def fresh(kind):
-        num[kind] += 1
-        return "%s%d" % (kind, num[kind] - 1)
+    def fresh(k):
+        num[k] += 1
+        return "%s%d" % (k, num[k] - 1)
 
-    def tile(n=PW):
-        return (fresh("@"), 0, n)
+    def tile(n=PW, rows=128):
+        return (fresh("@"), 0, n, 1, 0, rows)
 
     def load(q, out, src, a, b):
         add(q, lambda g, T: (g.sync if q == "s" else g.scalar).dma_start(ap(T, out), T[src][:, a:b]), [], [out], 100,
             sem=fresh("ld"), inc=16, dma=(b - a) * 256)
 
-    def wseg(u, s, a=EXT, b=WS):
-        return ("w%d" % u, W0 + s * WS + a, W0 + s * WS + b)
-
-    def blk(name, u):
-        return R(name, 128 * u, 128 * u + 128)
+    def wseg(u, s, a, b):
+        return R("w%d" % u, s * WS + a, s * WS + b)
 
     def col(name, k):
         return R(name, k, k + 1)
@@ -160,182 +173,173 @@ def plan(rank, n_ranks, bank):
     def cf(k):
         return col("cf", k)
 
+    sends, takes = rank + 1 < n_ranks, rank > 0
+
     load("a", R("kcs"), "kc", 0, 4)
     load("a", R("was"), "wa", 0, 4)
     load("a", R("hls"), "hl", 0, 8)
-    load("s", wseg(0, 0, EXT, EXT + PW), "x", 0, PW)
-    load("s", wseg(0, 0, EXT + PW, WS), "x", PW, SG)
-    for s in range(1, NSEG):
-        load("s", wseg(0, s), "x", s * SG, (s + 1) * SG)
+    for s in range(NSEG):
+        load("s", R("xs", s * SG, (s + 1) * SG), "x", s * SG, (s + 1) * SG)
     load("s", R("tab", 0, P // 2), "inv", 0, P // 2)
     load("s", R("tab", P // 2, P), "inv", P // 2, P)
 
     iota(cf(0), [[0, 1]], -15, 2)
     iota(cf(7), [[0, 1]], 0, 1)
-    iota(R("cm"), [[0, 8], [1, 16]], 0, 0)
-    iota(R("ga"), [[1, 8], [0, 16]], int(MG), 0)
+    iota(R("gc1"), [[0, 7], [1, 16]], int(MG) - 8)
+    iota(R("gi"), [[100, 3], [0, 2], [1, 8]], int(MG) - 100)
+    for end, v in ((NJ, -1), (32, 1), (16, 0)):
+        iota(part(cf(4), 0, end), [[0, 1]], v)
+    iota(part(cf(10), NJ, NJ + 2), [[0, 1]], 1, -1)
+    iota(R("cc", 0, PW), [[-2, PW]], 2047)
+    iota(R("gp"), [[8, 2], [1, 8], [0, 16]], 0)
+    for a in (1, 0, 3, 2, 5, 4):
+        j = a - 2
+        pat, base = ([[0, 128 >> j], [-4096, 2], [0, 1 << j]], 2048) if a > 1 else ([[0, 256]], (-2048, 16384)[a])
+        iota(part(R("cu"), 16 * (a - a % 2), 16 * a + 16), pat, base)
+    for h in range(2):
+        iota(part(R("cu", 128 * h, 128 * h + 128), NJ, NJ + 2), [[0, 128]], 1, -6145 - 1024 * h)
     iota(R("jj"), [[1, 144]], 0, -1)
-    iota(R("t16"), [[16, KC]], EXT, 0)
-    iota(col("one", 0), [[0, 1]], 1, 0)
-    for s in range(NSEG):
-        iota(col("rr", s * SS), [[0, 1]], 1, 0)
-        act(col("inc", s * SS + SG), col("one", 0), ACT.Copy, scale=-(WS - 1) * U)
+    iota(R("cm"), [[1, 16]], 0)
+    iota(R("cc", PW, SG), [[-2, PW]], 2047 - 2 * PW)
     ts(cf(1), cf(0), 1.0 / 32, MG, ALU.mult, ALU.add)
+    ts(R("g1"), R("gc1"), cf(1), None, ALU.is_equal)
+    for j in range(4):
+        ts(R("gw", 40 + 16 * j, 56 + 16 * j), R("g1", 40 + 16 * j, 56 + 16 * j), 2.0 ** j + 1, -1.0, ALU.mult, ALU.add)
+    for u in range(RU):
+        ts(R("wj", 112 * u, 112 * u + 40), R("g1", 0, 40), col("was", u), None, ALU.mult)
+        ts(R("wj", 112 * u + 40, 112 * u + 104), R("gw", 40, 104), col("kcs", u), None, ALU.is_equal)
+    ts(R("gs"), R("gi"), cf(1), -1.0 / 16, ALU.is_equal, ALU.mult)
+    ts(R("gt"), R("gi"), cf(1), 64.0, ALU.is_equal, ALU.mult)
+    fill(R("jb"), -63.5)
+    fill(col("jb", 0), -127.5)
+    t = tile(RU, 32)
+    later = (t[0], 1, RU, 1, 0, 32)
+    mm(t, [(R("gs", 16, 48), R("hls", 0, RU)), (R("gt", 16, 48), R("was", 1, RU), later), (R("gt", 0, 32), R("was", 1, RU), later),
+           (R("gs", 0, 32), R("hls", RU, 2 * RU))])
+    ts(part(R("jb"), 0, 32), t, part(cf(4), 0, 32), 0.5, ALU.subtract, ALU.add)
     ts(cf(2), cf(1), MG, -16.0, ALU.subtract, ALU.mult)
     ts(cf(8), cf(7), cf(2), None, ALU.add)
-    ts(R("gm"), R("ga"), cf(1), None, ALU.is_equal)
+    ts(R("mk"), R("gp"), cf(8), None, ALU.is_equal)
+    tt(part(R("ud"), 0, NJ), part(R("cu"), 0, NJ), part(R("mk"), 0, NJ), ALU.mult)
+    act(part(R("ud"), NJ, NJ + 2), part(R("cu"), NJ, NJ + 2), ACT.Copy)
+    ts(part(R("us"), 0, NJ), part(R("ud"), 0, NJ), part(cf(4), 0, NJ), None, ALU.mult)
+    for s in range(NSEG):
+        act(part(R("sj", s * PW, (s + 1) * PW), NJ, NJ + 2), part(R("cc", 0, PW), NJ, NJ + 2), ACT.Identity, bias=1.0,
+            scale=part(cf(10), NJ, NJ + 2))
+    ts(cf(9), cf(8), -2.0, 2.0 * (WS - E0), ALU.mult, ALU.add)
+    ts(R("st", 0, NSEG * SS, SS), R("cm", 0, NSEG), 0.0, cf(9), ALU.mult, ALU.add)
     ts(R("ib"), R("jj", 0, 128), 0.0, None, ALU.is_equal)
-    ts(R("pw", 0, 16), R("cm", 0, 16), cf(8), 1.0, ALU.is_lt, ALU.add)
-    ts(R("pw", 16, 32), R("cm", 0, 16), cf(8), 0.5, ALU.is_ge, ALU.max)
-    product(cf(3), R("pw", 0, 16))
-    product(cf(4), R("pw", 16, 32))
-    ts(R("ji"), R("cm"), cf(4), -0.4375, ALU.mult, ALU.add)
-    ts(R("jk"), R("ji"), 1, None, ALU.bitwise_and)
-    ts(R("m1"), R("jk"), -2.0, 1.0, ALU.mult, ALU.add)
-    tt(R("mm"), R("m1"), R("gm"), ALU.mult)
-    for u in range(RU):
-        ts(blk("wm", u), R("gm"), col("was", u), -2.0 if u == 0 else -256.0, ALU.mult, ALU.mult)
-        ts(blk("dk", u), R("ib"), col("kcs", u), None, ALU.mult)
-        t, t2 = tile(128), tile(128)
-        mm(t, [(R("gm"), blk("dk", u), 1)])
-        ts(blk("oh", u), t, cf(3), None, ALU.is_equal)
-        mm(t2, [(blk("oh", u), R("mm"), 1)])
-        act(blk("lb", u), t2, ACT.Copy, scale=65536.0)
-        act(blk("l4", u), t2, ACT.Copy, scale=-4.0)
-    t = tile(1)
-    mm(t, [(R("mm"), col("one", 0), 1)])
-    ts(cf(10), t, -32768.0, 524287.0, ALU.mult, ALU.add)
-    ts(cf(11), t, 2.0, -32.0, ALU.mult, ALU.add)
-    ts(R("thl"), R("hls", 4, 8), -2.0, None, ALU.mult)
-    ts(R("bhi"), R("hls", 0, 4), 2.0, cf(10), ALU.mult, ALU.add)
-    ts(col("bh2", 0), col("bhi", 0), 128.0, None, ALU.mult)
-    ts(R("wa2"), R("was"), 126.0, None, ALU.mult)
-    t = tile(4)
-    mm(t, [(R("gm"), R("wa2"), 1)])
-    tt(R("thl", 1, 4), R("thl", 1, 4), (t[0], 1, 4), ALU.add)
-    tt(R("bhi", 1, 4), R("bhi", 1, 4), (t[0], 1, 4), ALU.subtract)
-    ts(R("bh2", 1, 4), R("bhi", 1, 4), 128.0, None, ALU.mult)
-    for n, f in (("ih", 1.0), ("is", 1.0 / 128), ("i63", -63.0 / 128)):
+    for n, f in sorted(DIAG.items()):
         act(R(n), R("ib"), ACT.Copy, scale=f)
+    fill(R("th"), -WS / 4096.0)
+    fill(R("qb"), QB)
+    ts(R("pw"), R("cm"), cf(8), 1.0, ALU.is_lt, ALU.add)
+    add("v", lambda g, T: g.vector.tensor_reduce(ap(T, cf(3)), ap(T, R("pw")), AxisListType.X, ALU.mult), [R("pw")], [cf(3)], FIX + 64)
     ts(cf(5), cf(3), 4000.0, cf(3), ALU.is_lt, ALU.mult)
     ts(cf(6), cf(8), -1.0, 15.0, ALU.mult, ALU.add)
-    ts(cf(9), cf(6), U, -1.0, ALU.mult, ALU.add)
-    ts(R("zd"), R("jj"), cf(6), -1.0 / U, ALU.is_equal, ALU.mult)
+    ts(R("zd"), R("jj"), cf(6), -0.5, ALU.is_equal, ALU.mult)
     ts(R("zc"), R("jj"), cf(6), cf(5), ALU.is_equal, ALU.mult)
-    ts(R("th"), R("t16"), cf(8), None, ALU.add)
-    sends, takes = rank + 1 < n_ranks, rank > 0
     for u in range(RU):
-        if sends:
-            iota(R("msg%d" % u, 0, 8), [[0, 8]], 0, 0)
-        for s in range(NSEG):
-            if (s == 0 and not takes) or (s > 0 and sends and takes):
-                iota(wseg(u, s, 0, EXT), [[0, EXT]], 0, 0)
+        for s in range(NSEG + 1):
+            for a, b in ((0, E0), (E0 + EXT, X0)) if s == 0 and takes else ((0, X0 if s < NSEG else E0),):
+                iota(wseg(u, s, a, b), [[0, b - a]], EMPTY)
 
-    def end_of(name, s):
-        return col(name, s * SS + SG)
-
-    def step01(out, in0, edge, e, f):
-        if e == "a":
-            act(out, in0, ACT.Sigmoid, bias=-edge * 256.0, scale=256.0 / f)
-        else:
-            ts(out, in0, edge * f, None, ALU.is_ge)
+    def offsets(e, t, r0, out):
+        v, r, t2 = R("vn", r0, r0 + size(t)), R("rn", r0, r0 + size(t)), tile(size(t))
+        affine(e, v, t, 1.0, 0.0)
+        ts(r, v, MG, MG, ALU.add, ALU.subtract)
+        mm(t2, [(R("ib"), R("th", 0, size(t))), (R("ih"), v), (R("im"), r), (R("ie"), r)])
+        ts(out, t2, -4096.0, float(WS), ALU.mult, ALU.min)
 
     def judge(u, s):
-        o, f = (63.0, 1.0) if u == 0 else (0.0, 1.0 / 128)
-        c, k0 = s * SG, s * SS
-        for h in range(0, SG, PW):
-            w, b, k = wseg(u, s, EXT + h, EXT + h + PW), R("bit", c + h, c + h + PW), k0 + h
-            step01(b, w, 64.5 + o, cfg["bit"][8 * u + (c + h) // PW], f)
-            t, t2 = tile(), tile()
-            mm(t, [(blk("wm", u), w, 1)])
-            ts(R("inc", k, k + PW), t, col("thl", u), 1.0 - U, ALU.is_lt, ALU.subtract)
-            mm(t2, [(blk("wm", u), w, 1), (blk("lb", u), b, 1)])
-            act(R("rr", k + 1, k + 1 + PW), t2, ACT.Sigmoid, bias=col("bh2", u), scale=128.0)
-        if sends and takes:
-            cuts = [k0, k0 + SG - PW, k0 + SG + 1] if s + 1 == NSEG else [k0, k0 + SG + 1]
-            for a, b in zip(cuts, cuts[1:]):
-                scan("s1", a, b, col("s1", a - 1) if a > k0 else SG * U if s else -1.0)
-            z = end_of("s1", s)
-            step = (EXT - s * WS) * U if s + 1 == NSEG else (WS - (2 * SG - WS + 1)) * U
-            if s == 0:
-                ts(col("ex", 0), z, step, None, ALU.add)
-            else:
-                ts(col("ex", 4 + s), z, 0.0, col("ex", s - 1), ALU.is_ge, ALU.mult)
-                ts(col("ex", s), z, col("ex", 4 + s), step, ALU.add, ALU.add)
-        ts(R("low", c, c + SG), wseg(u, s), o, None, ALU.is_le)
-        if cfg["rc"][4 * u + s] == "a":
-            act(R("rc", c, c + SG), wseg(u, s), ACT.Relu, bias=-o)
-        else:
-            ts(R("rc", c, c + SG), wseg(u, s), o, 0.0, ALU.subtract, ALU.max)
+        c, k0, x = s * SG, s * SS, "a" if u else "xs"
+        t, sj = tile(PW, NJ), R("sj", s * PW, (s + 1) * PW)
+        mm(t, [(R("wj", 112 * u + 8 - 8 * h, 112 * u + 104 - 8 * h), R(x, c + h * PW, c + (h + 1) * PW)) for h in range(2)])
+        act(part(sj, 0, NJ), t, ACT.Sign, bias=part(col("jb", u), 0, NJ))
+        for h in range(2):
+            t, k = tile(), k0 + h * PW
+            mm(t, [(part(R("ud", 128 * h, 128 * h + 128), 0, NJ + 2), part(sj, 0, NJ + 2))])
+            o, d1, init = R("st", k + 1, k + 1 + PW), R("cc", h * PW, (h + 1) * PW), col("st", k)
+            add("v", lambda g, T, o=o, t=t, d1=d1, init=init: g.vector.tensor_tensor_scan(
+                ap(T, o), ap(T, t), ap(T, d1), ap(T, init), ALU.min, ALU.max), [t, d1, init], [o], vcost([o, t]))
+        affine(eng("win", u, s), wseg(u, s, X0, WS), R(x, c, c + SG), 1.0 / 512, -0.5 if u else -0.625)
 
-    def send(u):
-        add("g", None, [R("msg%d" % u)], [], 300, send=u)
+    def ends(s0, s1):
+        z, r, t = R("st", s0 * SS + SG, (s1 - 1) * SS + SG + 1, SS), R("rn", 256 + s0, 256 + s1), tile(s1 - s0)
+        ts(r, z, 2 * MG, 2 * MG, ALU.add, ALU.subtract)
+        mm(t, [(R("ib"), R("th", 0, s1 - s0)), (R("iz"), z), (R("ir"), r), (R("is"), r)])
+        ts(R("toff", 2 * s0, 2 * s1 - 1, 2), t, -4096.0, float(WS), ALU.mult, ALU.min)
 
-    def export(u):
-        e = col("ex", NSEG - 1)
-        ts(col("toff", 8), e, -1.0 / U, float(NSEG * WS - EXT - 1), ALU.mult, ALU.min)
-        ts(col("msg%d" % u, 7), e, -0.6, cf(9), ALU.is_ge, ALU.add)
-        gather(R("msg%d" % u, 8, 24), R("w%d" % u, W0 + EXT), col("toff", 8), "v", "copy")
-        send(u)
+    def carry(u, s, off, first=0):
+        out = wseg(u, s + 1, E0, E0 + EXT) if s + 1 < NSEG else R("msg%d" % u)
+        gather(out, wseg(u, s, first, WS + 1), col("toff", off), eng("carry", u, s), "copy")
+
+    def hand_on(u):
+        ends(0, NSEG - 1)
+        if sends:
+            if takes:
+                ts(col("toff", 8), col("toff", 0), float(E0 + EXT), None, ALU.subtract)
+                carry(u, 0, 8, E0 + EXT)
+            for s in range(1 if takes else 0, NSEG - 1):
+                carry(u, s, 2 * s)
+            ends(NSEG - 1, NSEG)
+            carry(u, NSEG - 1, 2 * NSEG - 2)
+            add("g", None, [R("msg%d" % u)], [], 300, send=u)
+        if takes:
+            add("x", None, [], [wseg(u, 0, E0, E0 + EXT)], 0, arrive=u)
+            for s in range(NSEG - 1):
+                carry(u, s, 2 * s)
 
     def point(u, s):
         c, k0 = s * SG, s * SS
-        if s == 0 and takes:
-            add("x", None, [], [("w%d" % u, W0 - 8, W0 + EXT)], 0, arrive=u)
-        if s == 0:
-            scan("st", k0, k0 + PW, col("w%d" % u, W0 - 1) if takes else -1.0)
-            scan("st", k0 + PW, k0 + SG + 1, col("st", k0 + PW - 1))
-        else:
-            scan("st", k0, k0 + SG + 1, col("ini", s))
-        z = end_of("st", s)
-        if s + 1 < NSEG or not takes:
-            last = s + 1 == NSEG
-            ts(col("msg%d" % u, 7) if last else col("ini", s + 1), z, -0.5, cf(9), ALU.is_ge, ALU.add)
-            ts(col("toff", 2 * s), z, -1.0 / U, WS - 1.0, ALU.mult, ALU.min)
-            gather(R("msg%d" % u, 8, 24) if last else wseg(u, s + 1, 0, EXT), wseg(u, s, 0), col("toff", 2 * s),
-                   cfg["carry"][4 * u + s], "copy")
-            if last:
-                send(u)
-        for h in range(0, SG, PW):
-            t = tile()
-            mm(t, [(blk("l4", u), R("bit", c + h, c + h + PW), 1), (R("ih"), R("st", k0 + h, k0 + h + PW), 1)])
-            act(R("vv", c + h, c + h + PW), t, ACT.Relu, bias=cf(11))
+        for h in range(2):
+            t, o = tile(), R("vv", c + h * PW, c + (h + 1) * PW)
+            mm(t, [(part(R("us", 128 * h, 128 * h + 128), 0, NJ), part(R("sj", s * PW, (s + 1) * PW), 0, NJ)),
+                   (R("ih"), R("st", k0 + h * PW, k0 + (h + 1) * PW))])
+            if eng("own", u, 2 * s + h) == "a":
+                act(o, t, ACT.Relu, bias=-24576.0)
+            else:
+                ts(o, t, -24576.0, 0.0, ALU.add, ALU.max)
         t = tile(KC)
-        mm(t, [(R("ih"), R("th"), 1)] + wrap("zd", R("vv", c, c + SG)))
-        cp(R("poff", c // 16, (c + SG) // 16), t)
+        mm(t, wrap("zd", R("vv", c, c + SG)))
+        offsets(eng("half", u, s), t, s * KC, R("poff", s * KC, (s + 1) * KC))
+        ts(R("bit", c, c + SG), R("a" if u else "xs", c, c + SG), 63.5 if u else 127.5, None, ALU.is_ge)
+        if u == 0:
+            affine(eng("shift", u, s), R("a", c, c + SG), R("xs", c, c + SG), 1.0, -64.0)
 
     def apply(u, s):
-        c = s * SG
-        a, b = c, c + SG
-        gather(R("gl", a, b), wseg(u, s, 0), R("poff", a // 16, b // 16), "v", R("low", a, b))
-        step01(R("gb", a, b), R("gl", a, b), 127.5 if u == 0 else 64.5, cfg["gb"][4 * u + s], 1.0 if u == 0 else 1.0 / 128)
+        a, b = s * SG, (s + 1) * SG
+        gather(R("cp", a, b), wseg(u, s, 0, WS + 1), R("poff", a // 16, b // 16), "v", R("a", a, b))
+        ts(R("gb", a, b), R("cp", a, b), MQ, MQ - 0.25, ALU.add, ALU.is_equal)
         t = tile(KC)
         mm(t, wrap("zc", R("bit", a, b)), last=False)
         mm(t, wrap("zc", R("gb", a, b)), first=False)
         cp(R("coff", a // 16, b // 16), t)
-        for a in range(c, c + SG, PW):
+        for a in range(s * SG, (s + 1) * SG, PW):
             b, j = a + PW, a // PW
-            gather(R("tg", a, b), R("tab"), R("coff", a // 16, b // 16), cfg["tg"][8 * u + j], "table")
-            t = tile()
-            mm(t, ([(R("i63"), R("low", a, b), 1)] if u == 0 else [])
-               + [(R("is" if u == 0 else "ib"), R(x, a, b), 1) for x in ("rc", "gl")] + [(R("ib"), R("tg", a, b), 1)])
-            act(R("sg", a, b), t, ACT.Sign, bias=-64.5 / 128)
-            if u + 1 < RU:
-                tt(wseg(u + 1, s, EXT + a - c, EXT + b - c), t, R("sg", a, b), ALU.subtract)
-                continue
-            tt(R("gb", a, b), t, R("sg", a, b), ALU.subtract)
-            if cfg["out"][j] == "a":
-                act(R("yo", a, b), R("gb", a, b), ACT.Identity, bias=63.0, scale=128.0)
+            gather(R("tg", a, b), R("tab"), R("coff", a // 16, b // 16), eng("tg", u, j), "table")
+            t, out, less = tile(), R("a" if u + 1 < RU else "yo", a, b), 64.0 if u + 1 < RU else 0.0
+            if eng("mod", u, j) == "p":
+                terms, t2 = [(R("i513"), R("cp", a, b)), (R("ih"), R("tg", a, b))], tile()
+                mm(t, terms)
+                affine(eng("qq", u, j), R("qq", a, b), t, 1.0 / 256, QB - 63.5 / 256)
+                mm(t2, terms, last=False)
+                mm(t2, [(R("iq"), R("qq", a, b))], first=False)
+                ts(out, t2, MG + 256 * QB, MG - 64 + less, ALU.add, ALU.subtract)
             else:
-                ts(R("yo", a, b), R("gb", a, b), 128.0, 63.0, ALU.mult, ALU.add)
+                mm(t, [(R("ib"), R("qb")), (R("j513"), R("cp", a, b)), (R("j1"), R("tg", a, b))])
+                affine(eng("qq", u, j), R("qq", a, b), t, 1.0, -5 - 63.5 / 256)
+                tt(R("ao", a, b), t, R("qq", a, b), ALU.subtract)
+                affine(eng("out", u, j), out, R("ao", a, b), 256.0, 64.0 - 1280 - less)
+            if u + 1 < RU:
+                continue
             add("s", lambda g, T, a=a, b=b: g.sync.dma_start(T["y"][:, a:b], T["yo"][:, a:b]), [R("yo", a, b)], [], 100,
                 sem=fresh("so"), inc=16, dma=PW * 256)
 
     for s in range(NSEG):
         judge(0, s)
     for u in range(RU):
-        if sends and takes:
-            export(u)
+        hand_on(u)
         for s in range(NSEG):
             point(u, s)
         for s in range(NSEG):
@@ -351,21 +355,33 @@ def link(ops):
         dep = set()
         acc = [(r, False) for r in o["rd"]] + [(r, True) for r in o["wr"]]
         for r, w in acc:
-            for (j, a, b, wj) in seen.get(r[0], []):
-                if r[0][0] == "@" or ((w or wj) and a < r[2] and r[1] < b):
+            for (j, e, wj) in seen.get(r[0], []):
+                if r[0][0] == "@" or ((w or wj) and meet(e, r)):
                     dep.add(j)
         for r, w in acc:
             if r[0][0] == "@":
-                o["tile"], o["opens"] = r[0], r[0] not in seen
-                seen[r[0]] = [(i, 0, 0, True)]
+                o["tile"], o["opens"] = r[0], o.get("opens") or r[0] not in seen
+                seen[r[0]] = [(i, r, True)]
             else:
-                keep = [e for e in seen.get(r[0], []) if not (w and r[1] <= e[1] and e[2] <= r[2])]
-                seen[r[0]] = keep + [(i, r[1], r[2], w)]
+                keep = [x for x in seen.get(r[0], []) if not (w and covers(r, x[1]))]
+                seen[r[0]] = keep + [(i, r, w)]
         dep.discard(i)
         o["dep"] = sorted(dep)
     for name in seen:
         if name[0] == "@":
             ops[seen[name][0][0]]["closes"] = True
+
+
+def meet(a, b):
+    if a[4] >= b[5] or b[4] >= a[5] or a[1] >= b[2] or b[1] >= a[2]:
+        return False
+    if a[3] < b[3]:
+        a, b = b, a
+    return a[3] == 1 or b[3] > 1 or any(b[1] <= k < b[2] for k in range(a[1], a[2], a[3]))
+
+
+def covers(a, b):
+    return a[3] == 1 and a[1] <= b[1] and b[2] <= a[2] and a[4] <= b[4] and b[5] <= a[5]
 
 
 def sweep(ops, pre, key, back):
@@ -452,13 +468,17 @@ def schedule(n_ranks):
     return CACHE[n_ranks]
 
 
+def message(u, there, here):
+    return there["w%d" % u][:, E0:E0 + EXT], here["msg%d" % u][:]
+
+
 def rank_program(g, core, T, topo):
     rank = T.rank_of(core)
     if rank is None:
         return
     ops, seq = schedule(len(T.cores))[:2]
     queue = {"v": g.vector, "a": g.scalar, "p": g.tensor, "g": g, "s": g.sync}
-    count, mark, known, sent = {}, {}, {}, 0
+    count, mark, known, sent, alone = {}, {}, {}, 0, False
 
     def wait(q, sem, val):
         if known.get((q, sem), 0) < val:
@@ -477,13 +497,18 @@ def rank_program(g, core, T, topo):
         for j in o["dep"]:
             if not (q == "p" and ops[j]["q"] == "p"):
                 need[mark[j][0]] = max(need.get(mark[j][0], 0), mark[j][1])
+        if q == "g" and "send" not in o:
+            if alone or o["wr"][0][4]:
+                need["qg"] = count.get("qg", 0)
+            alone = o["wr"][0][4] > 0
         for sem in sorted(need):
             wait(q, sem, need[sem])
         if "send" in o:
             u, dst = o["send"], T.cores[rank + 1]
             rid, pid = topo.addr(dst)[:2]
             mask = sum(1 << e for e in topo.engines(core, dst)[:NENG])
-            g.remote_dma(T["w%d" % u][:, W0 - 8:W0 + EXT], T["msg%d" % u][:], T.sem["arr%d" % u], T.sem["sent"], pid, rid, mask)
+            land, src = message(u, T, T)
+            g.remote_dma(land, src, T.sem["arr%d" % u], T.sem["sent"], pid, rid, mask)
             sent += NENG
             continue
         sem, inc = o.get("sem", "q" + q), o.get("inc", 1)

@@ -1,3 +1,4 @@
+import numpy as np
 from concourse.mybir import AluOpType, AxisListType, ActivationFunctionType
 
 ALU = AluOpType
@@ -15,15 +16,17 @@ NJ = 96
 MG = 12582912.0
 MQ = 3145728.25
 QB = 1536.0
-EMPTY = -1000
+EMPTY = -1024
 NENG = 8
 
 SCRATCH = {}
 for _u in range(RU):
     SCRATCH["w%d" % _u] = ("sbuf", [128, NSEG * WS + E0], "float32")
     SCRATCH["msg%d" % _u] = ("sbuf", [128, EXT], "float32")
-for _n in ("tab", "yo", "xs", "a", "bit", "gb"):
+for _n in ("tab", "yo", "bit", "gb"):
     SCRATCH[_n] = ("sbuf", [128, P], "bfloat16")
+for _n in ("xs", "a"):
+    SCRATCH[_n] = ("sbuf", [128, NSEG * WS + E0], "bfloat16")
 for _n in ("cp", "tg", "qq", "vv", "ao"):
     SCRATCH[_n] = ("sbuf", [128, P], "float16")
 DIAG = {"ih": 1.0, "iz": -0.5, "im": -1.0, "ie": -1.0 / 4096, "ir": 0.5, "is": 0.5 / 4096, "i513": 513.0, "iq": -256.0,
@@ -33,27 +36,30 @@ for _n in DIAG:
 SCRATCH.update({
     "st": ("sbuf", [128, NSEG * SS], "float16"), "sj": ("sbuf", [128, P // 2], "float16"), "cc": ("sbuf", [128, SG], "float32"),
     "ud": ("sbuf", [128, 256], "float16"), "us": ("sbuf", [128, 256], "float16"), "cu": ("sbuf", [128, 256], "float32"),
-    "gp": ("sbuf", [128, 256], "float32"), "mk": ("sbuf", [128, 256], "float32"),
+    "gp": ("sbuf", [128, 128], "float32"), "mk": ("sbuf", [128, 256], "float32"),
     "wj": ("sbuf", [128, RU * 112], "bfloat16"), "gc1": ("sbuf", [128, 112], "float32"), "g1": ("sbuf", [128, 112], "float32"),
     "gw": ("sbuf", [128, 112], "float32"), "gi": ("sbuf", [128, 48], "float32"), "gs": ("sbuf", [128, 48], "float32"),
-    "gt": ("sbuf", [128, 48], "bfloat16"), "jb": ("sbuf", [128, 4], "float32"),
+    "gt": ("sbuf", [128, 48], "bfloat16"), "jb": ("sbuf", [128, 4], "float32"), "ex": ("sbuf", [128, 8], "float32"),
     "ib": ("sbuf", [128, 128], "bfloat16"), "th": ("sbuf", [128, KC], "bfloat16"), "rn": ("sbuf", [128, 264], "float16"),
-    "vn": ("sbuf", [128, 256], "float16"), "qb": ("sbuf", [128, PW], "bfloat16"),
+    "vn": ("sbuf", [128, 256], "float16"), "qi": ("sbuf", [128, P], "int32"), "zero": ("sbuf", [128, 128], "bfloat16"),
     "poff": ("sbuf", [128, 256], "uint16"), "coff": ("sbuf", [128, 256], "uint16"), "toff": ("sbuf", [128, 16], "uint16"),
     "was": ("sbuf", [128, 4], "bfloat16"), "kcs": ("sbuf", [128, 4], "bfloat16"), "hls": ("sbuf", [128, 8], "float32"),
     "jj": ("sbuf", [128, 144], "float32"), "cm": ("sbuf", [128, 16], "float32"), "cf": ("sbuf", [128, 12], "float32"),
     "pw": ("sbuf", [128, 16], "float32"), "zd": ("sbuf", [128, 144], "float16"), "zc": ("sbuf", [128, 144], "bfloat16"),
+    "zh": ("sbuf", [128, 144], "bfloat16"),
 })
-for _k in range(NB):
-    SCRATCH["p%d" % _k] = ("psum", [128, PW], "float32")
+for _k in range(NB // 2):
+    SCRATCH["p%d" % _k] = ("psum", [128, 2 * PW], "float32")
 
 SEMAPHORES = (["qv", "qa", "qp", "qg", "sent"] + ["arr%d" % u for u in range(RU)]
-              + ["ld%d" % k for k in range(12)] + ["so%d" % k for k in range(8)])
+              + ["ld%d" % k for k in range(16)] + ["so%d" % k for k in range(16)])
 
 CY, PCY, GA, FIX, LAT, WIRE = 0.95, 0.48, 1.56, 60.0, 130.0, 2500.0
-ROUNDS, SLACK = 10, 60.0
+ROUNDS, SLACK, SHAKE, SEED, AHEAD = 150, ((60.0, 0.05), (0.0, 0.1), (30.0, 0.07), (0.0, 0.14)), 1000.0, 1, 8
 
-CFG = {"win": "a", "tg": "a", "qq": "a", "own": "a", "carry": "a", "shift": "v", "half": "a", "out": "v", "mod": "v"}
+CFG = {"win": "a", "tg": "a", "qq": "a", "own": "a", "carry": "a", "shift": "v", "half": "a", "out": "v", "mod": "v", "bit": "v",
+       "early": True, "nwin": PW, "nscan": SG, "nown": PW, "ncopy": SG, "ncode": SG, "ntab": PW, "nmod": PW}
+CFG.update({(_k, _u, _s): PW for _u in range(RU) for _k, _s in (("ncopy", 0), ("ncopy", NSEG - 1), ("nscan", NSEG - 1))})
 CFG.update({("mod", _u, _j): "p" for _u in range(RU) for _j in range(1, 2 * NSEG, 2)})
 
 
@@ -72,6 +78,10 @@ def plan(rank, n_ranks, bank):
     def R(name, a=0, b=None, step=1):
         return (name, a, SCRATCH[name][1][1] if b is None else b, step, 0, 128)
 
+    def X(u, a, b):
+        k = X0 * (a // SG + 1)
+        return R("a" if u else "xs", a + k, b + k)
+
     def part(r, p0, p1):
         return r[:4] + (p0, p1)
 
@@ -81,8 +91,10 @@ def plan(rank, n_ranks, bank):
     def ap(T, r):
         if not isinstance(r, tuple):
             return r
-        t = T["p%d" % bank[(rank, r[0])] if r[0][0] == "@" else r[0]]
-        return t[r[4]:r[5], r[1]:r[2]:r[3]] if r[3] > 1 else t[r[4]:r[5], r[1]:r[2]]
+        if r[0][0] == "@":
+            b = bank[(rank, r[0])]
+            return T["p%d" % (b // 2)][r[4]:r[5], b % 2 * PW + r[1]:b % 2 * PW + r[2]]
+        return T[r[0]][r[4]:r[5], r[1]:r[2]:r[3]] if r[3] > 1 else T[r[0]][r[4]:r[5], r[1]:r[2]]
 
     def kind(r):
         return "float32" if r[0][0] == "@" else SCRATCH[r[0]][2]
@@ -136,15 +148,11 @@ def plan(rank, n_ranks, bank):
     def gather(out, win, off, q, how):
         def fn(g, T):
             src = ap(T, win).indirect(ap(T, off))
+            if isinstance(how, tuple):
+                return g.vector.tensor_tensor(ap(T, out), src, ap(T, how), ALU.max)
             if q == "a":
-                if how == "copy":
-                    return g.scalar.activation(ap(T, out), src, ACT.Copy)
-                return g.scalar.activation(ap(T, out), src, ACT.Identity, bias=0.375)
-            if how == "table":
-                return g.vector.tensor_scalar(ap(T, out), src, 0.375, None, ALU.add)
-            if how == "copy":
-                return g.vector.tensor_copy(ap(T, out), src)
-            return g.vector.tensor_tensor(ap(T, out), src, ap(T, how), ALU.max)
+                return g.scalar.activation(ap(T, out), src, ACT.Identity, bias=how[1], scale=how[0])
+            return g.vector.tensor_scalar(ap(T, out), src, how[0], how[1], ALU.mult, ALU.add)
         return add(q, fn, [win, off] + ([how] if isinstance(how, tuple) else []), [out], FIX + max(64, size(out) * GA) * CY)
 
     def iota(out, pat, base, mult=0):
@@ -158,11 +166,20 @@ def plan(rank, n_ranks, bank):
         return "%s%d" % (k, num[k] - 1)
 
     def tile(n=PW, rows=128):
-        return (fresh("@"), 0, n, 1, 0, rows)
+        return (fresh("@") + ("w" if n > PW else ""), 0, n, 1, 0, rows)
+
+    def bankwise(t, terms, **kw):
+        for a in range(0, size(t), PW):
+            b = min(a + PW, size(t))
+            mm((t[0], a, b) + t[3:], terms(a, b), **kw)
+
+    def pieces(kind, u, s):
+        n = eng(kind, u, s)
+        return [(a, a + n) for a in range(s * SG, (s + 1) * SG, n)]
 
     def load(q, out, src, a, b):
         add(q, lambda g, T: (g.sync if q == "s" else g.scalar).dma_start(ap(T, out), T[src][:, a:b]), [], [out], 100,
-            sem=fresh("ld"), inc=16, dma=(b - a) * 256)
+            sem=fresh("ld"), inc=16, dma=(b - a) * 256 if b - a > 8 else 0)
 
     def wseg(u, s, a, b):
         return R("w%d" % u, s * WS + a, s * WS + b)
@@ -179,7 +196,7 @@ def plan(rank, n_ranks, bank):
     load("a", R("was"), "wa", 0, 4)
     load("a", R("hls"), "hl", 0, 8)
     for s in range(NSEG):
-        load("s", R("xs", s * SG, (s + 1) * SG), "x", s * SG, (s + 1) * SG)
+        load("s", X(0, s * SG, (s + 1) * SG), "x", s * SG, (s + 1) * SG)
     load("s", R("tab", 0, P // 2), "inv", 0, P // 2)
     load("s", R("tab", P // 2, P), "inv", P // 2, P)
 
@@ -187,24 +204,26 @@ def plan(rank, n_ranks, bank):
     iota(cf(7), [[0, 1]], 0, 1)
     iota(R("gc1"), [[0, 7], [1, 16]], int(MG) - 8)
     iota(R("gi"), [[100, 3], [0, 2], [1, 8]], int(MG) - 100)
-    for end, v in ((NJ, -1), (32, 1), (16, 0)):
-        iota(part(cf(4), 0, end), [[0, 1]], v)
-    iota(part(cf(10), NJ, NJ + 2), [[0, 1]], 1, -1)
+    for end, v in ((NJ, -1.0), (32, 1.0), (16, 0.0)):
+        fill(part(cf(4), 0, end), v)
+    for end, v in ((NJ + 2, 0.0), (NJ + 1, 1.0)):
+        fill(part(cf(10), NJ, end), v)
     iota(R("cc", 0, PW), [[-2, PW]], 2047)
-    iota(R("gp"), [[8, 2], [1, 8], [0, 16]], 0)
-    for a in (1, 0, 3, 2, 5, 4):
-        j = a - 2
-        pat, base = ([[0, 128 >> j], [-4096, 2], [0, 1 << j]], 2048) if a > 1 else ([[0, 256]], (-2048, 16384)[a])
-        iota(part(R("cu"), 16 * (a - a % 2), 16 * a + 16), pat, base)
+    act(R("cc", PW, SG), R("cc", 0, PW), ACT.Identity, bias=-2.0 * PW)
+    iota(R("gp"), [[1, 8], [0, 16]], 0)
+    for a in (1, 0):
+        fill(part(R("cu", 0, 128), 0, 16 * a + 16), (-2048.0, 16384.0)[a])
+    for a in (3, 2, 5, 4):
+        iota(part(R("cu", 0, 128), 16 * (a - a % 2), 16 * a + 16), [[0, 256 >> a], [-4096, 2], [0, 1 << (a - 2)]], 2048)
     for h in range(2):
-        iota(part(R("cu", 128 * h, 128 * h + 128), NJ, NJ + 2), [[0, 128]], 1, -6145 - 1024 * h)
+        fill(part(R("cu", 128 * h, 128 * h + 128), NJ, NJ + 2), -6144.0 - 1024 * h)
+    fill(part(R("cu"), NJ, NJ + 1), 1.0)
     iota(R("jj"), [[1, 144]], 0, -1)
     iota(R("cm"), [[1, 16]], 0)
-    iota(R("cc", PW, SG), [[-2, PW]], 2047 - 2 * PW)
     ts(cf(1), cf(0), 1.0 / 32, MG, ALU.mult, ALU.add)
     ts(R("g1"), R("gc1"), cf(1), None, ALU.is_equal)
     for j in range(4):
-        ts(R("gw", 40 + 16 * j, 56 + 16 * j), R("g1", 40 + 16 * j, 56 + 16 * j), 2.0 ** j + 1, -1.0, ALU.mult, ALU.add)
+        affine("a", R("gw", 40 + 16 * j, 56 + 16 * j), R("g1", 40 + 16 * j, 56 + 16 * j), 2.0 ** j + 1, -1.0)
     for u in range(RU):
         ts(R("wj", 112 * u, 112 * u + 40), R("g1", 0, 40), col("was", u), None, ALU.mult)
         ts(R("wj", 112 * u + 40, 112 * u + 104), R("gw", 40, 104), col("kcs", u), None, ALU.is_equal)
@@ -219,30 +238,37 @@ def plan(rank, n_ranks, bank):
     ts(part(R("jb"), 0, 32), t, part(cf(4), 0, 32), 0.5, ALU.subtract, ALU.add)
     ts(cf(2), cf(1), MG, -16.0, ALU.subtract, ALU.mult)
     ts(cf(8), cf(7), cf(2), None, ALU.add)
-    ts(R("mk"), R("gp"), cf(8), None, ALU.is_equal)
-    tt(part(R("ud"), 0, NJ), part(R("cu"), 0, NJ), part(R("mk"), 0, NJ), ALU.mult)
+    for h in range(2):
+        mk = R("mk", 128 * h, 128 * h + 128)
+        ts(mk, R("gp"), cf(8), -8.0 * h, ALU.subtract, ALU.is_equal)
+        tt(part(R("ud", 128 * h, 128 * h + 128), 0, NJ), part(R("cu", 0, 128), 0, NJ), part(mk, 0, NJ), ALU.mult)
     act(part(R("ud"), NJ, NJ + 2), part(R("cu"), NJ, NJ + 2), ACT.Copy)
-    ts(part(R("us"), 0, NJ), part(R("ud"), 0, NJ), part(cf(4), 0, NJ), None, ALU.mult)
-    for s in range(NSEG):
-        act(part(R("sj", s * PW, (s + 1) * PW), NJ, NJ + 2), part(R("cc", 0, PW), NJ, NJ + 2), ACT.Identity, bias=1.0,
-            scale=part(cf(10), NJ, NJ + 2))
-    ts(cf(9), cf(8), -2.0, 2.0 * (WS - E0), ALU.mult, ALU.add)
-    ts(R("st", 0, NSEG * SS, SS), R("cm", 0, NSEG), 0.0, cf(9), ALU.mult, ALU.add)
-    ts(R("ib"), R("jj", 0, 128), 0.0, None, ALU.is_equal)
-    for n, f in sorted(DIAG.items()):
-        act(R(n), R("ib"), ACT.Copy, scale=f)
+    act(part(R("us"), 0, NJ), part(R("ud"), 0, NJ), ACT.Identity, scale=part(cf(4), 0, NJ))
+    rows = [part(R("sj", s * PW, (s + 1) * PW), NJ, NJ + 2) for s in range(NSEG)]
+    act(rows[0], part(R("cc", 0, PW), NJ, NJ + 2), ACT.Identity, bias=1.0, scale=part(cf(10), NJ, NJ + 2))
+    for r in rows[1:]:
+        add("s", lambda g, T, r=r: g.sync.dma_start(ap(T, r), ap(T, rows[0])), [rows[0]], [r], 100, sem=fresh("ld"), inc=16, dma=0)
+    affine("a", cf(9), cf(8), -2.0, 2.0 * (WS - E0))
+    act(R("st", 0, NSEG * SS, SS), R("cm", 0, NSEG), ACT.Identity, bias=cf(9), scale=0.0)
+    iota(R("zero"), [[0, 128]], 0)
+    for n, f in [("ib", 1.0)] + sorted(DIAG.items()):
+        add("g", lambda g, T, n=n, f=f: g.affine_select(ap(T, R(n)), ap(T, R("zero")), [[-1, 128]], ALU.not_equal, f, 0, 1),
+            [R("zero")], [R(n)], 170 + 256 * CY)
     fill(R("th"), -WS / 4096.0)
-    fill(R("qb"), QB)
     ts(R("pw"), R("cm"), cf(8), 1.0, ALU.is_lt, ALU.add)
     add("v", lambda g, T: g.vector.tensor_reduce(ap(T, cf(3)), ap(T, R("pw")), AxisListType.X, ALU.mult), [R("pw")], [cf(3)], FIX + 64)
     ts(cf(5), cf(3), 4000.0, cf(3), ALU.is_lt, ALU.mult)
-    ts(cf(6), cf(8), -1.0, 15.0, ALU.mult, ALU.add)
+    affine("a", cf(6), cf(8), -1.0, 15.0)
     ts(R("zd"), R("jj"), cf(6), -0.5, ALU.is_equal, ALU.mult)
     ts(R("zc"), R("jj"), cf(6), cf(5), ALU.is_equal, ALU.mult)
+    if any(eng("bit", u, s) == "a" for u in range(RU) for s in range(NSEG)):
+        act(R("zh"), R("zc"), ACT.Copy, scale=0.5)
     for u in range(RU):
         for s in range(NSEG + 1):
             for a, b in ((0, E0), (E0 + EXT, X0)) if s == 0 and takes else ((0, X0 if s < NSEG else E0),):
                 iota(wseg(u, s, a, b), [[0, b - a]], EMPTY)
+            if sends and u < 2:
+                iota(R("a" if u else "xs", s * WS, s * WS + (X0 if s < NSEG else E0)), [[0, X0 if s < NSEG else E0]], 512 * EMPTY)
 
     def offsets(e, t, r0, out):
         v, r, t2 = R("vn", r0, r0 + size(t)), R("rn", r0, r0 + size(t)), tile(size(t))
@@ -252,17 +278,18 @@ def plan(rank, n_ranks, bank):
         ts(out, t2, -4096.0, float(WS), ALU.mult, ALU.min)
 
     def judge(u, s):
-        c, k0, x = s * SG, s * SS, "a" if u else "xs"
+        c, k0 = s * SG, s * SS
         t, sj = tile(PW, NJ), R("sj", s * PW, (s + 1) * PW)
-        mm(t, [(R("wj", 112 * u + 8 - 8 * h, 112 * u + 104 - 8 * h), R(x, c + h * PW, c + (h + 1) * PW)) for h in range(2)])
+        mm(t, [(R("wj", 112 * u + 8 - 8 * h, 112 * u + 104 - 8 * h), X(u, c + h * PW, c + (h + 1) * PW)) for h in range(2)])
         act(part(sj, 0, NJ), t, ACT.Sign, bias=part(col("jb", u), 0, NJ))
-        for h in range(2):
-            t, k = tile(), k0 + h * PW
-            mm(t, [(part(R("ud", 128 * h, 128 * h + 128), 0, NJ + 2), part(sj, 0, NJ + 2))])
-            o, d1, init = R("st", k + 1, k + 1 + PW), R("cc", h * PW, (h + 1) * PW), col("st", k)
+        for a, b in pieces("nscan", u, s):
+            t, k = tile(b - a), k0 + a - c
+            bankwise(t, lambda i, j: [(part(R("ud", (a - c + i) // 4, (a - c + i) // 4 + 128), 0, NJ + 2), part(sj, 0, NJ + 2))])
+            o, d1, init = R("st", k + 1, k + 1 + b - a), R("cc", a - c, b - c), col("st", k)
             add("v", lambda g, T, o=o, t=t, d1=d1, init=init: g.vector.tensor_tensor_scan(
                 ap(T, o), ap(T, t), ap(T, d1), ap(T, init), ALU.min, ALU.max), [t, d1, init], [o], vcost([o, t]))
-        affine(eng("win", u, s), wseg(u, s, X0, WS), R(x, c, c + SG), 1.0 / 512, -0.5 if u else -0.625)
+        for a, b in pieces("nwin", u, s):
+            affine(eng("win", u, a // PW), wseg(u, s, X0 + a - c, X0 + b - c), X(u, a, b), 1.0 / 512, -0.5 if u else -0.625)
 
     def ends(s0, s1):
         z, r, t = R("st", s0 * SS + SG, (s1 - 1) * SS + SG + 1, SS), R("rn", 256 + s0, 256 + s1), tile(s1 - s0)
@@ -270,71 +297,71 @@ def plan(rank, n_ranks, bank):
         mm(t, [(R("ib"), R("th", 0, s1 - s0)), (R("iz"), z), (R("ir"), r), (R("is"), r)])
         ts(R("toff", 2 * s0, 2 * s1 - 1, 2), t, -4096.0, float(WS), ALU.mult, ALU.min)
 
-    def carry(u, s, off, first=0):
-        out = wseg(u, s + 1, E0, E0 + EXT) if s + 1 < NSEG else R("msg%d" % u)
-        gather(out, wseg(u, s, first, WS + 1), col("toff", off), eng("carry", u, s), "copy")
-
     def hand_on(u):
         ends(0, NSEG - 1)
         if sends:
-            if takes:
-                ts(col("toff", 8), col("toff", 0), float(E0 + EXT), None, ALU.subtract)
-                carry(u, 0, 8, E0 + EXT)
-            for s in range(1 if takes else 0, NSEG - 1):
-                carry(u, s, 2 * s)
             ends(NSEG - 1, NSEG)
-            carry(u, NSEG - 1, 2 * NSEG - 2)
+            x = "a" if u else "xs"
+            for s in range(NSEG):
+                k, last = s * WS, s + 1 == NSEG
+                gather(R("msg%d" % u) if last else R(x, k + WS + E0, k + WS + E0 + EXT), R(x, k, k + WS + 1), col("toff", 2 * s),
+                       eng("carry", u, s), [1.0 / 512, -0.5 if u else -0.625] if last else [1.0, 0.0])
             add("g", None, [R("msg%d" % u)], [], 300, send=u)
         if takes:
             add("x", None, [], [wseg(u, 0, E0, E0 + EXT)], 0, arrive=u)
-            for s in range(NSEG - 1):
-                carry(u, s, 2 * s)
+        for s in range(NSEG - 1):
+            gather(wseg(u, s + 1, E0, E0 + EXT), wseg(u, s, 0, WS + 1), col("toff", 2 * s), eng("carry", u, s), [1.0, 0.0])
 
     def point(u, s):
         c, k0 = s * SG, s * SS
-        for h in range(2):
-            t, o = tile(), R("vv", c + h * PW, c + (h + 1) * PW)
-            mm(t, [(part(R("us", 128 * h, 128 * h + 128), 0, NJ), part(R("sj", s * PW, (s + 1) * PW), 0, NJ)),
-                   (R("ih"), R("st", k0 + h * PW, k0 + (h + 1) * PW))])
-            if eng("own", u, 2 * s + h) == "a":
+        for a, b in pieces("nown", u, s):
+            t, o = tile(b - a), R("vv", a, b)
+            bankwise(t, lambda i, j: [(part(R("us", (a - c + i) // 4, (a - c + i) // 4 + 128), 0, NJ), part(R("sj", s * PW, (s + 1) * PW), 0, NJ)),
+                                      (R("ih"), R("st", k0 + a - c + i, k0 + a - c + j))])
+            if eng("own", u, a // PW) == "a":
                 act(o, t, ACT.Relu, bias=-24576.0)
             else:
                 ts(o, t, -24576.0, 0.0, ALU.add, ALU.max)
         t = tile(KC)
         mm(t, wrap("zd", R("vv", c, c + SG)))
         offsets(eng("half", u, s), t, s * KC, R("poff", s * KC, (s + 1) * KC))
-        ts(R("bit", c, c + SG), R("a" if u else "xs", c, c + SG), 63.5 if u else 127.5, None, ALU.is_ge)
+        if eng("bit", u, s) == "a":
+            act(R("bit", c, c + SG), X(u, c, c + SG), ACT.Sign, bias=-63.5 if u else -127.5)
+        else:
+            ts(R("bit", c, c + SG), X(u, c, c + SG), 63.5 if u else 127.5, None, ALU.is_ge)
         if u == 0:
-            affine(eng("shift", u, s), R("a", c, c + SG), R("xs", c, c + SG), 1.0, -64.0)
+            affine(eng("shift", u, s), X(1, c, c + SG), X(0, c, c + SG), 1.0, -64.0)
 
     def apply(u, s):
-        a, b = s * SG, (s + 1) * SG
-        gather(R("cp", a, b), wseg(u, s, 0, WS + 1), R("poff", a // 16, b // 16), "v", R("a", a, b))
-        ts(R("gb", a, b), R("cp", a, b), MQ, MQ - 0.25, ALU.add, ALU.is_equal)
-        t = tile(KC)
-        mm(t, wrap("zc", R("bit", a, b)), last=False)
-        mm(t, wrap("zc", R("gb", a, b)), first=False)
-        cp(R("coff", a // 16, b // 16), t)
-        for a in range(s * SG, (s + 1) * SG, PW):
-            b, j = a + PW, a // PW
-            gather(R("tg", a, b), R("tab"), R("coff", a // 16, b // 16), eng("tg", u, j), "table")
-            t, out, less = tile(), R("a" if u + 1 < RU else "yo", a, b), 64.0 if u + 1 < RU else 0.0
+        for a, b in pieces("ncopy", u, s):
+            gather(R("cp", a, b), wseg(u, s, 0, WS + 1), R("poff", a // 16, b // 16), "v", X(1, a, b))
+            ts(R("gb", a, b), R("cp", a, b), MQ, MQ - 0.25, ALU.add, ALU.is_equal)
+        for a, b in pieces("ncode", u, s):
+            t, sign = tile((b - a) // 16), eng("bit", u, s) == "a"
+            mm(t, wrap("zh" if sign else "zc", R("bit", a, b)), last=False)
+            mm(t, wrap("zc", R("gb", a, b)), first=False)
+            ts(R("coff", a // 16, b // 16), t, 2047.5 if sign else 0.0, None, ALU.add)
+        for a, b in pieces("ntab", u, s):
+            gather(R("tg", a, b), R("tab"), R("coff", a // 16, b // 16), eng("tg", u, a // PW), [1.0, 0.375])
+        for a, b in pieces("nmod", u, s):
+            j = a // PW
+            t, out, less = tile(b - a), X(1, a, b) if u + 1 < RU else R("yo", a, b), 64.0 if u + 1 < RU else 0.0
             if eng("mod", u, j) == "p":
-                terms, t2 = [(R("i513"), R("cp", a, b)), (R("ih"), R("tg", a, b))], tile()
-                mm(t, terms)
+                t2, early = tile(b - a), eng("early", u, s)
+                for k in (t, t2) if early else (t,):
+                    bankwise(k, lambda i, j: [(R("i513"), R("cp", a + i, a + j)), (R("ih"), R("tg", a + i, a + j))], last=k is t)
                 affine(eng("qq", u, j), R("qq", a, b), t, 1.0 / 256, QB - 63.5 / 256)
-                mm(t2, terms, last=False)
-                mm(t2, [(R("iq"), R("qq", a, b))], first=False)
+                bankwise(t2, lambda i, j: ([] if early else [(R("i513"), R("cp", a + i, a + j)), (R("ih"), R("tg", a + i, a + j))])
+                         + [(R("iq"), R("qq", a + i, a + j))], first=not early)
                 ts(out, t2, MG + 256 * QB, MG - 64 + less, ALU.add, ALU.subtract)
             else:
-                mm(t, [(R("ib"), R("qb")), (R("j513"), R("cp", a, b)), (R("j1"), R("tg", a, b))])
-                affine(eng("qq", u, j), R("qq", a, b), t, 1.0, -5 - 63.5 / 256)
-                tt(R("ao", a, b), t, R("qq", a, b), ALU.subtract)
+                bankwise(t, lambda i, j: [(R("j513"), R("cp", a + i, a + j)), (R("j1"), R("tg", a + i, a + j))])
+                affine(eng("qq", u, j), R("qi", a, b), t, 1.0, -5 - 63.5 / 256)
+                tt(R("ao", a, b), t, R("qi", a, b), ALU.subtract)
                 affine(eng("out", u, j), out, R("ao", a, b), 256.0, 64.0 - 1280 - less)
-            if u + 1 < RU:
-                continue
-            add("s", lambda g, T, a=a, b=b: g.sync.dma_start(T["y"][:, a:b], T["yo"][:, a:b]), [R("yo", a, b)], [], 100,
-                sem=fresh("so"), inc=16, dma=PW * 256)
+            if u + 1 == RU:
+                add("s", lambda g, T, a=a, b=b: g.sync.dma_start(T["y"][:, a:b], T["yo"][:, a:b]), [R("yo", a, b)], [], 100,
+                    sem=fresh("so"), inc=16, dma=(b - a) * 256)
 
     for s in range(NSEG):
         judge(0, s)
@@ -350,7 +377,7 @@ def plan(rank, n_ranks, bank):
 
 
 def link(ops):
-    seen = {}
+    seen, opener = {}, {}
     for i, o in enumerate(ops):
         dep = set()
         acc = [(r, False) for r in o["rd"]] + [(r, True) for r in o["wr"]]
@@ -362,6 +389,10 @@ def link(ops):
             if r[0][0] == "@":
                 o["tile"], o["opens"] = r[0], o.get("opens") or r[0] not in seen
                 seen[r[0]] = [(i, r, True)]
+                if o["opens"]:
+                    opener[r[0]] = o
+                elif o["q"] != "p" and r[0] in opener:
+                    opener.pop(r[0])["reader"], o["reads"] = o["q"], True
             else:
                 keep = [x for x in seen.get(r[0], []) if not (w and covers(r, x[1]))]
                 seen[r[0]] = keep + [(i, r, w)]
@@ -384,48 +415,77 @@ def covers(a, b):
     return a[3] == 1 and a[1] <= b[1] and b[2] <= a[2] and a[4] <= b[4] and b[5] <= a[5]
 
 
-def sweep(ops, pre, key, back):
+def sweep(ops, edges, key, back, slack):
     n = len(ops)
-    succ = [[] for _ in ops]
-    for i in range(n):
-        for j, d in pre[i]:
-            succ[j].append((i, d))
-    left, due, ready = [len(p) for p in pre], [0.0] * n, {}
+    pre, succ = edges
+    opens, closes = ("closes", "opens") if back else ("opens", "closes")
+    eng = [o["e"] for o in ops]
+    need = [(1 + (o["tile"][-1] == "w")) if o.get(opens) else 0 for o in ops]
+    left, due, ready = [len(p) for p in pre], [0.0] * n, {e: [] for e in sorted(set(eng))}
     for i in range(n):
         if not left[i]:
-            ready.setdefault(ops[i]["e"], []).append(i)
-    free, at, end, seq, after, bank, banks, wire = {}, [0.0] * n, [0.0] * n, [], {}, {}, {}, {}
-    opens, closes = ("closes", "opens") if back else ("opens", "closes")
+            ready[eng[i]].append(i)
+    free, at, end, seq, after, bank, wire = {e: 0.0 for e in ready}, [0.0] * n, [0.0] * n, [], {}, {}, {}
+    banks = {e[0]: {k: (0.0, None) for k in range(NB)} for e in ready}
+    mates = {r: [e for e in ready if e[0] == r] for r in banks}
+    never = float("inf")
+    turns = {e: [0.0] * (n if back else AHEAD) for e in ready}
+    reader = [o.get("reader") for o in ops]
+
+    def starts(e):
+        bk, f = banks[e[0]], free[e]
+        bt = (f, max(f, min([v[0] for v in bk.values()], default=never)),
+              max(f, min([max(bk[k][0], bk[k + 1][0]) for k in range(0, NB, 2) if k in bk and k + 1 in bk], default=never)))
+        if back or e[1] != "p":
+            return [(max(due[i], bt[need[i]]), i) for i in ready[e]]
+        turn = {q: min(turns[(e[0], q)], default=never) for q in "va"}
+        return [(max(due[i], bt[need[i]], turn.get(reader[i], 0.0)), i) for i in ready[e]]
+
+    cand = {e: starts(e) for e in ready}
+    first = {e: min(cand[e], default=(never,))[0] for e in ready}
     for _ in range(n):
-        best = None
-        for e, line in ready.items():
-            bk = banks.setdefault(e[0], {k: (0.0, None) for k in range(NB)})
-            bt = min([v[0] for v in bk.values()]) if bk else None
-            f = free.get(e, 0.0)
-            st = [(max(due[i], f, bt if ops[i].get(opens) else 0.0), i) for i in line if bt is not None or not ops[i].get(opens)]
-            if st and (best is None or min(st)[0] < best[0]):
-                best = (min(st)[0], e, st)
-        t0, e, st = best
-        t, i = min([x for x in st if x[0] <= t0 + SLACK], key=lambda x: (key[x[1]], x[1]))
+        e = min(first, key=first.get)
+        if first[e] == never:
+            return None
+        lim = first[e] + slack[0]
+        t, i = min(cand[e], key=lambda x: max(x[0], lim) + slack[1] * key[x[1]])
         o = ops[i]
         ready[e].remove(i)
         at[i] = t
         end[i] = free[e] = t + o["cost"]
-        bk = banks[e[0]]
-        if o.get(opens):
-            b = min(bk, key=lambda k: bk[k][0])
+        bk, touched = banks[e[0]], {e}
+        if not back and reader[i]:
+            turns[(e[0], reader[i])].remove(min(turns[(e[0], reader[i])]))
+        if not back and o.get("reads"):
+            turns[e].append(t)
+            touched.add((e[0], "p"))
+        if need[i]:
+            if need[i] == 2:
+                b = min([k for k in range(0, NB, 2) if k in bk and k + 1 in bk], key=lambda k: max(bk[k][0], bk[k + 1][0]))
+            else:
+                b = min(bk, key=lambda k: (max(bk[k][0], t), k ^ 1 in bk, bk[k][0]))
             bank[(e[0], o["tile"])] = b
-            after[i] = bk.pop(b)[1]
+            after[i] = [bk.pop(k)[1] for k in range(b, b + need[i])]
+            touched.update(mates[e[0]])
         if o.get(closes):
-            bk[bank[(e[0], o["tile"])]] = (end[i] + LAT, i)
+            for k in range(1 + (o["tile"][-1] == "w")):
+                bk[bank[(e[0], o["tile"])] + k] = (end[i] + LAT, i)
+            touched.update(mates[e[0]])
         if "dma" in o and not back:
-            wire[e[0]] = end[i] = max(wire.get(e[0], 0.0), end[i] + 1500) + o["dma"] / 250.0
+            end[i] = max(wire.get(e[0], 0.0) if o["dma"] else 0.0, end[i] + 1500) + o["dma"] / 250.0
+            if o["dma"]:
+                wire[e[0]] = end[i]
         seq.append(i)
         for k, d in succ[i]:
-            due[k] = max(due[k], end[i] + d)
+            if end[i] + d > due[k]:
+                due[k] = end[i] + d
             left[k] -= 1
             if not left[k]:
-                ready.setdefault(ops[k]["e"], []).append(k)
+                ready[eng[k]].append(k)
+                touched.add(eng[k])
+        for e in touched:
+            cand[e] = starts(e)
+            first[e] = min(cand[e])[0] if cand[e] else never
     return seq, at, end, after, bank
 
 
@@ -450,20 +510,29 @@ def schedule(n_ranks):
                 p.append((sent[(r - 1, o["arrive"])], WIRE))
             pre.append(p)
         ops += mine
-    rev = [[] for _ in ops]
+    succ, rev, rsucc = [[] for _ in ops], [[] for _ in ops], [[] for _ in ops]
     for i, p in enumerate(pre):
         for j, d in p:
-            rev[j].append((i, d + (1500 + ops[j]["dma"] / 250.0 if "dma" in ops[j] else 0)))
+            succ[j].append((i, d))
+            d += 1500 + ops[j]["dma"] / 250.0 if "dma" in ops[j] else 0
+            rev[j].append((i, d))
+            rsucc[i].append((j, d))
+    rng = np.random.default_rng(SEED)
     key, best = list(range(len(ops))), None
-    for _ in range(ROUNDS):
-        out = sweep(ops, pre, key, False)
-        if best is None or max(out[2]) < max(best[2]):
+    for k in range(ROUNDS):
+        out = sweep(ops, (pre, succ), key, False, SLACK[k % len(SLACK)])
+        if out and (best is None or max(out[2]) < max(best[2])):
             best = out
-        key = [-x for x in sweep(ops, rev, [-x for x in out[2]], True)[2]]
+        if k % 3 == 2 or not out:
+            out = best
+            key = (rng.normal(0.0, SHAKE, len(ops)) - np.array(out[2])).tolist()
+        else:
+            key = [-x for x in out[2]]
+        back = sweep(ops, (rev, rsucc), key, True, SLACK[k % len(SLACK)])
+        key = [-x for x in back[2]] if back else best[1]
     bank.update(best[4])
-    for i, j in best[3].items():
-        if j is not None:
-            ops[i]["dep"].append(j)
+    for i, js in best[3].items():
+        ops[i]["dep"] += [j for j in js if j is not None]
     CACHE[n_ranks] = (ops,) + best[:3]
     return CACHE[n_ranks]
 

@@ -14,10 +14,9 @@ PW = 512
 NB = 8
 NJ = 96
 MG = 12582912.0
-MQ = 3145728.25
-QB = 1536.0
+MQ = 6291456.5
 EMPTY = -1024
-NENG = 8
+NENG = 16
 
 SCRATCH = {}
 for _u in range(RU):
@@ -27,21 +26,20 @@ for _n in ("tab", "yo", "bit", "gb"):
     SCRATCH[_n] = ("sbuf", [128, P], "bfloat16")
 for _n in ("xs", "a"):
     SCRATCH[_n] = ("sbuf", [128, NSEG * WS + E0], "bfloat16")
-for _n in ("cp", "tg", "qq", "vv", "ao"):
+for _n in ("cp", "tg", "vv", "ao", "qq"):
     SCRATCH[_n] = ("sbuf", [128, P], "float16")
-DIAG = {"ih": 1.0, "iz": -0.5, "im": -1.0, "ie": -1.0 / 4096, "ir": 0.5, "is": 0.5 / 4096, "i513": 513.0, "iq": -256.0,
-        "j513": 513.0 / 256, "j1": 1.0 / 256}
+DIAG = {"ih": 1.0, "il": 513.0 / 512}
 for _n in DIAG:
     SCRATCH[_n] = ("sbuf", [128, 128], "float16")
 SCRATCH.update({
     "st": ("sbuf", [128, NSEG * SS], "float16"), "sj": ("sbuf", [128, P // 2], "float16"), "cc": ("sbuf", [128, SG], "float32"),
-    "ud": ("sbuf", [128, 256], "float16"), "us": ("sbuf", [128, 256], "float16"), "cu": ("sbuf", [128, 256], "float32"),
+    "ud": ("sbuf", [128, 256], "float16"), "us": ("sbuf", [128, 256], "float16"), "um": ("sbuf", [128, 256], "float16"), "cu": ("sbuf", [128, 256], "float32"),
     "gp": ("sbuf", [128, 128], "float32"), "mk": ("sbuf", [128, 256], "float32"),
-    "wj": ("sbuf", [128, RU * 112], "bfloat16"), "gc1": ("sbuf", [128, 112], "float32"), "g1": ("sbuf", [128, 112], "float32"),
+    "wj": ("sbuf", [128, 112], "bfloat16"), "wk": ("sbuf", [128, RU * 112], "float16"), "gc1": ("sbuf", [128, 112], "float32"), "g1": ("sbuf", [128, 112], "float32"),
     "gw": ("sbuf", [128, 112], "float32"), "gi": ("sbuf", [128, 48], "float32"), "gs": ("sbuf", [128, 48], "float32"),
-    "gt": ("sbuf", [128, 48], "bfloat16"), "jb": ("sbuf", [128, 4], "float32"), "ex": ("sbuf", [128, 8], "float32"),
-    "ib": ("sbuf", [128, 128], "bfloat16"), "th": ("sbuf", [128, KC], "bfloat16"), "rn": ("sbuf", [128, 264], "float16"),
-    "vn": ("sbuf", [128, 256], "float16"), "qi": ("sbuf", [128, P], "int32"), "zero": ("sbuf", [128, 128], "bfloat16"),
+    "gt": ("sbuf", [128, 48], "bfloat16"), "jb": ("sbuf", [128, 4], "float32"), "waf": ("sbuf", [128, 4], "float32"),
+    "ni": ("sbuf", [128, 264], "int32"), "mi": ("sbuf", [128, 264], "int32"),
+    "qi": ("sbuf", [128, P], "int32"), "zero": ("sbuf", [128, 128], "bfloat16"),
     "poff": ("sbuf", [128, 256], "uint16"), "coff": ("sbuf", [128, 256], "uint16"), "toff": ("sbuf", [128, 16], "uint16"),
     "was": ("sbuf", [128, 4], "bfloat16"), "kcs": ("sbuf", [128, 4], "bfloat16"), "hls": ("sbuf", [128, 8], "float32"),
     "jj": ("sbuf", [128, 144], "float32"), "cm": ("sbuf", [128, 16], "float32"), "cf": ("sbuf", [128, 12], "float32"),
@@ -52,25 +50,29 @@ for _k in range(NB // 2):
     SCRATCH["p%d" % _k] = ("psum", [128, 2 * PW], "float32")
 
 SEMAPHORES = (["qv", "qa", "qp", "qg", "sent"] + ["arr%d" % u for u in range(RU)]
-              + ["ld%d" % k for k in range(16)] + ["so%d" % k for k in range(16)])
+              + ["ld%d" % k for k in range(32)] + ["so%d" % k for k in range(16)] + ["ac%d" % k for k in range(16)])
+HOT = (0.0, 0.0, 0.0)
+QB = 1536.0
 
-CY, PCY, GA, FIX, LAT, WIRE = 0.95, 0.48, 1.56, 60.0, 130.0, 2500.0
-ROUNDS, SLACK, SHAKE, SEED, AHEAD = 150, ((60.0, 0.05), (0.0, 0.1), (30.0, 0.07), (0.0, 0.14)), 1000.0, 1, 8
+CY, PCY, GA, FIX, FIXA, FIXG, LAT, WIRE = 0.95, 0.58, 1.56, 60.0, 75.0, 66.0, 120.0, 2200.0
+ROUNDS, SLACK, URGE, SHAKE, SEED, AHEAD = 400, 100.0, (0.03, 0.15), 300.0, 1, 8
 
-CFG = {"win": "a", "tg": "a", "qq": "a", "own": "a", "carry": "a", "shift": "v", "half": "a", "out": "v", "mod": "v", "bit": "v",
-       "early": True, "nwin": PW, "nscan": SG, "nown": PW, "ncopy": SG, "ncode": SG, "ntab": PW, "nmod": PW}
-CFG.update({(_k, _u, _s): PW for _u in range(RU) for _k, _s in (("ncopy", 0), ("ncopy", NSEG - 1), ("nscan", NSEG - 1))})
-CFG.update({("mod", _u, _j): "p" for _u in range(RU) for _j in range(1, 2 * NSEG, 2)})
+CFG = {"win": "a", "tg": "a", "qq": "a", "own": "a", "carry": "a", "shift": "g", ("shift", 0): "v", "fin": "a", "least": False, "after": False, "cc0": 128, "cca": 256, "cu0": 32, ("nmod", RU - 1, NSEG - 1): PW // 2, ("ntab", RU - 1, NSEG - 1): PW // 2, "poff": "v", "ends": ("vv", "vv"), "half": "a", "out": "v", "mod": "v", "bit": "v",
+       "early": True, "split": False, "once": False, "join": (1, 1, 1, 1), "fill": "a", "fills": ("cu",), "wsum": "a", "coff": "a",
+       "nout": SG, "nwin": SG, "nscan": SG, "nown": SG, "ncopy": SG, "ncode": SG, "ntab": PW, "nmod": PW}
+CFG.update({(_k, _u, _s): PW for _u in range(RU) for _k, _s in (("ncopy", 0), ("nown", 0), ("nscan", NSEG - 1))})
+CFG.update({"nwin": PW, "nown": PW, "win": "g", ("win", 0): "a", "shift": "v"})
+CFG.update({("shift", _u, _j): "a" for _u in range(1, RU) for _j in (0, 2)})
 
 
 def plan(rank, n_ranks, bank):
-    ops = []
+    ops, hot = [], [0.0]
 
     def eng(kind, u, j):
         return CFG.get((kind, rank, u, j), CFG.get((kind, u, j), CFG.get((kind, u), CFG[kind])))
 
     def add(q, fn, rd, wr, cost, **kw):
-        d = {"q": q, "fn": fn, "rd": rd, "wr": wr, "cost": cost}
+        d = {"q": q, "fn": fn, "rd": rd, "wr": wr, "cost": cost, "hot": hot[0]}
         d.update(kw)
         ops.append(d)
         return d
@@ -81,6 +83,12 @@ def plan(rank, n_ranks, bank):
     def X(u, a, b):
         k = X0 * (a // SG + 1)
         return R("a" if u else "xs", a + k, b + k)
+
+    def Z(u, a, b):
+        return R("ao", a, b) if u else X(0, a, b)
+
+    def wj(u, a, b):
+        return R("wk", 112 * u + a, 112 * u + b) if u else R("wj", a, b)
 
     def part(r, p0, p1):
         return r[:4] + (p0, p1)
@@ -121,12 +129,14 @@ def plan(rank, n_ranks, bank):
         return add("v", lambda g, T: g.vector.tensor_copy(ap(T, out), ap(T, in0)), [in0], [out], vcost([out, in0]))
 
     def fill(out, c):
+        if CFG["fill"] == "a" and out[0] in CFG["fills"]:
+            return act(out, part(R("gp", 0, size(out)), out[4], out[5]), ACT.Identity, bias=c, scale=0.0)
         return add("v", lambda g, T: g.vector.memset(ap(T, out), c), [], [out], vcost([out]))
 
     def act(out, in0, func, bias=0.0, scale=1.0):
         rd = [in0] + [s for s in (bias, scale) if isinstance(s, tuple)]
         return add("a", lambda g, T: g.scalar.activation(ap(T, out), ap(T, in0), func, bias=ap(T, bias), scale=ap(T, scale)),
-                   rd, [out], FIX + max(64, size(out)) * CY)
+                   rd, [out], FIXA + max(64, size(out)) * CY)
 
     def affine(e, out, in0, scale, bias):
         if e == "a":
@@ -153,13 +163,13 @@ def plan(rank, n_ranks, bank):
             if q == "a":
                 return g.scalar.activation(ap(T, out), src, ACT.Identity, bias=how[1], scale=how[0])
             return g.vector.tensor_scalar(ap(T, out), src, how[0], how[1], ALU.mult, ALU.add)
-        return add(q, fn, [win, off] + ([how] if isinstance(how, tuple) else []), [out], FIX + max(64, size(out) * GA) * CY)
+        return add(q, fn, [win, off] + ([how] if isinstance(how, tuple) else []), [out], FIXG + max(64, size(out) * GA) * CY)
 
     def iota(out, pat, base, mult=0):
         return add("g", lambda g, T: g.iota(ap(T, out), pat, base, mult, allow_small_or_imprecise_dtypes=True), [], [out],
                    130 + 2 * size(out) * CY)
 
-    num = {"ld": 0, "so": 0, "@": 0}
+    num = {"ld": 0, "so": 0, "ac": 0, "@": 0}
 
     def fresh(k):
         num[k] += 1
@@ -200,6 +210,7 @@ def plan(rank, n_ranks, bank):
     load("s", R("tab", 0, P // 2), "inv", 0, P // 2)
     load("s", R("tab", P // 2, P), "inv", P // 2, P)
 
+    iota(R("gp"), [[1, 8], [0, 16]], 0)
     iota(cf(0), [[0, 1]], -15, 2)
     iota(cf(7), [[0, 1]], 0, 1)
     iota(R("gc1"), [[0, 7], [1, 16]], int(MG) - 8)
@@ -208,16 +219,22 @@ def plan(rank, n_ranks, bank):
         fill(part(cf(4), 0, end), v)
     for end, v in ((NJ + 2, 0.0), (NJ + 1, 1.0)):
         fill(part(cf(10), NJ, end), v)
-    iota(R("cc", 0, PW), [[-2, PW]], 2047)
-    act(R("cc", PW, SG), R("cc", 0, PW), ACT.Identity, bias=-2.0 * PW)
-    iota(R("gp"), [[1, 8], [0, 16]], 0)
+    n = CFG["cc0"]
+    iota(R("cc", 0, n), [[-2, n]], 2047)
+    while n < SG:
+        affine("a" if n >= CFG["cca"] else "v", R("cc", n, 2 * n), R("cc", 0, n), 1.0, -2.0 * n)
+        n *= 2
+    n = CFG["cu0"]
     for a in (1, 0):
-        fill(part(R("cu", 0, 128), 0, 16 * a + 16), (-2048.0, 16384.0)[a])
+        fill(part(R("cu", 0, n), 0, 16 * a + 16), (-2048.0, 16384.0)[a])
     for a in (3, 2, 5, 4):
-        iota(part(R("cu", 0, 128), 16 * (a - a % 2), 16 * a + 16), [[0, 256 >> a], [-4096, 2], [0, 1 << (a - 2)]], 2048)
+        iota(part(R("cu", 0, n), 16 * (a - a % 2), 16 * a + 16), [[0, 2 * n >> a], [-4096, 2], [0, 1 << (a - 2)]], 2048)
+    while n < 128:
+        cp(part(R("cu", n, 2 * n), 0, NJ), part(R("cu", 0, n), 0, NJ))
+        n *= 2
     for h in range(2):
         fill(part(R("cu", 128 * h, 128 * h + 128), NJ, NJ + 2), -6144.0 - 1024 * h)
-    fill(part(R("cu"), NJ, NJ + 1), 1.0)
+        fill(part(R("cu", 128 * h, 128 * h + 128), NJ, NJ + 1), 1.0)
     iota(R("jj"), [[1, 144]], 0, -1)
     iota(R("cm"), [[1, 16]], 0)
     ts(cf(1), cf(0), 1.0 / 32, MG, ALU.mult, ALU.add)
@@ -225,11 +242,11 @@ def plan(rank, n_ranks, bank):
     for j in range(4):
         affine("a", R("gw", 40 + 16 * j, 56 + 16 * j), R("g1", 40 + 16 * j, 56 + 16 * j), 2.0 ** j + 1, -1.0)
     for u in range(RU):
-        ts(R("wj", 112 * u, 112 * u + 40), R("g1", 0, 40), col("was", u), None, ALU.mult)
-        ts(R("wj", 112 * u + 40, 112 * u + 104), R("gw", 40, 104), col("kcs", u), None, ALU.is_equal)
+        ts(wj(u, 0, 40), R("g1", 0, 40), col("was", u), 256.0 if u else 1.0, ALU.mult, ALU.mult)
+        ts(wj(u, 40, 104), R("gw", 40, 104), col("kcs", u), 256.0 if u else 1.0, ALU.is_equal, ALU.mult)
     ts(R("gs"), R("gi"), cf(1), -1.0 / 16, ALU.is_equal, ALU.mult)
-    ts(R("gt"), R("gi"), cf(1), 64.0, ALU.is_equal, ALU.mult)
-    fill(R("jb"), -63.5)
+    ts(R("gt"), R("gi"), cf(1), -1216.0, ALU.is_equal, ALU.mult)
+    fill(R("jb"), -1343.5)
     fill(col("jb", 0), -127.5)
     t = tile(RU, 32)
     later = (t[0], 1, RU, 1, 0, 32)
@@ -244,6 +261,12 @@ def plan(rank, n_ranks, bank):
         tt(part(R("ud", 128 * h, 128 * h + 128), 0, NJ), part(R("cu", 0, 128), 0, NJ), part(mk, 0, NJ), ALU.mult)
     act(part(R("ud"), NJ, NJ + 2), part(R("cu"), NJ, NJ + 2), ACT.Copy)
     act(part(R("us"), 0, NJ), part(R("ud"), 0, NJ), ACT.Identity, scale=part(cf(4), 0, NJ))
+    if any(eng("least", u, s) for u in range(RU) for s in range(NSEG)):
+        for end, v in ((NJ, -2.0), (32, 2176.0 / 16384), (16, 0.0)):
+            fill(part(cf(11), 0, end), v)
+        act(part(R("um"), 0, NJ), part(R("ud"), 0, NJ), ACT.Identity, scale=part(cf(11), 0, NJ))
+        for end, v in ((NJ + 2, -14464.0), (NJ + 1, 0.0)):
+            act(part(R("um"), NJ, end), part(R("cu"), NJ, end), ACT.Identity, bias=v, scale=0.0)
     rows = [part(R("sj", s * PW, (s + 1) * PW), NJ, NJ + 2) for s in range(NSEG)]
     act(rows[0], part(R("cc", 0, PW), NJ, NJ + 2), ACT.Identity, bias=1.0, scale=part(cf(10), NJ, NJ + 2))
     for r in rows[1:]:
@@ -251,15 +274,14 @@ def plan(rank, n_ranks, bank):
     affine("a", cf(9), cf(8), -2.0, 2.0 * (WS - E0))
     act(R("st", 0, NSEG * SS, SS), R("cm", 0, NSEG), ACT.Identity, bias=cf(9), scale=0.0)
     iota(R("zero"), [[0, 128]], 0)
-    for n, f in [("ib", 1.0)] + sorted(DIAG.items()):
+    for n, f in sorted(DIAG.items()):
         add("g", lambda g, T, n=n, f=f: g.affine_select(ap(T, R(n)), ap(T, R("zero")), [[-1, 128]], ALU.not_equal, f, 0, 1),
             [R("zero")], [R(n)], 170 + 256 * CY)
-    fill(R("th"), -WS / 4096.0)
     ts(R("pw"), R("cm"), cf(8), 1.0, ALU.is_lt, ALU.add)
     add("v", lambda g, T: g.vector.tensor_reduce(ap(T, cf(3)), ap(T, R("pw")), AxisListType.X, ALU.mult), [R("pw")], [cf(3)], FIX + 64)
     ts(cf(5), cf(3), 4000.0, cf(3), ALU.is_lt, ALU.mult)
     affine("a", cf(6), cf(8), -1.0, 15.0)
-    ts(R("zd"), R("jj"), cf(6), -0.5, ALU.is_equal, ALU.mult)
+    ts(R("zd"), R("jj"), cf(6), None, ALU.is_equal)
     ts(R("zc"), R("jj"), cf(6), cf(5), ALU.is_equal, ALU.mult)
     if any(eng("bit", u, s) == "a" for u in range(RU) for s in range(NSEG)):
         act(R("zh"), R("zc"), ACT.Copy, scale=0.5)
@@ -270,17 +292,25 @@ def plan(rank, n_ranks, bank):
             if sends and u < 2:
                 iota(R("a" if u else "xs", s * WS, s * WS + (X0 if s < NSEG else E0)), [[0, X0 if s < NSEG else E0]], 512 * EMPTY)
 
-    def offsets(e, t, r0, out):
-        v, r, t2 = R("vn", r0, r0 + size(t)), R("rn", r0, r0 + size(t)), tile(size(t))
-        affine(e, v, t, 1.0, 0.0)
-        ts(r, v, MG, MG, ALU.add, ALU.subtract)
-        mm(t2, [(R("ib"), R("th", 0, size(t))), (R("ih"), v), (R("im"), r), (R("ie"), r)])
-        ts(out, t2, -4096.0, float(WS), ALU.mult, ALU.min)
+    def offsets(e, t, r0, out, less=0.0, e3="v"):
+        n, m = R("ni", r0, r0 + size(t)), R("mi", r0, r0 + size(t))
+        if less:
+            ts(n, t, less, 4097.0, ALU.add, ALU.mult)
+        else:
+            affine(e, n, t, 4097.0, 0.0)
+        ts(m, n, 0x1FFE, None, ALU.bitwise_and)
+        affine(e3, out, m, -0.5, float(WS))
 
     def judge(u, s):
         c, k0 = s * SG, s * SS
+        hot[0] = HOT[2] if sends else 0.0
         t, sj = tile(PW, NJ), R("sj", s * PW, (s + 1) * PW)
-        mm(t, [(R("wj", 112 * u + 8 - 8 * h, 112 * u + 104 - 8 * h), X(u, c + h * PW, c + (h + 1) * PW)) for h in range(2)])
+        terms = [(wj(u, 8 - 8 * h, 104 - 8 * h), Z(u, c + h * PW, c + (h + 1) * PW)) for h in range(2)]
+        if eng("split", u, s):
+            mm(t, terms[:1], last=False)
+            mm(t, terms[1:], first=False)
+        else:
+            mm(t, terms)
         act(part(sj, 0, NJ), t, ACT.Sign, bias=part(col("jb", u), 0, NJ))
         for a, b in pieces("nscan", u, s):
             t, k = tile(b - a), k0 + a - c
@@ -288,77 +318,107 @@ def plan(rank, n_ranks, bank):
             o, d1, init = R("st", k + 1, k + 1 + b - a), R("cc", a - c, b - c), col("st", k)
             add("v", lambda g, T, o=o, t=t, d1=d1, init=init: g.vector.tensor_tensor_scan(
                 ap(T, o), ap(T, t), ap(T, d1), ap(T, init), ALU.min, ALU.max), [t, d1, init], [o], vcost([o, t]))
+        hot[0] = 0.0
+        for a, b in pieces("nout", u, s):
+            affine(eng("shift", u, a // PW), X(1, a, b), Z(u, a, b), *((512.0, -2554.0) if u else (2.0, -122.0)))
+        if s + 1 < NSEG or not CFG["after"]:
+            window(u, s, [])
+
+    def window(u, s, after):
+        c = s * SG
         for a, b in pieces("nwin", u, s):
-            affine(eng("win", u, a // PW), wseg(u, s, X0 + a - c, X0 + b - c), X(u, a, b), 1.0 / 512, -0.5 if u else -0.625)
+            e, w, z = eng("win", u, a // PW), wseg(u, s, X0 + a - c, X0 + b - c), R("ao", a, b)
+            if e != "g":
+                affine(e, w, Z(u, a, b), *((1.0, 0.0) if u else (1.0 / 256, 4.75)))
+                continue
+            if u == 0:
+                affine("v", z, Z(u, a, b), 1.0 / 256, 4.75)
+            add("g", lambda g, T, w=w, z=z: g.affine_select(ap(T, w), ap(T, z), [[0, size(z)]], ALU.is_gt, 0.0, 1, 0),
+                [z] + after, [w], 170 + 2 * size(z) * CY)
 
     def ends(s0, s1):
-        z, r, t = R("st", s0 * SS + SG, (s1 - 1) * SS + SG + 1, SS), R("rn", 256 + s0, 256 + s1), tile(s1 - s0)
-        ts(r, z, 2 * MG, 2 * MG, ALU.add, ALU.subtract)
-        mm(t, [(R("ib"), R("th", 0, s1 - s0)), (R("iz"), z), (R("ir"), r), (R("is"), r)])
-        ts(R("toff", 2 * s0, 2 * s1 - 1, 2), t, -4096.0, float(WS), ALU.mult, ALU.min)
+        e = CFG["ends"][s0 > 0]
+        offsets(e[0], R("st", s0 * SS + SG, (s1 - 1) * SS + SG + 1, SS), 256 + s0, R("toff", 2 * s0, 2 * s1 - 1, 2), 0.0, e[1])
 
     def hand_on(u):
+        def carry(x, s, off, first=0, how=(1.0, 0.0)):
+            k, last = s * WS, s + 1 == NSEG
+            gather(R("msg%d" % u) if last else R(x, k + WS + E0, k + WS + E0 + EXT), R(x, k + first, k + WS + 1), col("toff", off),
+                   eng("carry", u, s), list(how if last else (1.0, 0.0)))
+
+        w = "w%d" % u
+        hot[0] = HOT[0]
         ends(0, NSEG - 1)
         if sends:
             ends(NSEG - 1, NSEG)
-            x = "a" if u else "xs"
             for s in range(NSEG):
-                k, last = s * WS, s + 1 == NSEG
-                gather(R("msg%d" % u) if last else R(x, k + WS + E0, k + WS + E0 + EXT), R(x, k, k + WS + 1), col("toff", 2 * s),
-                       eng("carry", u, s), [1.0 / 512, -0.5 if u else -0.625] if last else [1.0, 0.0])
-            add("g", None, [R("msg%d" % u)], [], 300, send=u)
+                carry("a" if u else "xs", s, 2 * s, how=(1.0 / 512, 2554.0 / 512) if u else (1.0 / 256, 4.75))
+            add("g", None, [R("msg%d" % u)], [("sent", u, u + 1, 1, 0, 128)], 300, send=u)
+        if CFG["after"]:
+            hot[0] = 0.0
+            window(u, NSEG - 1, [("sent", u, u + 1, 1, 0, 128)])
         if takes:
             add("x", None, [], [wseg(u, 0, E0, E0 + EXT)], 0, arrive=u)
+        hot[0] = HOT[1]
         for s in range(NSEG - 1):
-            gather(wseg(u, s + 1, E0, E0 + EXT), wseg(u, s, 0, WS + 1), col("toff", 2 * s), eng("carry", u, s), [1.0, 0.0])
+            carry(w, s, 2 * s)
+        hot[0] = 0.0
 
     def point(u, s):
         c, k0 = s * SG, s * SS
         for a, b in pieces("nown", u, s):
             t, o = tile(b - a), R("vv", a, b)
+            if eng("least", u, s):
+                bankwise(t, lambda i, j: [(part(R("um", (a - c + i) // 4, (a - c + i) // 4 + 128), 0, NJ + 2),
+                                           part(R("sj", s * PW, (s + 1) * PW), 0, NJ + 2))])
+                tt(o, t, R("st", k0 + a - c, k0 + b - c), ALU.min)
+                continue
             bankwise(t, lambda i, j: [(part(R("us", (a - c + i) // 4, (a - c + i) // 4 + 128), 0, NJ), part(R("sj", s * PW, (s + 1) * PW), 0, NJ)),
                                       (R("ih"), R("st", k0 + a - c + i, k0 + a - c + j))])
             if eng("own", u, a // PW) == "a":
                 act(o, t, ACT.Relu, bias=-24576.0)
             else:
                 ts(o, t, -24576.0, 0.0, ALU.add, ALU.max)
-        t = tile(KC)
-        mm(t, wrap("zd", R("vv", c, c + SG)))
-        offsets(eng("half", u, s), t, s * KC, R("poff", s * KC, (s + 1) * KC))
+        n = CFG["join"][s]
+        if n:
+            t = tile(n * KC)
+            mm(t, wrap("zd", R("vv", c + SG - n * SG, c + SG)))
+            offsets(eng("half", u, s), t, (s + 1 - n) * KC, R("poff", (s + 1 - n) * KC, (s + 1) * KC), 200704.0 if eng("least", u, s) else 0.0,
+                    eng("poff", u, s))
+        edge = 63.5 / 256 + 5 if u else 127.5
         if eng("bit", u, s) == "a":
-            act(R("bit", c, c + SG), X(u, c, c + SG), ACT.Sign, bias=-63.5 if u else -127.5)
+            act(R("bit", c, c + SG), Z(u, c, c + SG), ACT.Sign, bias=-edge)
         else:
-            ts(R("bit", c, c + SG), X(u, c, c + SG), 63.5 if u else 127.5, None, ALU.is_ge)
-        if u == 0:
-            affine(eng("shift", u, s), X(1, c, c + SG), X(0, c, c + SG), 1.0, -64.0)
+            ts(R("bit", c, c + SG), Z(u, c, c + SG), edge, None, ALU.is_ge)
 
     def apply(u, s):
         for a, b in pieces("ncopy", u, s):
             gather(R("cp", a, b), wseg(u, s, 0, WS + 1), R("poff", a // 16, b // 16), "v", X(1, a, b))
-            ts(R("gb", a, b), R("cp", a, b), MQ, MQ - 0.25, ALU.add, ALU.is_equal)
+            ts(R("gb", a, b), R("cp", a, b), MQ, MQ + 5.5, ALU.add, ALU.is_equal)
         for a, b in pieces("ncode", u, s):
             t, sign = tile((b - a) // 16), eng("bit", u, s) == "a"
             mm(t, wrap("zh" if sign else "zc", R("bit", a, b)), last=False)
             mm(t, wrap("zc", R("gb", a, b)), first=False)
-            ts(R("coff", a // 16, b // 16), t, 2047.5 if sign else 0.0, None, ALU.add)
+            affine(eng("coff", u, s), R("coff", a // 16, b // 16), t, 1.0, 2047.5 if sign else 0.0)
         for a, b in pieces("ntab", u, s):
-            gather(R("tg", a, b), R("tab"), R("coff", a // 16, b // 16), eng("tg", u, a // PW), [1.0, 0.375])
+            gather(R("tg", a, b), R("tab"), R("coff", a // 16, b // 16), eng("tg", u, a // PW), [1.0 / 256, -2.625 / 256])
         for a, b in pieces("nmod", u, s):
-            j = a // PW
-            t, out, less = tile(b - a), X(1, a, b) if u + 1 < RU else R("yo", a, b), 64.0 if u + 1 < RU else 0.0
+            j, t = a // PW, tile(b - a)
+            bankwise(t, lambda i, j: [(R("il"), R("cp", a + i, a + j)), (R("ih"), R("tg", a + i, a + j))])
             if eng("mod", u, j) == "p":
-                t2, early = tile(b - a), eng("early", u, s)
-                for k in (t, t2) if early else (t,):
-                    bankwise(k, lambda i, j: [(R("i513"), R("cp", a + i, a + j)), (R("ih"), R("tg", a + i, a + j))], last=k is t)
-                affine(eng("qq", u, j), R("qq", a, b), t, 1.0 / 256, QB - 63.5 / 256)
-                bankwise(t2, lambda i, j: ([] if early else [(R("i513"), R("cp", a + i, a + j)), (R("ih"), R("tg", a + i, a + j))])
-                         + [(R("iq"), R("qq", a + i, a + j))], first=not early)
-                ts(out, t2, MG + 256 * QB, MG - 64 + less, ALU.add, ALU.subtract)
+                t2, z = tile(b - a), ("il", "ih", "im") if u + 1 < RU else ("jl", "jh", "jm")
+                bankwise(t2, lambda i, j: [(R(z[0]), R("cp", a + i, a + j)), (R(z[1]), R("tg", a + i, a + j))], last=False)
+                affine(eng("qq", u, j), R("qq", a, b), t, 1.0, QB - 5 - 63.5 / 256)
+                bankwise(t2, lambda i, j: [(R(z[2]), R("qq", a + i, a + j))], first=False)
+                if u + 1 < RU:
+                    affine(eng("fin", u, j), R("ao", a, b), t2, 1.0, QB)
+                else:
+                    ts(R("yo", a, b), t2, MG + 256 * QB, MG + 1216, ALU.add, ALU.subtract)
             else:
-                bankwise(t, lambda i, j: [(R("j513"), R("cp", a + i, a + j)), (R("j1"), R("tg", a + i, a + j))])
                 affine(eng("qq", u, j), R("qi", a, b), t, 1.0, -5 - 63.5 / 256)
                 tt(R("ao", a, b), t, R("qi", a, b), ALU.subtract)
-                affine(eng("out", u, j), out, R("ao", a, b), 256.0, 64.0 - 1280 - less)
+                if u + 1 == RU:
+                    affine(eng("out", u, j), R("yo", a, b), R("ao", a, b), 256.0, -1216.0)
             if u + 1 == RU:
                 add("s", lambda g, T, a=a, b=b: g.sync.dma_start(T["y"][:, a:b], T["yo"][:, a:b]), [R("yo", a, b)], [], 100,
                     sem=fresh("so"), inc=16, dma=(b - a) * 256)
@@ -518,18 +578,17 @@ def schedule(n_ranks):
             rev[j].append((i, d))
             rsucc[i].append((j, d))
     rng = np.random.default_rng(SEED)
-    key, best = list(range(len(ops))), None
+    key, best, cur = list(range(len(ops))), None, None
     for k in range(ROUNDS):
-        out = sweep(ops, (pre, succ), key, False, SLACK[k % len(SLACK)])
+        out = sweep(ops, (pre, succ), key, False, (rng.uniform(0.0, SLACK), rng.uniform(*URGE)))
         if out and (best is None or max(out[2]) < max(best[2])):
             best = out
-        if k % 3 == 2 or not out:
-            out = best
-            key = (rng.normal(0.0, SHAKE, len(ops)) - np.array(out[2])).tolist()
-        else:
-            key = [-x for x in out[2]]
-        back = sweep(ops, (rev, rsucc), key, True, SLACK[k % len(SLACK)])
-        key = [-x for x in back[2]] if back else best[1]
+        if out and (cur is None or max(out[2]) < max(cur[2]) + SHAKE):
+            cur = out
+        base, shake = (best, 3 * SHAKE) if k % 5 == 4 else (cur, SHAKE * (k % 2))
+        key = (rng.normal(0.0, 1.0, len(ops)) * shake - np.array(base[2])).tolist()
+        back = sweep(ops, (rev, rsucc), key, True, (rng.uniform(0.0, SLACK), rng.uniform(*URGE)))
+        key = [-x - o["hot"] for x, o in zip(back[2], ops)] if back else best[1]
     bank.update(best[4])
     for i, js in best[3].items():
         ops[i]["dep"] += [j for j in js if j is not None]
@@ -547,13 +606,15 @@ def rank_program(g, core, T, topo):
         return
     ops, seq = schedule(len(T.cores))[:2]
     queue = {"v": g.vector, "a": g.scalar, "p": g.tensor, "g": g, "s": g.sync}
-    count, mark, known, sent, alone = {}, {}, {}, 0, False
+    count, mark, known, behind, sent, alone = {}, {}, {q: {} for q in queue}, {}, 0, False
 
     def wait(q, sem, val):
-        if known.get((q, sem), 0) < val:
-            known[(q, sem)] = val
+        if known[q].get(sem, 0) < val:
             queue[q].wait_ge(T.sem[sem], val)
+            for s, v in list(behind.get((sem, val), {}).items()) + [(sem, val)]:
+                known[q][s] = max(known[q].get(s, 0), v)
 
+    place = {i: k for k, i in enumerate(seq)}
     for i in seq:
         o = ops[i]
         if o["e"][0] != rank:
@@ -562,16 +623,13 @@ def rank_program(g, core, T, topo):
         if "arrive" in o:
             mark[i] = ("arr%d" % o["arrive"], NENG)
             continue
-        need = {}
-        for j in o["dep"]:
-            if not (q == "p" and ops[j]["q"] == "p"):
-                need[mark[j][0]] = max(need.get(mark[j][0], 0), mark[j][1])
-        if q == "g" and "send" not in o:
+        for j in sorted(o["dep"], key=place.get, reverse=True):
+            if not (q == "p" and ops[j]["q"] == "p") and "send" not in ops[j]:
+                wait(q, *mark[j])
+        if q == "g" and "send" not in o and "dma" not in o:
             if alone or o["wr"][0][4]:
-                need["qg"] = count.get("qg", 0)
+                wait(q, "qg", count.get("qg", 0))
             alone = o["wr"][0][4] > 0
-        for sem in sorted(need):
-            wait(q, sem, need[sem])
         if "send" in o:
             u, dst = o["send"], T.cores[rank + 1]
             rid, pid = topo.addr(dst)[:2]
@@ -583,6 +641,7 @@ def rank_program(g, core, T, topo):
         sem, inc = o.get("sem", "q" + q), o.get("inc", 1)
         count[sem] = count.get(sem, 0) + inc
         mark[i] = (sem, count[sem])
+        behind[mark[i]] = dict(known[q])
         o["fn"](g, T).then_inc(T.sem[sem], inc)
     for sem in sorted(count):
         wait("s", sem, count[sem])

import numpy as np
from concourse.mybir import AluOpType, AxisListType, ActivationFunctionType

ALU = AluOpType
ACT = ActivationFunctionType
P, RU, NSEG = 4096, 4, 4
SG = P // NSEG
EXT = 16
E0, X0 = 8, 32
WS = SG + X0
SS = SG + 8
KC = SG // 16
PW = 512
NB = 8
NJ = 96
MG = 12582912.0
MQ = 6291456.5
EMPTY = -1024
NENG = 16

SCRATCH = {}
for _u in range(RU):
    SCRATCH["w%d" % _u] = ("sbuf", [128, NSEG * WS + E0], "float32")
    SCRATCH["msg%d" % _u] = ("sbuf", [128, EXT], "float32")
for _n in ("tab", "yo", "bit", "gb"):
    SCRATCH[_n] = ("sbuf", [128, P], "bfloat16")
for _n in ("xs", "a"):
    SCRATCH[_n] = ("sbuf", [128, NSEG * WS + E0], "bfloat16")
for _n in ("cp", "tg", "vv", "ao", "qq"):
    SCRATCH[_n] = ("sbuf", [128, P], "float16")
DIAG = {"ih": 1.0, "il": 513.0 / 512}
for _n in DIAG:
    SCRATCH[_n] = ("sbuf", [128, 128], "float16")
SCRATCH.update({
    "st": ("sbuf", [128, NSEG * SS], "float16"), "sj": ("sbuf", [128, P // 2], "float16"), "cc": ("sbuf", [128, SG], "float32"),
    "ud": ("sbuf", [128, 256], "float16"), "us": ("sbuf", [128, 256], "float16"), "um": ("sbuf", [128, 256], "float16"), "cu": ("sbuf", [128, 256], "float32"),
    "gp": ("sbuf", [128, 128], "float32"), "mk": ("sbuf", [128, 256], "float32"),
    "wj": ("sbuf", [128, 112], "bfloat16"), "wk": ("sbuf", [128, RU * 112], "float16"), "gc1": ("sbuf", [128, 112], "float32"), "g1": ("sbuf", [128, 112], "float32"),
    "gw": ("sbuf", [128, 112], "float32"), "gi": ("sbuf", [128, 48], "float32"), "gs": ("sbuf", [128, 48], "float32"),
    "gt": ("sbuf", [128, 48], "bfloat16"), "jb": ("sbuf", [128, 4], "float32"), "waf": ("sbuf", [128, 4], "float32"),
    "ni": ("sbuf", [128, 264], "int32"), "mi": ("sbuf", [128, 264], "int32"),
    "qi": ("sbuf", [128, P], "int32"), "zero": ("sbuf", [128, 128], "bfloat16"),
    "poff": ("sbuf", [128, 256], "uint16"), "coff": ("sbuf", [128, 256], "uint16"), "toff": ("sbuf", [128, 16], "uint16"),
    "was": ("sbuf", [128, 4], "bfloat16"), "kcs": ("sbuf", [128, 4], "bfloat16"), "hls": ("sbuf", [128, 8], "float32"),
    "jj": ("sbuf", [128, 144], "float32"), "cm": ("sbuf", [128, 16], "float32"), "cf": ("sbuf", [128, 12], "float32"),
    "pw": ("sbuf", [128, 16], "float32"), "zd": ("sbuf", [128, 144], "float16"), "zc": ("sbuf", [128, 144], "bfloat16"),
    "zh": ("sbuf", [128, 144], "bfloat16"),
})
for _k in range(NB // 2):
    SCRATCH["p%d" % _k] = ("psum", [128, 2 * PW], "float32")

SEMAPHORES = (["qv", "qa", "qp", "qg", "sent"] + ["arr%d" % u for u in range(RU)]
              + ["ld%d" % k for k in range(32)] + ["so%d" % k for k in range(16)] + ["ac%d" % k for k in range(16)])
HOT = (0.0, 0.0, 0.0)
QB = 1536.0

CY, PCY, GA, FIX, FIXA, FIXG, LAT, WIRE = 0.95, 0.58, 1.56, 60.0, 75.0, 66.0, 120.0, 2200.0
ROUNDS, SLACK, URGE, SHAKE, SEED, AHEAD = 400, 100.0, (0.03, 0.15), 300.0, 1, 8

CFG = {"win": "a", "tg": "a", "qq": "a", "own": "a", "carry": "a", "shift": "g", ("shift", 0): "v", "fin": "a", "least": False, "after": False, "cc0": 128, "cca": 256, "cu0": 32, ("nmod", RU - 1, NSEG - 1): PW // 2, ("ntab", RU - 1, NSEG - 1): PW // 2, "poff": "v", "ends": ("vv", "vv"), "half": "a", "out": "v", "mod": "v", "bit": "v",
       "early": True, "split": False, "once": False, "join": (1, 1, 1, 1), "fill": "a", "fills": ("cu",), "wsum": "a", "coff": "a",
       "nout": SG, "nwin": SG, "nscan": SG, "nown": SG, "ncopy": SG, "ncode": SG, "ntab": PW, "nmod": PW}
CFG.update({(_k, _u, _s): PW for _u in range(RU) for _k, _s in (("ncopy", 0), ("nown", 0), ("nscan", NSEG - 1))})
CFG.update({"nwin": PW, "nown": PW, "win": "g", ("win", 0): "a", "shift": "v"})
CFG.update({("shift", _u, _j): "a" for _u in range(1, RU) for _j in (0, 2)})


def plan(rank, n_ranks, bank):
    ops, hot = [], [0.0]

    def eng(kind, u, j):
        return CFG.get((kind, rank, u, j), CFG.get((kind, u, j), CFG.get((kind, u), CFG[kind])))

    def add(q, fn, rd, wr, cost, **kw):
        d = {"q": q, "fn": fn, "rd": rd, "wr": wr, "cost": cost, "hot": hot[0]}
        d.update(kw)
        ops.append(d)
        return d

    def R(name, a=0, b=None, step=1):
        return (name, a, SCRATCH[name][1][1] if b is None else b, step, 0, 128)

    def X(u, a, b):
        k = X0 * (a // SG + 1)
        return R("a" if u else "xs", a + k, b + k)

    def Z(u, a, b):
        return R("ao", a, b) if u else X(0, a, b)

    def wj(u, a, b):
        return R("wk", 112 * u + a, 112 * u + b) if u else R("wj", a, b)

    def part(r, p0, p1):
        return r[:4] + (p0, p1)

    def size(r):
        return len(range(r[1], r[2], r[3]))

    def ap(T, r):
        if not isinstance(r, tuple):
            return r
        if r[0][0] == "@":
            b = bank[(rank, r[0])]
            return T["p%d" % (b // 2)][r[4]:r[5], b % 2 * PW + r[1]:b % 2 * PW + r[2]]
        return T[r[0]][r[4]:r[5], r[1]:r[2]:r[3]] if r[3] > 1 else T[r[0]][r[4]:r[5], r[1]:r[2]]

    def kind(r):
        return "float32" if r[0][0] == "@" else SCRATCH[r[0]][2]

    def vcost(rs):
        half = all(kind(r) in ("bfloat16", "float16", "uint16") for r in rs)
        return FIX + max(64, size(rs[0]) * (0.5 if half else 1.0)) * CY

    def ts(out, in0, s1, s2, op0, op1=None):
        rd = [in0] + [s for s in (s1, s2) if isinstance(s, tuple)]

        def fn(g, T):
            if op1 is None:
                return g.vector.tensor_scalar(ap(T, out), ap(T, in0), ap(T, s1), None, op0)
            return g.vector.tensor_scalar(ap(T, out), ap(T, in0), ap(T, s1), ap(T, s2), op0, op1)
        return add("v", fn, rd, [out], vcost([out, in0]))

    def tt(out, in0, in1, op):
        f = 1 if "@" in (in0[0][0], in1[0][0]) else 2
        return add("v", lambda g, T: g.vector.tensor_tensor(ap(T, out), ap(T, in0), ap(T, in1), op), [in0, in1], [out],
                   FIX + max(64, f * size(out)) * CY)

    def cp(out, in0):
        return add("v", lambda g, T: g.vector.tensor_copy(ap(T, out), ap(T, in0)), [in0], [out], vcost([out, in0]))

    def fill(out, c):
        if CFG["fill"] == "a" and out[0] in CFG["fills"]:
            return act(out, part(R("gp", 0, size(out)), out[4], out[5]), ACT.Identity, bias=c, scale=0.0)
        return add("v", lambda g, T: g.vector.memset(ap(T, out), c), [], [out], vcost([out]))

    def act(out, in0, func, bias=0.0, scale=1.0):
        rd = [in0] + [s for s in (bias, scale) if isinstance(s, tuple)]
        return add("a", lambda g, T: g.scalar.activation(ap(T, out), ap(T, in0), func, bias=ap(T, bias), scale=ap(T, scale)),
                   rd, [out], FIXA + max(64, size(out)) * CY)

    def affine(e, out, in0, scale, bias):
        if e == "a":
            return act(out, in0, ACT.Identity, bias=bias, scale=scale)
        return ts(out, in0, scale, bias, ALU.mult, ALU.add)

    def mm(out, terms, first=True, last=True):
        def fn(g, T):
            for k, t in enumerate(terms):
                ins = g.tensor.matmul(ap(T, t[2] if len(t) > 2 else out), ap(T, t[0]), ap(T, t[1]),
                                      first and k == 0, last and k == len(terms) - 1)
            return ins
        cost = sum(max(64, size(out)) * PCY * (4 if kind(t[0]) == "float32" else 1) for t in terms)
        return add("p", fn, [t[0] for t in terms] + [t[1] for t in terms], [out], 30 + cost)

    def wrap(z, src):
        return [(R(z, 15 - i, 143 - i), R(src[0], src[1] + i, src[2], 16)) for i in range(16)]

    def gather(out, win, off, q, how):
        def fn(g, T):
            src = ap(T, win).indirect(ap(T, off))
            if isinstance(how, tuple):
                return g.vector.tensor_tensor(ap(T, out), src, ap(T, how), ALU.max)
            if q == "a":
                return g.scalar.activation(ap(T, out), src, ACT.Identity, bias=how[1], scale=how[0])
            return g.vector.tensor_scalar(ap(T, out), src, how[0], how[1], ALU.mult, ALU.add)
        return add(q, fn, [win, off] + ([how] if isinstance(how, tuple) else []), [out], FIXG + max(64, size(out) * GA) * CY)

    def iota(out, pat, base, mult=0):
        return add("g", lambda g, T: g.iota(ap(T, out), pat, base, mult, allow_small_or_imprecise_dtypes=True), [], [out],
                   130 + 2 * size(out) * CY)

    num = {"ld": 0, "so": 0, "ac": 0, "@": 0}

    def fresh(k):
        num[k] += 1
        return "%s%d" % (k, num[k] - 1)

    def tile(n=PW, rows=128):
        return (fresh("@") + ("w" if n > PW else ""), 0, n, 1, 0, rows)

    def bankwise(t, terms, **kw):
        for a in range(0, size(t), PW):
            b = min(a + PW, size(t))
            mm((t[0], a, b) + t[3:], terms(a, b), **kw)

    def pieces(kind, u, s):
        n = eng(kind, u, s)
        return [(a, a + n) for a in range(s * SG, (s + 1) * SG, n)]

    def load(q, out, src, a, b):
        add(q, lambda g, T: (g.sync if q == "s" else g.scalar).dma_start(ap(T, out), T[src][:, a:b]), [], [out], 100,
            sem=fresh("ld"), inc=16, dma=(b - a) * 256 if b - a > 8 else 0)

    def wseg(u, s, a, b):
        return R("w%d" % u, s * WS + a, s * WS + b)

    def col(name, k):
        return R(name, k, k + 1)

    def cf(k):
        return col("cf", k)

    sends, takes = rank + 1 < n_ranks, rank > 0

    load("a", R("kcs"), "kc", 0, 4)
    load("a", R("was"), "wa", 0, 4)
    load("a", R("hls"), "hl", 0, 8)
    for s in range(NSEG):
        load("s", X(0, s * SG, (s + 1) * SG), "x", s * SG, (s + 1) * SG)
    load("s", R("tab", 0, P // 2), "inv", 0, P // 2)
    load("s", R("tab", P // 2, P), "inv", P // 2, P)

    iota(R("gp"), [[1, 8], [0, 16]], 0)
    iota(cf(0), [[0, 1]], -15, 2)
    iota(cf(7), [[0, 1]], 0, 1)
    iota(R("gc1"), [[0, 7], [1, 16]], int(MG) - 8)
    iota(R("gi"), [[100, 3], [0, 2], [1, 8]], int(MG) - 100)
    for end, v in ((NJ, -1.0), (32, 1.0), (16, 0.0)):
        fill(part(cf(4), 0, end), v)
    for end, v in ((NJ + 2, 0.0), (NJ + 1, 1.0)):
        fill(part(cf(10), NJ, end), v)
    n = CFG["cc0"]
    iota(R("cc", 0, n), [[-2, n]], 2047)
    while n < SG:
        affine("a" if n >= CFG["cca"] else "v", R("cc", n, 2 * n), R("cc", 0, n), 1.0, -2.0 * n)
        n *= 2
    n = CFG["cu0"]
    for a in (1, 0):
        fill(part(R("cu", 0, n), 0, 16 * a + 16), (-2048.0, 16384.0)[a])
    for a in (3, 2, 5, 4):
        iota(part(R("cu", 0, n), 16 * (a - a % 2), 16 * a + 16), [[0, 2 * n >> a], [-4096, 2], [0, 1 << (a - 2)]], 2048)
    while n < 128:
        cp(part(R("cu", n, 2 * n), 0, NJ), part(R("cu", 0, n), 0, NJ))
        n *= 2
    for h in range(2):
        fill(part(R("cu", 128 * h, 128 * h + 128), NJ, NJ + 2), -6144.0 - 1024 * h)
        fill(part(R("cu", 128 * h, 128 * h + 128), NJ, NJ + 1), 1.0)
    iota(R("jj"), [[1, 144]], 0, -1)
    iota(R("cm"), [[1, 16]], 0)
    ts(cf(1), cf(0), 1.0 / 32, MG, ALU.mult, ALU.add)
    ts(R("g1"), R("gc1"), cf(1), None, ALU.is_equal)
    for j in range(4):
        affine("a", R("gw", 40 + 16 * j, 56 + 16 * j), R("g1", 40 + 16 * j, 56 + 16 * j), 2.0 ** j + 1, -1.0)
    for u in range(RU):
        ts(wj(u, 0, 40), R("g1", 0, 40), col("was", u), 256.0 if u else 1.0, ALU.mult, ALU.mult)
        ts(wj(u, 40, 104), R("gw", 40, 104), col("kcs", u), 256.0 if u else 1.0, ALU.is_equal, ALU.mult)
    ts(R("gs"), R("gi"), cf(1), -1.0 / 16, ALU.is_equal, ALU.mult)
    ts(R("gt"), R("gi"), cf(1), -1216.0, ALU.is_equal, ALU.mult)
    fill(R("jb"), -1343.5)
    fill(col("jb", 0), -127.5)
    t = tile(RU, 32)
    later = (t[0], 1, RU, 1, 0, 32)
    mm(t, [(R("gs", 16, 48), R("hls", 0, RU)), (R("gt", 16, 48), R("was", 1, RU), later), (R("gt", 0, 32), R("was", 1, RU), later),
           (R("gs", 0, 32), R("hls", RU, 2 * RU))])
    ts(part(R("jb"), 0, 32), t, part(cf(4), 0, 32), 0.5, ALU.subtract, ALU.add)
    ts(cf(2), cf(1), MG, -16.0, ALU.subtract, ALU.mult)
    ts(cf(8), cf(7), cf(2), None, ALU.add)
    for h in range(2):
        mk = R("mk", 128 * h, 128 * h + 128)
        ts(mk, R("gp"), cf(8), -8.0 * h, ALU.subtract, ALU.is_equal)
        tt(part(R("ud", 128 * h, 128 * h + 128), 0, NJ), part(R("cu", 0, 128), 0, NJ), part(mk, 0, NJ), ALU.mult)
    act(part(R("ud"), NJ, NJ + 2), part(R("cu"), NJ, NJ + 2), ACT.Copy)
    act(part(R("us"), 0, NJ), part(R("ud"), 0, NJ), ACT.Identity, scale=part(cf(4), 0, NJ))
    if any(eng("least", u, s) for u in range(RU) for s in range(NSEG)):
        for end, v in ((NJ, -2.0), (32, 2176.0 / 16384), (16, 0.0)):
            fill(part(cf(11), 0, end), v)
        act(part(R("um"), 0, NJ), part(R("ud"), 0, NJ), ACT.Identity, scale=part(cf(11), 0, NJ))
        for end, v in ((NJ + 2, -14464.0), (NJ + 1, 0.0)):
            act(part(R("um"), NJ, end), part(R("cu"), NJ, end), ACT.Identity, bias=v, scale=0.0)
    rows = [part(R("sj", s * PW, (s + 1) * PW), NJ, NJ + 2) for s in range(NSEG)]
    act(rows[0], part(R("cc", 0, PW), NJ, NJ + 2), ACT.Identity, bias=1.0, scale=part(cf(10), NJ, NJ + 2))
    for r in rows[1:]:
        add("s", lambda g, T, r=r: g.sync.dma_start(ap(T, r), ap(T, rows[0])), [rows[0]], [r], 100, sem=fresh("ld"), inc=16, dma=0)
    affine("a", cf(9), cf(8), -2.0, 2.0 * (WS - E0))
    act(R("st", 0, NSEG * SS, SS), R("cm", 0, NSEG), ACT.Identity, bias=cf(9), scale=0.0)
    iota(R("zero"), [[0, 128]], 0)
    for n, f in sorted(DIAG.items()):
        add("g", lambda g, T, n=n, f=f: g.affine_select(ap(T, R(n)), ap(T, R("zero")), [[-1, 128]], ALU.not_equal, f, 0, 1),
            [R("zero")], [R(n)], 170 + 256 * CY)
    ts(R("pw"), R("cm"), cf(8), 1.0, ALU.is_lt, ALU.add)
    add("v", lambda g, T: g.vector.tensor_reduce(ap(T, cf(3)), ap(T, R("pw")), AxisListType.X, ALU.mult), [R("pw")], [cf(3)], FIX + 64)
    ts(cf(5), cf(3), 4000.0, cf(3), ALU.is_lt, ALU.mult)
    affine("a", cf(6), cf(8), -1.0, 15.0)
    ts(R("zd"), R("jj"), cf(6), None, ALU.is_equal)
    ts(R("zc"), R("jj"), cf(6), cf(5), ALU.is_equal, ALU.mult)
    if any(eng("bit", u, s) == "a" for u in range(RU) for s in range(NSEG)):
        act(R("zh"), R("zc"), ACT.Copy, scale=0.5)
    for u in range(RU):
        for s in range(NSEG + 1):
            for a, b in ((0, E0), (E0 + EXT, X0)) if s == 0 and takes else ((0, X0 if s < NSEG else E0),):
                iota(wseg(u, s, a, b), [[0, b - a]], EMPTY)
            if sends and u < 2:
                iota(R("a" if u else "xs", s * WS, s * WS + (X0 if s < NSEG else E0)), [[0, X0 if s < NSEG else E0]], 512 * EMPTY)

    def offsets(e, t, r0, out, less=0.0, e3="v"):
        n, m = R("ni", r0, r0 + size(t)), R("mi", r0, r0 + size(t))
        if less:
            ts(n, t, less, 4097.0, ALU.add, ALU.mult)
        else:
            affine(e, n, t, 4097.0, 0.0)
        ts(m, n, 0x1FFE, None, ALU.bitwise_and)
        affine(e3, out, m, -0.5, float(WS))

    def judge(u, s):
        c, k0 = s * SG, s * SS
        hot[0] = HOT[2] if sends else 0.0
        t, sj = tile(PW, NJ), R("sj", s * PW, (s + 1) * PW)
        terms = [(wj(u, 8 - 8 * h, 104 - 8 * h), Z(u, c + h * PW, c + (h + 1) * PW)) for h in range(2)]
        if eng("split", u, s):
            mm(t, terms[:1], last=False)
            mm(t, terms[1:], first=False)
        else:
            mm(t, terms)
        act(part(sj, 0, NJ), t, ACT.Sign, bias=part(col("jb", u), 0, NJ))
        for a, b in pieces("nscan", u, s):
            t, k = tile(b - a), k0 + a - c
            bankwise(t, lambda i, j: [(part(R("ud", (a - c + i) // 4, (a - c + i) // 4 + 128), 0, NJ + 2), part(sj, 0, NJ + 2))])
            o, d1, init = R("st", k + 1, k + 1 + b - a), R("cc", a - c, b - c), col("st", k)
            add("v", lambda g, T, o=o, t=t, d1=d1, init=init: g.vector.tensor_tensor_scan(
                ap(T, o), ap(T, t), ap(T, d1), ap(T, init), ALU.min, ALU.max), [t, d1, init], [o], vcost([o, t]))
        hot[0] = 0.0
        for a, b in pieces("nout", u, s):
            affine(eng("shift", u, a // PW), X(1, a, b), Z(u, a, b), *((512.0, -2554.0) if u else (2.0, -122.0)))
        if s + 1 < NSEG or not CFG["after"]:
            window(u, s, [])

    def window(u, s, after):
        c = s * SG
        for a, b in pieces("nwin", u, s):
            e, w, z = eng("win", u, a // PW), wseg(u, s, X0 + a - c, X0 + b - c), R("ao", a, b)
            if e != "g":
                affine(e, w, Z(u, a, b), *((1.0, 0.0) if u else (1.0 / 256, 4.75)))
                continue
            if u == 0:
                affine("v", z, Z(u, a, b), 1.0 / 256, 4.75)
            add("g", lambda g, T, w=w, z=z: g.affine_select(ap(T, w), ap(T, z), [[0, size(z)]], ALU.is_gt, 0.0, 1, 0),
                [z] + after, [w], 170 + 2 * size(z) * CY)

    def ends(s0, s1):
        e = CFG["ends"][s0 > 0]
        offsets(e[0], R("st", s0 * SS + SG, (s1 - 1) * SS + SG + 1, SS), 256 + s0, R("toff", 2 * s0, 2 * s1 - 1, 2), 0.0, e[1])

    def hand_on(u):
        def carry(x, s, off, first=0, how=(1.0, 0.0)):
            k, last = s * WS, s + 1 == NSEG
            gather(R("msg%d" % u) if last else R(x, k + WS + E0, k + WS + E0 + EXT), R(x, k + first, k + WS + 1), col("toff", off),
                   eng("carry", u, s), list(how if last else (1.0, 0.0)))

        w = "w%d" % u
        hot[0] = HOT[0]
        ends(0, NSEG - 1)
        if sends:
            ends(NSEG - 1, NSEG)
            for s in range(NSEG):
                carry("a" if u else "xs", s, 2 * s, how=(1.0 / 512, 2554.0 / 512) if u else (1.0 / 256, 4.75))
            add("g", None, [R("msg%d" % u)], [("sent", u, u + 1, 1, 0, 128)], 300, send=u)
        if CFG["after"]:
            hot[0] = 0.0
            window(u, NSEG - 1, [("sent", u, u + 1, 1, 0, 128)])
        if takes:
            add("x", None, [], [wseg(u, 0, E0, E0 + EXT)], 0, arrive=u)
        hot[0] = HOT[1]
        for s in range(NSEG - 1):
            carry(w, s, 2 * s)
        hot[0] = 0.0

    def point(u, s):
        c, k0 = s * SG, s * SS
        for a, b in pieces("nown", u, s):
            t, o = tile(b - a), R("vv", a, b)
            if eng("least", u, s):
                bankwise(t, lambda i, j: [(part(R("um", (a - c + i) // 4, (a - c + i) // 4 + 128), 0, NJ + 2),
                                           part(R("sj", s * PW, (s + 1) * PW), 0, NJ + 2))])
                tt(o, t, R("st", k0 + a - c, k0 + b - c), ALU.min)
                continue
            bankwise(t, lambda i, j: [(part(R("us", (a - c + i) // 4, (a - c + i) // 4 + 128), 0, NJ), part(R("sj", s * PW, (s + 1) * PW), 0, NJ)),
                                      (R("ih"), R("st", k0 + a - c + i, k0 + a - c + j))])
            if eng("own", u, a // PW) == "a":
                act(o, t, ACT.Relu, bias=-24576.0)
            else:
                ts(o, t, -24576.0, 0.0, ALU.add, ALU.max)
        n = CFG["join"][s]
        if n:
            t = tile(n * KC)
            mm(t, wrap("zd", R("vv", c + SG - n * SG, c + SG)))
            offsets(eng("half", u, s), t, (s + 1 - n) * KC, R("poff", (s + 1 - n) * KC, (s + 1) * KC), 200704.0 if eng("least", u, s) else 0.0,
                    eng("poff", u, s))
        edge = 63.5 / 256 + 5 if u else 127.5
        if eng("bit", u, s) == "a":
            act(R("bit", c, c + SG), Z(u, c, c + SG), ACT.Sign, bias=-edge)
        else:
            ts(R("bit", c, c + SG), Z(u, c, c + SG), edge, None, ALU.is_ge)

    def apply(u, s):
        for a, b in pieces("ncopy", u, s):
            gather(R("cp", a, b), wseg(u, s, 0, WS + 1), R("poff", a // 16, b // 16), "v", X(1, a, b))
            ts(R("gb", a, b), R("cp", a, b), MQ, MQ + 5.5, ALU.add, ALU.is_equal)
        for a, b in pieces("ncode", u, s):
            t, sign = tile((b - a) // 16), eng("bit", u, s) == "a"
            mm(t, wrap("zh" if sign else "zc", R("bit", a, b)), last=False)
            mm(t, wrap("zc", R("gb", a, b)), first=False)
            affine(eng("coff", u, s), R("coff", a // 16, b // 16), t, 1.0, 2047.5 if sign else 0.0)
        for a, b in pieces("ntab", u, s):
            gather(R("tg", a, b), R("tab"), R("coff", a // 16, b // 16), eng("tg", u, a // PW), [1.0 / 256, -2.625 / 256])
        for a, b in pieces("nmod", u, s):
            j, t = a // PW, tile(b - a)
            bankwise(t, lambda i, j: [(R("il"), R("cp", a + i, a + j)), (R("ih"), R("tg", a + i, a + j))])
            if eng("mod", u, j) == "p":
                t2, z = tile(b - a), ("il", "ih", "im") if u + 1 < RU else ("jl", "jh", "jm")
                bankwise(t2, lambda i, j: [(R(z[0]), R("cp", a + i, a + j)), (R(z[1]), R("tg", a + i, a + j))], last=False)
                affine(eng("qq", u, j), R("qq", a, b), t, 1.0, QB - 5 - 63.5 / 256)
                bankwise(t2, lambda i, j: [(R(z[2]), R("qq", a + i, a + j))], first=False)
                if u + 1 < RU:
                    affine(eng("fin", u, j), R("ao", a, b), t2, 1.0, QB)
                else:
                    ts(R("yo", a, b), t2, MG + 256 * QB, MG + 1216, ALU.add, ALU.subtract)
            else:
                affine(eng("qq", u, j), R("qi", a, b), t, 1.0, -5 - 63.5 / 256)
                tt(R("ao", a, b), t, R("qi", a, b), ALU.subtract)
                if u + 1 == RU:
                    affine(eng("out", u, j), R("yo", a, b), R("ao", a, b), 256.0, -1216.0)
            if u + 1 == RU:
                add("s", lambda g, T, a=a, b=b: g.sync.dma_start(T["y"][:, a:b], T["yo"][:, a:b]), [R("yo", a, b)], [], 100,
                    sem=fresh("so"), inc=16, dma=(b - a) * 256)

    for s in range(NSEG):
        judge(0, s)
    for u in range(RU):
        hand_on(u)
        for s in range(NSEG):
            point(u, s)
        for s in range(NSEG):
            apply(u, s)
            if u + 1 < RU:
                judge(u + 1, s)
    return ops


def link(ops):
    seen, opener = {}, {}
    for i, o in enumerate(ops):
        dep = set()
        acc = [(r, False) for r in o["rd"]] + [(r, True) for r in o["wr"]]
        for r, w in acc:
            for (j, e, wj) in seen.get(r[0], []):
                if r[0][0] == "@" or ((w or wj) and meet(e, r)):
                    dep.add(j)
        for r, w in acc:
            if r[0][0] == "@":
                o["tile"], o["opens"] = r[0], o.get("opens") or r[0] not in seen
                seen[r[0]] = [(i, r, True)]
                if o["opens"]:
                    opener[r[0]] = o
                elif o["q"] != "p" and r[0] in opener:
                    opener.pop(r[0])["reader"], o["reads"] = o["q"], True
            else:
                keep = [x for x in seen.get(r[0], []) if not (w and covers(r, x[1]))]
                seen[r[0]] = keep + [(i, r, w)]
        dep.discard(i)
        o["dep"] = sorted(dep)
    for name in seen:
        if name[0] == "@":
            ops[seen[name][0][0]]["closes"] = True


def meet(a, b):
    if a[4] >= b[5] or b[4] >= a[5] or a[1] >= b[2] or b[1] >= a[2]:
        return False
    if a[3] < b[3]:
        a, b = b, a
    return a[3] == 1 or b[3] > 1 or any(b[1] <= k < b[2] for k in range(a[1], a[2], a[3]))


def covers(a, b):
    return a[3] == 1 and a[1] <= b[1] and b[2] <= a[2] and a[4] <= b[4] and b[5] <= a[5]


def sweep(ops, edges, key, back, slack):
    n = len(ops)
    pre, succ = edges
    opens, closes = ("closes", "opens") if back else ("opens", "closes")
    eng = [o["e"] for o in ops]
    need = [(1 + (o["tile"][-1] == "w")) if o.get(opens) else 0 for o in ops]
    left, due, ready = [len(p) for p in pre], [0.0] * n, {e: [] for e in sorted(set(eng))}
    for i in range(n):
        if not left[i]:
            ready[eng[i]].append(i)
    free, at, end, seq, after, bank, wire = {e: 0.0 for e in ready}, [0.0] * n, [0.0] * n, [], {}, {}, {}
    banks = {e[0]: {k: (0.0, None) for k in range(NB)} for e in ready}
    mates = {r: [e for e in ready if e[0] == r] for r in banks}
    never = float("inf")
    turns = {e: [0.0] * (n if back else AHEAD) for e in ready}
    reader = [o.get("reader") for o in ops]

    def starts(e):
        bk, f = banks[e[0]], free[e]
        bt = (f, max(f, min([v[0] for v in bk.values()], default=never)),
              max(f, min([max(bk[k][0], bk[k + 1][0]) for k in range(0, NB, 2) if k in bk and k + 1 in bk], default=never)))
        if back or e[1] != "p":
            return [(max(due[i], bt[need[i]]), i) for i in ready[e]]
        turn = {q: min(turns[(e[0], q)], default=never) for q in "va"}
        return [(max(due[i], bt[need[i]], turn.get(reader[i], 0.0)), i) for i in ready[e]]

    cand = {e: starts(e) for e in ready}
    first = {e: min(cand[e], default=(never,))[0] for e in ready}
    for _ in range(n):
        e = min(first, key=first.get)
        if first[e] == never:
            return None
        lim = first[e] + slack[0]
        t, i = min(cand[e], key=lambda x: max(x[0], lim) + slack[1] * key[x[1]])
        o = ops[i]
        ready[e].remove(i)
        at[i] = t
        end[i] = free[e] = t + o["cost"]
        bk, touched = banks[e[0]], {e}
        if not back and reader[i]:
            turns[(e[0], reader[i])].remove(min(turns[(e[0], reader[i])]))
        if not back and o.get("reads"):
            turns[e].append(t)
            touched.add((e[0], "p"))
        if need[i]:
            if need[i] == 2:
                b = min([k for k in range(0, NB, 2) if k in bk and k + 1 in bk], key=lambda k: max(bk[k][0], bk[k + 1][0]))
            else:
                b = min(bk, key=lambda k: (max(bk[k][0], t), k ^ 1 in bk, bk[k][0]))
            bank[(e[0], o["tile"])] = b
            after[i] = [bk.pop(k)[1] for k in range(b, b + need[i])]
            touched.update(mates[e[0]])
        if o.get(closes):
            for k in range(1 + (o["tile"][-1] == "w")):
                bk[bank[(e[0], o["tile"])] + k] = (end[i] + LAT, i)
            touched.update(mates[e[0]])
        if "dma" in o and not back:
            end[i] = max(wire.get(e[0], 0.0) if o["dma"] else 0.0, end[i] + 1500) + o["dma"] / 250.0
            if o["dma"]:
                wire[e[0]] = end[i]
        seq.append(i)
        for k, d in succ[i]:
            if end[i] + d > due[k]:
                due[k] = end[i] + d
            left[k] -= 1
            if not left[k]:
                ready[eng[k]].append(k)
                touched.add(eng[k])
        for e in touched:
            cand[e] = starts(e)
            first[e] = min(cand[e])[0] if cand[e] else never
    return seq, at, end, after, bank


CACHE = {}


def schedule(n_ranks):
    if n_ranks in CACHE:
        return CACHE[n_ranks]
    ops, pre, sent, bank = [], [], {}, {}
    for r in range(n_ranks):
        mine = plan(r, n_ranks, bank)
        link(mine)
        base = len(ops)
        for i, o in enumerate(mine):
            o["e"] = (r, o["q"])
            p = [(base + j, 0.0 if mine[j]["q"] == "p" == o["q"] else LAT) for j in o["dep"]]
            o["dep"] = [base + j for j in o["dep"]]
            if "send" in o:
                sent[(r, o["send"])] = base + i
            if "arrive" in o:
                p.append((sent[(r - 1, o["arrive"])], WIRE))
            pre.append(p)
        ops += mine
    succ, rev, rsucc = [[] for _ in ops], [[] for _ in ops], [[] for _ in ops]
    for i, p in enumerate(pre):
        for j, d in p:
            succ[j].append((i, d))
            d += 1500 + ops[j]["dma"] / 250.0 if "dma" in ops[j] else 0
            rev[j].append((i, d))
            rsucc[i].append((j, d))
    rng = np.random.default_rng(SEED)
    key, best, cur = list(range(len(ops))), None, None
    for k in range(ROUNDS):
        out = sweep(ops, (pre, succ), key, False, (rng.uniform(0.0, SLACK), rng.uniform(*URGE)))
        if out and (best is None or max(out[2]) < max(best[2])):
            best = out
        if out and (cur is None or max(out[2]) < max(cur[2]) + SHAKE):
            cur = out
        base, shake = (best, 3 * SHAKE) if k % 5 == 4 else (cur, SHAKE * (k % 2))
        key = (rng.normal(0.0, 1.0, len(ops)) * shake - np.array(base[2])).tolist()
        back = sweep(ops, (rev, rsucc), key, True, (rng.uniform(0.0, SLACK), rng.uniform(*URGE)))
        key = [-x - o["hot"] for x, o in zip(back[2], ops)] if back else best[1]
    bank.update(best[4])
    for i, js in best[3].items():
        ops[i]["dep"] += [j for j in js if j is not None]
    CACHE[n_ranks] = (ops,) + best[:3]
    return CACHE[n_ranks]


def message(u, there, here):
    return there["w%d" % u][:, E0:E0 + EXT], here["msg%d" % u][:]


def rank_program(g, core, T, topo):
    rank = T.rank_of(core)
    if rank is None:
        return
    ops, seq = schedule(len(T.cores))[:2]
    queue = {"v": g.vector, "a": g.scalar, "p": g.tensor, "g": g, "s": g.sync}
    count, mark, known, behind, sent, alone = {}, {}, {q: {} for q in queue}, {}, 0, False

    def wait(q, sem, val):
        if known[q].get(sem, 0) < val:
            queue[q].wait_ge(T.sem[sem], val)
            for s, v in list(behind.get((sem, val), {}).items()) + [(sem, val)]:
                known[q][s] = max(known[q].get(s, 0), v)

    place = {i: k for k, i in enumerate(seq)}
    for i in seq:
        o = ops[i]
        if o["e"][0] != rank:
            continue
        q = o["q"]
        if "arrive" in o:
            mark[i] = ("arr%d" % o["arrive"], NENG)
            continue
        for j in sorted(o["dep"], key=place.get, reverse=True):
            if not (q == "p" and ops[j]["q"] == "p") and "send" not in ops[j]:
                wait(q, *mark[j])
        if q == "g" and "send" not in o and "dma" not in o:
            if alone or o["wr"][0][4]:
                wait(q, "qg", count.get("qg", 0))
            alone = o["wr"][0][4] > 0
        if "send" in o:
            u, dst = o["send"], T.cores[rank + 1]
            rid, pid = topo.addr(dst)[:2]
            mask = sum(1 << e for e in topo.engines(core, dst)[:NENG])
            land, src = message(u, T, T)
            g.remote_dma(land, src, T.sem["arr%d" % u], T.sem["sent"], pid, rid, mask)
            sent += NENG
            continue
        sem, inc = o.get("sem", "q" + q), o.get("inc", 1)
        count[sem] = count.get(sem, 0) + inc
        mark[i] = (sem, count[sem])
        behind[mark[i]] = dict(known[q])
        o["fn"](g, T).then_inc(T.sem[sem], inc)
    for sem in sorted(count):
        wait("s", sem, count[sem])
    if sent:
        wait("g", "sent", sent)
